import numpy as np
import ml_dtypes


def mxq(x, axis, fmt="e4m3"):
    dtype, down = {"e4m3": (ml_dtypes.float8_e4m3fn, 7), "e5m2": (ml_dtypes.float8_e5m2, 14)}[fmt]
    v = np.moveaxis(np.asarray(x, np.float32).astype(ml_dtypes.bfloat16).astype(np.float64), axis, -1)
    blocks = v.reshape(v.shape[:-1] + (-1, 32))
    amax = np.abs(blocks).max(-1, keepdims=True)
    byte = np.maximum(np.where(amax > 0, np.frexp(amax)[1] - 1 + 127, 0) - down, 1)
    scale = np.exp2(byte - 127.0)
    codes = (blocks / scale).astype(np.float32).astype(dtype).astype(np.float64)
    return np.moveaxis((codes * scale).reshape(v.shape), -1, axis)


WIDE = False


def mx_kscale(k):
    if not WIDE:
        return np.ones(k)
    levels = np.array([10, -10, 5, -5, 0])
    if k % 512:
        return np.exp2(np.random.permutation(np.resize(levels, k // 32))).repeat(32)
    a = np.empty((k // 512, 16))
    for p in range(k // 512):
        a[p, :8] = np.random.permutation(np.resize(levels, 8))
        for g in range(8):
            far = levels[np.abs(levels - a[p, g]) >= 10]
            a[p, g + 8] = far[np.random.randint(len(far))]
    return np.exp2(a.ravel()).repeat(32)


def f64(x):
    return np.asarray(x).astype(np.float64)


def striped(idx):
    return np.tile(idx.reshape(-1, 16).T, (8, 1)).astype(np.uint16)


def unstriped(offs):
    return offs[:16].T.reshape(-1).astype(np.int64)


def relu2(v):
    return np.maximum(v, 0.0) ** 2


K, T, E, C, H, N = 512, 512, 8, 256, 512, 256
TOP = 4


def by_expert(wq, xq):
    return np.concatenate([wq[e].T @ xq[:, e * C:(e + 1) * C] for e in range(E)], axis=1)


def setup_inputs():
    n = np.random.standard_normal
    s = mx_kscale(K)[:, None]
    u = mx_kscale(H)
    deal = np.repeat(np.arange(E), C).reshape(TOP, T)[:, np.random.permutation(T)]
    deal = np.take_along_axis(deal, np.argsort(np.random.rand(TOP, T), axis=0), axis=0)
    for _ in range(8):
        s_, t_ = np.random.permutation(T).reshape(2, -1); r = np.random.randint(TOP, size=T // 2); x, y = deal[r, s_].copy(), deal[r, t_].copy()
        ok = ~((deal[:, s_] == y).any(0) | (deal[:, t_] == x).any(0)); deal[r[ok], s_[ok]] = y[ok]; deal[r[ok], t_[ok]] = x[ok]
    order = np.lexsort((np.random.rand(TOP * T), deal.reshape(-1)))
    slot_token = order % T; pos = np.empty(TOP * T, np.int64); pos[order] = np.arange(TOP * T); pos = pos.reshape(TOP, T)
    g = np.random.uniform(0.5, 1.5, (TOP, T)); g = g / g.sum(0)
    return {
        "xT": (n((K, T)) * s).astype(np.float32),
        "w1": (n((E, K, H)) / np.sqrt(K) / s[None] * u[None, None, :]).astype(np.float32),
        "w2": (n((E, H, N)) / np.sqrt(H) / u[None, :, None] ** 2).astype(np.float32),
        "gate": np.stack([np.tile(r, (N, 1)) for r in g]).astype(np.float32),
        "offs": striped(slot_token),
        "pos1": striped(pos[0]),
        "pos2": striped(pos[1]),
        "pos3": striped(pos[2]),
        "pos4": striped(pos[3]),
    }


def reference(xT, w1, w2, gate, offs, pos1, pos2, pos3, pos4):
    idx = unstriped(offs)
    xq = mxq(f64(xT)[:, idx], 0, "e4m3")
    h = relu2(by_expert(mxq(f64(w1), 1, "e4m3"), xq))
    y = by_expert(mxq(f64(w2), 1, "e4m3"), mxq(h, 0, "e4m3"))
    return sum(f64(gate[r]) * y[:, unstriped(p)] for r, p in enumerate((pos1, pos2, pos3, pos4)))

@@ -1,0 +1,214 @@
+from contextlib import ExitStack
+
+import concourse.mybir as mybir
+
+K, T, E, C, H, N = 512, 512, 8, 256, 512, 256
+TOP = 4
+P = 128
+PACK = 4
+FLOPS = 2 * E * C * (K * H + H * N)
+
+F32 = mybir.dt.float32
+BF16 = mybir.dt.bfloat16
+U32 = mybir.dt.uint32
+U16 = mybir.dt.uint16
+U8 = mybir.dt.uint8
+FP8X4 = mybir.dt.float8_e4m3fn_x4
+MULT = mybir.AluOpType.mult
+ADD = mybir.AluOpType.add
+RELU = mybir.ActivationFunctionType.Relu
+SQUARE = mybir.ActivationFunctionType.Square
+
+W1_VECTOR = (0, 48, 128, 128, 128, 0, 112, 128)
+SQUARE_ON_VECTOR = ()
+W2_ON_VECTOR = ((0, 0), (0, 2), (0, 3), (1, 0), (1, 1),)
+PIECE = 384
+
+
+def tile_moe_tk_mlp_relu2_kernel(tc, xT, w1, w2, gate, offs, pos1, pos2, pos3, pos4, out):
+    nc = tc.nc
+    pos = (pos1, pos2, pos3, pos4)
+    with ExitStack() as ctx:
+        keep = ctx.enter_context(tc.tile_pool(name="keep", bufs=1))
+        stage = ctx.enter_context(tc.tile_pool(name="stage", bufs=2))
+        grouped = ctx.enter_context(tc.tile_pool(name="grouped", bufs=3))
+        slots_pool = ctx.enter_context(tc.tile_pool(name="slots", bufs=2))
+        grouped2 = ctx.enter_context(tc.tile_pool(name="grouped2", bufs=4))
+        codes2 = ctx.enter_context(tc.tile_pool(name="codes2", bufs=5))
+        sums = ctx.enter_context(tc.tile_pool(name="sums", bufs=1))
+        codes = ctx.enter_context(tc.tile_pool(name="codes", bufs=3))
+        psum1 = ctx.enter_context(tc.psum_pool(name="psum1", bufs=4))
+        psum2 = ctx.enter_context(tc.psum_pool(name="psum2", bufs=4))
+
+        xs = keep.tile([P, T], U8, name="xs", align_bytes=64)
+        nc.gpsimd.memset(xs[:], 0)
+        x_view = xT.rearrange("(p j) t -> p j t", j=PACK)
+        x_raw = []
+        for c in range(2):
+            t_ = keep.tile([P, PACK, T // 2], F32, name=f"x_raw{c}", align_bytes=64)
+            nc.sync.dma_start(out=t_[:], in_=x_view[:, :, c * (T // 2) : (c + 1) * (T // 2)])
+            x_raw.append(t_)
+        offs_t = keep.tile([P, E * C // 16], U16, name="offs_t")
+        nc.sync.dma_start(offs_t[:], offs)
+        w1_raw = []
+        for e in range(E):
+            n_parts = 2 if e == 0 else 1
+            parts = []
+            for i in range(n_parts):
+                width = H // n_parts
+                t_ = keep.tile([P, PACK, width], F32, name=f"w1_raw{e}_{i}", align_bytes=64)
+                nc.sync.dma_start(out=t_[:], in_=w1[e].rearrange("(p j) c -> p j c", j=PACK)[:, :, i * width : (i + 1) * width])
+                parts.append(t_)
+            w1_raw.append(parts)
+        w2_raw = []
+        for q in range(E // 2):
+            t_ = keep.tile([P, 2, PACK, N], F32, name=f"w2_raw{q}", align_bytes=64)
+            nc.sync.dma_start(out=t_[:], in_=w2[2 * q : 2 * q + 2].rearrange("i (p j) n -> p i j n", j=PACK))
+            w2_raw.append(t_)
+        pos_t = []
+        for r in range(TOP):
+            t_ = keep.tile([P, T // 16], U16, name=f"pos_t{r}")
+            nc.sync.dma_start(t_[:], pos[r])
+            pos_t.append(t_)
+        gates = []
+        for h in range(2):
+            t_ = keep.tile([P, TOP, T], F32, name=f"gates{h}", align_bytes=64)
+            nc.sync.dma_start(out=t_[:], in_=gate[:, h * P : (h + 1) * P, :].rearrange("r p t -> p r t"))
+            gates.append(t_)
+
+        xw = keep.tile([P, T], U32, name="xw", align_bytes=64)
+        for c in range(2):
+            xg = keep.tile([P, T // 2, PACK], BF16, name=f"xg{c}", align_bytes=64)
+            nc.vector.tensor_copy(
+                out=xg[:].rearrange("p (c i) j -> p c j i", i=2),
+                in_=x_raw[c][:].rearrange("p j (c i) -> p c j i", i=2),
+            )
+            cols = slice(c * (T // 2), (c + 1) * (T // 2))
+            nc.vector.quantize_mx(out=xw[:, cols].bitcast(FP8X4), scales=xs[:, cols], in_=xg[:].rearrange("p c j -> p (c j)"))
+
+        hb_pair, h_codes, h_scales, pieces, first = [], [], [], [], [0]
+
+        def w1_copy(e):
+            g = grouped.tile([P, PACK * H], BF16, name="w1_grouped", align_bytes=64)
+            dst = g[:].rearrange("p (t m j) -> p m j t", t=4, j=PACK)
+            if e == 0:
+                a0, a1 = [t_[:].rearrange("p j (m t) -> p m j t", t=4) for t_ in w1_raw[e]]
+                nc.scalar.copy(out=dst[:, : P // 2], in_=a0)
+                nc.scalar.copy(out=dst[:, P // 2 :], in_=a1)
+                return g
+            src = w1_raw[e][0][:].rearrange("p j (m t) -> p m j t", t=4)
+            v = W1_VECTOR[e]
+            if v < P:
+                nc.scalar.copy(out=dst[:, v:], in_=src[:, v:])
+            if v > 0:
+                nc.vector.tensor_copy(out=dst[:, :v], in_=src[:, :v])
+            return g
+
+        def expert_first(e):
+            g = w1_copy(e)
+            while len(pieces) * PIECE < (e + 1) * C:
+                s0 = len(pieces) * PIECE
+                s1 = min(s0 + PIECE, E * C)
+                xe = slots_pool.tile([P, PIECE], U32, name="xe", align_bytes=64)
+                xse = slots_pool.tile([P, PIECE], U8, name="xse", align_bytes=64)
+                lst = offs_t[:, s0 // 16 : s1 // 16]
+                nc.vector.tensor_copy(xe[:, : s1 - s0], xw[:].indirect(lst))
+                nc.vector.tensor_copy(xse[:, : s1 - s0], xs[:].indirect(lst))
+                pieces.append((xe, xse))
+            wc = codes.tile([P, H], U32, name="w1_codes", align_bytes=64)
+            ws = codes.tile([P, H], U8, name="w1_scales", align_bytes=64)
+            nc.vector.quantize_mx(out=wc[:].bitcast(FP8X4), scales=ws[:], in_=g[:])
+            pos_part = stage.tile([P, C, PACK], F32, name="pos_part", align_bytes=64)
+            for b in range(2):
+                ps = psum1.tile([P, PACK, P], F32, name="ps1")
+                cols = slice(b * P, (b + 1) * P)
+                s0 = e * C + b * P
+                xe, xse = pieces[s0 // PIECE]
+                part = slice(s0 % PIECE, s0 % PIECE + P)
+                for t in range(PACK):
+                    m = slice(t * P, (t + 1) * P)
+                    nc.tensor.matmul_mx(
+                        out=ps[:, t, :], lhsT=wc[:, m].bitcast(FP8X4), lhsT_scale=ws[:, m],
+                        rhs=xe[:, part].bitcast(FP8X4), rhs_scale=xse[:, part], start=True, stop=True,
+                    )
+                nc.scalar.activation(pos_part[:, cols, :], ps[:].rearrange("p t n -> p n t"), RELU)
+            if e in (0, 4, 6):
+                n = 4 if e == 0 else 2
+                first[0] = e
+                hb_pair.append(keep.tile([P, n * C * PACK], BF16, name=f"hb{e}", align_bytes=64))
+                h_codes.append(keep.tile([P, n * C], U32, name=f"h_codes{e}", align_bytes=64))
+                h_scales.append(keep.tile([P, n * C], U8, name=f"h_scales{e}", align_bytes=64))
+            i = e - first[0]
+            hb = hb_pair[-1][:, i * C * PACK : (i + 1) * C * PACK]
+            flat = pos_part[:].rearrange("p n t -> p (n t)")
+            if e in SQUARE_ON_VECTOR:
+                nc.vector.tensor_tensor(hb, flat, flat, MULT)
+            else:
+                nc.scalar.activation(hb, flat, SQUARE)
+            if e >= 6:
+                cols, src = slice(i * C, (i + 1) * C), hb
+            elif e in (3, 5):
+                cols, src = slice(0, (i + 1) * C), hb_pair[-1][:]
+            else:
+                return
+            nc.vector.quantize_mx(out=h_codes[-1][:, cols].bitcast(FP8X4), scales=h_scales[-1][:, cols], in_=src)
+
+        y = [keep.tile([P, E * C], F32, name=f"y{h}") for h in range(2)]
+
+        def pair_second(q, h):
+            g = grouped2.tile([P, 2, P, PACK], BF16, name="w2_grouped", align_bytes=64)
+            dst = g[:].rearrange("p e (c i) j -> p e c j i", i=2)
+            src = w2_raw[q][:, :, :, h * P : (h + 1) * P].rearrange("p e j (c i) -> p e c j i", i=2)
+            if (h, q) in W2_ON_VECTOR:
+                nc.vector.tensor_copy(out=dst, in_=src)
+            else:
+                nc.scalar.copy(out=dst, in_=src)
+            wc = codes2.tile([P, 2 * P], U32, name="w2_codes", align_bytes=64)
+            ws = codes2.tile([P, 2 * P], U8, name="w2_scales", align_bytes=64)
+            nc.vector.quantize_mx(out=wc[:].bitcast(FP8X4), scales=ws[:], in_=g[:].rearrange("p i c j -> p (i c j)"))
+            ps = psum2.tile([P, 2, C], F32, name="ps2")
+            for i in range(2):
+                m = slice(i * P, (i + 1) * P)
+                k = q if q > 1 else 0
+                k = 0 if q < 2 else q - 1
+                e0 = (2 * q if q < 2 else 0) + i
+                cols = slice(e0 * C, (e0 + 1) * C)
+                nc.tensor.matmul_mx(
+                    out=ps[:, i, :], lhsT=wc[:, m].bitcast(FP8X4), lhsT_scale=ws[:, m],
+                    rhs=h_codes[k][:, cols].bitcast(FP8X4), rhs_scale=h_scales[k][:, cols], start=True, stop=True,
+                )
+            nc.scalar.copy(out=y[h][:, 2 * q * C : (2 * q + 2) * C], in_=ps[:].rearrange("p i c -> p (i c)"))
+
+        def combine(h):
+            prod = [sums.tile([P, T], F32, name=f"prod{r}") for r in range(TOP)]
+
+            def fetch(r, t0, t1):
+                nc.vector.tensor_tensor(
+                    prod[r][:, t0:t1], y[h][:].indirect(pos_t[r][:, t0 // 16 : t1 // 16]), gates[h][:, r, t0:t1], MULT
+                )
+
+            s01 = sums.tile([P, T], F32, name="s01")
+            s23 = sums.tile([P, T], F32, name="s23")
+            res = sums.tile([P, T], F32, name="res")
+            for r in range(TOP):
+                fetch(r, 0, T)
+            nc.vector.tensor_tensor(s01[:], prod[0][:], prod[1][:], ADD)
+            halves = [slice(c * (T // 2), (c + 1) * (T // 2)) for c in range(2)]
+            for cols in halves:
+                nc.vector.tensor_tensor(s23[:, cols], prod[2][:, cols], prod[3][:, cols], ADD)
+            for cols in halves:
+                nc.vector.tensor_tensor(res[:, cols], s01[:, cols], s23[:, cols], ADD)
+                nc.sync.dma_start(out[h * P : (h + 1) * P, cols], res[:, cols])
+
+        early = {0: 6, 1: 7, 2: 7}
+        for e in range(E):
+            expert_first(e)
+            for q in early:
+                if early[q] == e:
+                    pair_second(q, 0)
+        for h in range(2):
+            for q in range(E // 2):
+                if h == 1 or q not in early:
+                    pair_second(q, h)
+        for h in range(2):
+            combine(h)

@@ -1,15 +1,18 @@
 from contextlib import ExitStack
 
 import concourse.mybir as mybir
+from concourse.masks import make_identity
 
 K, T, E, C, H, N = 512, 512, 8, 256, 512, 256
 TOP = 4
 P = 128
 PACK = 4
+PAIRS = E // 2
 FLOPS = 2 * E * C * (K * H + H * N)
 
 F32 = mybir.dt.float32
 BF16 = mybir.dt.bfloat16
+I32 = mybir.dt.int32
 U32 = mybir.dt.uint32
 U16 = mybir.dt.uint16
 U8 = mybir.dt.uint8
@@ -19,10 +22,7 @@ ADD = mybir.AluOpType.add
 RELU = mybir.ActivationFunctionType.Relu
 SQUARE = mybir.ActivationFunctionType.Square
 
-W1_VECTOR = (0, 48, 128, 128, 128, 0, 112, 128)
-SQUARE_ON_VECTOR = ()
-W2_ON_VECTOR = ((0, 0), (0, 2), (0, 3), (1, 0), (1, 1),)
-PIECE = 384
+W1_SCALAR = 40
 
 
 def tile_moe_tk_mlp_relu2_kernel(tc, xT, w1, w2, gate, offs, pos1, pos2, pos3, pos4, out):
@@ -31,17 +31,14 @@ def tile_moe_tk_mlp_relu2_kernel(tc, xT, w1, w2, gate, offs, pos1, pos2, pos3, p
     with ExitStack() as ctx:
         keep = ctx.enter_context(tc.tile_pool(name="keep", bufs=1))
         stage = ctx.enter_context(tc.tile_pool(name="stage", bufs=2))
-        grouped = ctx.enter_context(tc.tile_pool(name="grouped", bufs=3))
-        slots_pool = ctx.enter_context(tc.tile_pool(name="slots", bufs=2))
-        grouped2 = ctx.enter_context(tc.tile_pool(name="grouped2", bufs=4))
-        codes2 = ctx.enter_context(tc.tile_pool(name="codes2", bufs=5))
-        sums = ctx.enter_context(tc.tile_pool(name="sums", bufs=1))
-        codes = ctx.enter_context(tc.tile_pool(name="codes", bufs=3))
-        psum1 = ctx.enter_context(tc.psum_pool(name="psum1", bufs=4))
-        psum2 = ctx.enter_context(tc.psum_pool(name="psum2", bufs=4))
+        psum = ctx.enter_context(tc.psum_pool(name="psum", bufs=8))
 
-        xs = keep.tile([P, T], U8, name="xs", align_bytes=64)
-        nc.gpsimd.memset(xs[:], 0)
+        xs = keep.tile([P, 2 * T], U8, name="xs", align_bytes=64)
+        nc.gpsimd.memset(xs[:].bitcast(I32), 0)
+        xw = keep.tile([P, 2 * T], I32, name="xw", align_bytes=64)
+        nc.vector.memset(xw[:, T:], 0)
+        ident = keep.tile([P, P], F32, name="ident")
+        make_identity(nc, ident[:])
         x_view = xT.rearrange("(p j) t -> p j t", j=PACK)
         x_raw = []
         for c in range(2):
@@ -52,7 +49,7 @@ def tile_moe_tk_mlp_relu2_kernel(tc, xT, w1, w2, gate, offs, pos1, pos2, pos3, p
         nc.sync.dma_start(offs_t[:], offs)
         w1_raw = []
         for e in range(E):
-            n_parts = 2 if e == 0 else 1
+            n_parts = 2 if e < 2 else 1
             parts = []
             for i in range(n_parts):
                 width = H // n_parts
@@ -60,23 +57,19 @@ def tile_moe_tk_mlp_relu2_kernel(tc, xT, w1, w2, gate, offs, pos1, pos2, pos3, p
                 nc.sync.dma_start(out=t_[:], in_=w1[e].rearrange("(p j) c -> p j c", j=PACK)[:, :, i * width : (i + 1) * width])
                 parts.append(t_)
             w1_raw.append(parts)
-        w2_raw = []
-        for q in range(E // 2):
-            t_ = keep.tile([P, 2, PACK, N], F32, name=f"w2_raw{q}", align_bytes=64)
-            nc.sync.dma_start(out=t_[:], in_=w2[2 * q : 2 * q + 2].rearrange("i (p j) n -> p i j n", j=PACK))
-            w2_raw.append(t_)
+        w2_raw = keep.tile([P, E, PACK, N], F32, name="w2_raw", align_bytes=64)
+        for q in range(PAIRS):
+            nc.sync.dma_start(
+                out=w2_raw[:, 2 * q : 2 * q + 2], in_=w2[2 * q : 2 * q + 2].rearrange("i (p j) n -> p i j n", j=PACK)
+            )
         pos_t = []
         for r in range(TOP):
             t_ = keep.tile([P, T // 16], U16, name=f"pos_t{r}")
             nc.sync.dma_start(t_[:], pos[r])
             pos_t.append(t_)
-        gates = []
-        for h in range(2):
-            t_ = keep.tile([P, TOP, T], F32, name=f"gates{h}", align_bytes=64)
-            nc.sync.dma_start(out=t_[:], in_=gate[:, h * P : (h + 1) * P, :].rearrange("r p t -> p r t"))
-            gates.append(t_)
+        gates = keep.tile([P, TOP, T], F32, name="gates", align_bytes=64)
+        nc.sync.dma_start(out=gates[:], in_=gate[:, :P, :].rearrange("r p t -> p r t"))
 
-        xw = keep.tile([P, T], U32, name="xw", align_bytes=64)
         for c in range(2):
             xg = keep.tile([P, T // 2, PACK], BF16, name=f"xg{c}", align_bytes=64)
             nc.vector.tensor_copy(
@@ -86,129 +79,171 @@ def tile_moe_tk_mlp_relu2_kernel(tc, xT, w1, w2, gate, offs, pos1, pos2, pos3, p
             cols = slice(c * (T // 2), (c + 1) * (T // 2))
             nc.vector.quantize_mx(out=xw[:, cols].bitcast(FP8X4), scales=xs[:, cols], in_=xg[:].rearrange("p c j -> p (c j)"))
 
-        hb_pair, h_codes, h_scales, pieces, first = [], [], [], [], [0]
+        w1_grouped, slot_words, slot_scales, banks, y_banks = {}, {}, {}, {}, {}
+        h_codes, h_scales, w2_codes, w2_scales = {}, {}, {}, {}
+        h_bf = [keep.tile([P, 2 * C * PACK], BF16, name=f"h_bf{q}", align_bytes=64) for q in range(PAIRS)]
+        y = [keep.tile([P, E * C], F32, name=f"y{h}") for h in range(2)]
 
         def w1_copy(e):
-            g = grouped.tile([P, PACK * H], BF16, name="w1_grouped", align_bytes=64)
+            g = stage.tile([P, PACK * H], BF16, name="w1_grouped", align_bytes=64)
+            w1_grouped[e] = g
             dst = g[:].rearrange("p (t m j) -> p m j t", t=4, j=PACK)
-            if e == 0:
-                a0, a1 = [t_[:].rearrange("p j (m t) -> p m j t", t=4) for t_ in w1_raw[e]]
-                nc.scalar.copy(out=dst[:, : P // 2], in_=a0)
-                nc.scalar.copy(out=dst[:, P // 2 :], in_=a1)
-                return g
+            if e < 2:
+                for i in range(2):
+                    nc.scalar.copy(
+                        out=dst[:, i * P // 2 : (i + 1) * P // 2], in_=w1_raw[e][i][:].rearrange("p j (m t) -> p m j t", t=4)
+                    )
+                return
             src = w1_raw[e][0][:].rearrange("p j (m t) -> p m j t", t=4)
-            v = W1_VECTOR[e]
-            if v < P:
-                nc.scalar.copy(out=dst[:, v:], in_=src[:, v:])
-            if v > 0:
-                nc.vector.tensor_copy(out=dst[:, :v], in_=src[:, :v])
-            return g
+            nc.scalar.copy(out=dst[:, :W1_SCALAR], in_=src[:, :W1_SCALAR])
+            nc.vector.tensor_copy(out=dst[:, W1_SCALAR:], in_=src[:, W1_SCALAR:])
 
-        def expert_first(e):
-            g = w1_copy(e)
-            while len(pieces) * PIECE < (e + 1) * C:
-                s0 = len(pieces) * PIECE
-                s1 = min(s0 + PIECE, E * C)
-                xe = slots_pool.tile([P, PIECE], U32, name="xe", align_bytes=64)
-                xse = slots_pool.tile([P, PIECE], U8, name="xse", align_bytes=64)
-                lst = offs_t[:, s0 // 16 : s1 // 16]
-                nc.vector.tensor_copy(xe[:, : s1 - s0], xw[:].indirect(lst))
-                nc.vector.tensor_copy(xse[:, : s1 - s0], xs[:].indirect(lst))
-                pieces.append((xe, xse))
-            wc = codes.tile([P, H], U32, name="w1_codes", align_bytes=64)
-            ws = codes.tile([P, H], U8, name="w1_scales", align_bytes=64)
-            nc.vector.quantize_mx(out=wc[:].bitcast(FP8X4), scales=ws[:], in_=g[:])
-            pos_part = stage.tile([P, C, PACK], F32, name="pos_part", align_bytes=64)
+        def pair_list(q):
+            return offs_t[:, 2 * q * C // 16 : (2 * q + 2) * C // 16]
+
+        def gather_words(q):
+            tag = "slot_words0" if q == 0 else ("w1_raw0_1" if q == 1 else f"w1_raw{2 * q - 2}_0")
+            slot_words[q] = keep.tile([P, 2 * C], U32, name=f"slot_words{q}", tag=tag, align_bytes=64)
+            nc.vector.tensor_copy(slot_words[q][:], xw[:].bitcast(U32).indirect(pair_list(q)))
+
+        def gather_scales(q):
+            tag = "slot_scales0" if q == 0 else ("w1_raw1_1" if q == 1 else f"w1_raw{2 * q - 1}_0")
+            slot_scales[q] = keep.tile([P, 2 * C], U8, name=f"slot_scales{q}", tag=tag, align_bytes=64)
+            nc.vector.tensor_copy(slot_scales[q][:], xs[:].indirect(pair_list(q)))
+
+        def first_product(e):
+            wc = stage.tile([P, H], U32, name="w1_codes", align_bytes=64)
+            ws = stage.tile([P, H], U8, name="w1_scales", align_bytes=64)
+            nc.vector.quantize_mx(out=wc[:].bitcast(FP8X4), scales=ws[:], in_=w1_grouped[e][:])
+            banks[e] = []
             for b in range(2):
-                ps = psum1.tile([P, PACK, P], F32, name="ps1")
-                cols = slice(b * P, (b + 1) * P)
-                s0 = e * C + b * P
-                xe, xse = pieces[s0 // PIECE]
-                part = slice(s0 % PIECE, s0 % PIECE + P)
+                ps = psum.tile([P, PACK, P], F32, name="bank")
+                part = slice((e % 2) * C + b * P, (e % 2) * C + (b + 1) * P)
                 for t in range(PACK):
                     m = slice(t * P, (t + 1) * P)
                     nc.tensor.matmul_mx(
                         out=ps[:, t, :], lhsT=wc[:, m].bitcast(FP8X4), lhsT_scale=ws[:, m],
-                        rhs=xe[:, part].bitcast(FP8X4), rhs_scale=xse[:, part], start=True, stop=True,
+                        rhs=slot_words[e // 2][:, part].bitcast(FP8X4), rhs_scale=slot_scales[e // 2][:, part],
+                        start=True, stop=True,
                     )
-                nc.scalar.activation(pos_part[:, cols, :], ps[:].rearrange("p t n -> p n t"), RELU)
-            if e in (0, 4, 6):
-                n = 4 if e == 0 else 2
-                first[0] = e
-                hb_pair.append(keep.tile([P, n * C * PACK], BF16, name=f"hb{e}", align_bytes=64))
-                h_codes.append(keep.tile([P, n * C], U32, name=f"h_codes{e}", align_bytes=64))
-                h_scales.append(keep.tile([P, n * C], U8, name=f"h_scales{e}", align_bytes=64))
-            i = e - first[0]
-            hb = hb_pair[-1][:, i * C * PACK : (i + 1) * C * PACK]
-            flat = pos_part[:].rearrange("p n t -> p (n t)")
-            if e in SQUARE_ON_VECTOR:
-                nc.vector.tensor_tensor(hb, flat, flat, MULT)
-            else:
-                nc.scalar.activation(hb, flat, SQUARE)
-            if e >= 6:
-                cols, src = slice(i * C, (i + 1) * C), hb
-            elif e in (3, 5):
-                cols, src = slice(0, (i + 1) * C), hb_pair[-1][:]
-            else:
-                return
-            nc.vector.quantize_mx(out=h_codes[-1][:, cols].bitcast(FP8X4), scales=h_scales[-1][:, cols], in_=src)
+                banks[e].append(ps)
 
-        y = [keep.tile([P, E * C], F32, name=f"y{h}") for h in range(2)]
+        def squared_relu(e):
+            pos_part = stage.tile([P, C, PACK], F32, name="pos_part", align_bytes=64)
+            for b in range(2):
+                nc.scalar.activation(pos_part[:, b * P : (b + 1) * P, :], banks[e][b][:].rearrange("p t n -> p n t"), RELU)
+            mine = slice((e % 2) * C * PACK, (e % 2 + 1) * C * PACK)
+            nc.scalar.activation(h_bf[e // 2][:, mine], pos_part[:].rearrange("p n t -> p (n t)"), SQUARE)
 
-        def pair_second(q, h):
-            g = grouped2.tile([P, 2, P, PACK], BF16, name="w2_grouped", align_bytes=64)
+        def quantise_h(e0, e1, tag):
+            hc = keep.tile([P, (e1 - e0) * C], U32, name=f"h_codes{e0}", tag=tag, align_bytes=64)
+            hs = keep.tile([P, (e1 - e0) * C], U8, name=f"h_scales{e0}", align_bytes=64)
+            first = (e0 % 2) * C * PACK
+            nc.vector.quantize_mx(
+                out=hc[:].bitcast(FP8X4), scales=hs[:], in_=h_bf[e0 // 2][:, first : first + (e1 - e0) * C * PACK]
+            )
+            for e in range(e0, e1):
+                h_codes[e], h_scales[e] = hc[:, (e - e0) * C : (e - e0 + 1) * C], hs[:, (e - e0) * C : (e - e0 + 1) * C]
+
+        def quantise_w2(h, e0, e1, on_vector, layout_pool, layout_tag):
+            n_e = e1 - e0
+            g = layout_pool.tile([P, n_e, P, PACK], BF16, name="w2_grouped", tag=layout_tag, align_bytes=64)
             dst = g[:].rearrange("p e (c i) j -> p e c j i", i=2)
-            src = w2_raw[q][:, :, :, h * P : (h + 1) * P].rearrange("p e j (c i) -> p e c j i", i=2)
-            if (h, q) in W2_ON_VECTOR:
+            src = w2_raw[:, e0:e1, :, h * P : (h + 1) * P].rearrange("p e j (c i) -> p e c j i", i=2)
+            if on_vector:
                 nc.vector.tensor_copy(out=dst, in_=src)
             else:
                 nc.scalar.copy(out=dst, in_=src)
-            wc = codes2.tile([P, 2 * P], U32, name="w2_codes", align_bytes=64)
-            ws = codes2.tile([P, 2 * P], U8, name="w2_scales", align_bytes=64)
+            wc = keep.tile([P, n_e * P], U32, name=f"w2_codes{h}_{e0}", align_bytes=64)
+            ws = keep.tile([P, n_e * P], U8, name=f"w2_scales{h}_{e0}", align_bytes=64)
             nc.vector.quantize_mx(out=wc[:].bitcast(FP8X4), scales=ws[:], in_=g[:].rearrange("p i c j -> p (i c j)"))
-            ps = psum2.tile([P, 2, C], F32, name="ps2")
+            for e in range(e0, e1):
+                w2_codes[h, e], w2_scales[h, e] = wc[:, (e - e0) * P : (e - e0 + 1) * P], ws[:, (e - e0) * P : (e - e0 + 1) * P]
+
+        def second_product(h, q):
+            ps = psum.tile([P, 2, C], F32, name="bank")
             for i in range(2):
-                m = slice(i * P, (i + 1) * P)
-                k = q if q > 1 else 0
-                k = 0 if q < 2 else q - 1
-                e0 = (2 * q if q < 2 else 0) + i
-                cols = slice(e0 * C, (e0 + 1) * C)
+                e = 2 * q + i
                 nc.tensor.matmul_mx(
-                    out=ps[:, i, :], lhsT=wc[:, m].bitcast(FP8X4), lhsT_scale=ws[:, m],
-                    rhs=h_codes[k][:, cols].bitcast(FP8X4), rhs_scale=h_scales[k][:, cols], start=True, stop=True,
+                    out=ps[:, i, :], lhsT=w2_codes[h, e].bitcast(FP8X4), lhsT_scale=w2_scales[h, e],
+                    rhs=h_codes[e].bitcast(FP8X4), rhs_scale=h_scales[e], start=True, stop=True,
                 )
-            nc.scalar.copy(out=y[h][:, 2 * q * C : (2 * q + 2) * C], in_=ps[:].rearrange("p i c -> p (i c)"))
+            y_banks[q, h] = ps
 
-        def combine(h):
-            prod = [sums.tile([P, T], F32, name=f"prod{r}") for r in range(TOP)]
+        def y_copy(q, h):
+            nc.scalar.copy(out=y[h][:, 2 * q * C : (2 * q + 2) * C], in_=y_banks[q, h][:].rearrange("p i c -> p (i c)"))
 
-            def fetch(r, t0, t1):
-                nc.vector.tensor_tensor(
-                    prod[r][:, t0:t1], y[h][:].indirect(pos_t[r][:, t0 // 16 : t1 // 16]), gates[h][:, r, t0:t1], MULT
+        def fetch(h, r, tag):
+            prod = keep.tile([P, T], F32, name=f"prod{h}_{r}", tag=tag, align_bytes=64)
+            nc.vector.tensor_tensor(prod[:], y[h][:].indirect(pos_t[r][:]), gates[:, r, :], MULT)
+            return prod
+
+        def add_turned(acc, prod, first, last):
+            for c in range(T // P):
+                nc.tensor.matmul(
+                    acc[c][:], lhsT=prod[:, c * P : (c + 1) * P], rhs=ident[:], is_transpose=True, start=first, stop=last
                 )
 
-            s01 = sums.tile([P, T], F32, name="s01")
-            s23 = sums.tile([P, T], F32, name="s23")
-            res = sums.tile([P, T], F32, name="res")
-            for r in range(TOP):
-                fetch(r, 0, T)
-            nc.vector.tensor_tensor(s01[:], prod[0][:], prod[1][:], ADD)
-            halves = [slice(c * (T // 2), (c + 1) * (T // 2)) for c in range(2)]
-            for cols in halves:
-                nc.vector.tensor_tensor(s23[:, cols], prod[2][:, cols], prod[3][:, cols], ADD)
-            for cols in halves:
-                nc.vector.tensor_tensor(res[:, cols], s01[:, cols], s23[:, cols], ADD)
-                nc.sync.dma_start(out[h * P : (h + 1) * P, cols], res[:, cols])
+        def turn_back(acc, tag):
+            turned = keep.tile([P, T // P, P], F32, name="turned", tag=tag, align_bytes=64)
+            back = psum.tile([P, T // P, P], F32, name="bank")
+            for c in range(T // P):
+                nc.scalar.copy(out=turned[:, c, :], in_=acc[c][:])
+                nc.tensor.transpose(back[:, c, :], turned[:, c, :], ident[:])
+            return back[:].rearrange("p c t -> p (c t)")
 
-        early = {0: 6, 1: 7, 2: 7}
+        gather_words(0)
+        gather_scales(0)
+        w1_copy(0)
+        first_product(0)
+        w1_copy(1)
+        gather_words(1)
         for e in range(E):
-            expert_first(e)
-            for q in early:
-                if early[q] == e:
-                    pair_second(q, 0)
-        for h in range(2):
-            for q in range(E // 2):
-                if h == 1 or q not in early:
-                    pair_second(q, h)
-        for h in range(2):
-            combine(h)
+            squared_relu(e)
+            if e + 1 < E:
+                first_product(e + 1)
+            if e % 2 == 0 and e + 2 < E:
+                gather_scales(e // 2 + 1)
+            if e % 2 == 1 and e + 3 < E:
+                gather_words(e // 2 + 2)
+            if e + 2 < E:
+                w1_copy(e + 2)
+            if e == E - 2:
+                quantise_h(e, e + 1, "h_codes6")
+            elif e % 2 == 1 and e < E - 1:
+                quantise_h(e - 1, e + 1, f"h_codes{e - 1}")
+        quantise_w2(0, 0, E // 2, True, stage, "w1_grouped")
+        quantise_w2(0, E // 2, E, True, keep, "w2_last")
+        quantise_h(E - 1, E, "w2_last")
+        for q in range(PAIRS):
+            second_product(0, q)
+        for q in range(PAIRS):
+            y_copy(q, 0)
+        quantise_w2(1, 0, E // 2, True, keep, "h_bf3")
+        quantise_w2(1, E // 2, E, False, keep, "w2_codes0_4")
+        for q in range(PAIRS):
+            second_product(1, q)
+        for q in range(PAIRS):
+            y_copy(q, 1)
+
+        acc = [psum.tile([P, P], F32, name="bank") for c in range(T // P)]
+        for r, tag in enumerate(("prod0_0", "prod0_1", "w2_codes0_4", "prod0_3")):
+            add_turned(acc, fetch(0, r, tag), r == 0, r == TOP - 1)
+        back0 = turn_back(acc, "w2_codes1_4")
+        res0 = keep.tile([P, T], F32, name="res0")
+        nc.scalar.copy(out=res0[:], in_=back0)
+        nc.sync.dma_start(out[:P, :], res0[:])
+
+        acc = [psum.tile([P, P], F32, name="bank") for c in range(T // P)]
+        for r in range(2):
+            add_turned(acc, fetch(1, r, f"prod1_{r}"), r == 0, r == 1)
+        back1 = turn_back(acc, "turned1")
+        prod2 = fetch(1, 2, "prod1_2")
+        prod3 = fetch(1, 3, "prod1_3")
+        s23 = keep.tile([P, T], F32, name="s23")
+        res1 = keep.tile([P, T], F32, name="res1")
+        nc.vector.tensor_tensor(s23[:], prod2[:], prod3[:], ADD)
+        for c in range(2):
+            cols = slice(c * (T // 2), (c + 1) * (T // 2))
+            nc.vector.tensor_tensor(res1[:, cols], back1[:, cols], s23[:, cols], ADD)
+            nc.sync.dma_start(out[P:, cols], res1[:, cols])

@@ -39,21 +39,18 @@ def tile_moe_tk_mlp_relu2_kernel(tc, xT, w1, w2, gate, offs, pos1, pos2, pos3, p
         nc.vector.memset(xw[:, T:], 0)
         ident = keep.tile([P, P], F32, name="ident")
         make_identity(nc, ident[:])
-        x_view = xT.rearrange("(p j) t -> p j t", j=PACK)
-        x_raw = []
-        for c in range(2):
-            t_ = keep.tile([P, PACK, T // 2], F32, name=f"x_raw{c}", align_bytes=64)
-            nc.sync.dma_start(out=t_[:], in_=x_view[:, :, c * (T // 2) : (c + 1) * (T // 2)])
-            x_raw.append(t_)
+        x_raw = keep.tile([P, PACK, T], F32, name="x_raw", align_bytes=64)
+        nc.sync.dma_start(out=x_raw[:], in_=xT.rearrange("(p j) t -> p j t", j=PACK))
         offs_t = keep.tile([P, E * C // 16], U16, name="offs_t")
         nc.sync.dma_start(offs_t[:], offs)
         w1_raw = []
         for e in range(E):
             n_parts = 2 if e < 2 else 1
+            width = H // n_parts
             parts = []
             for i in range(n_parts):
-                width = H // n_parts
-                t_ = keep.tile([P, PACK, width], F32, name=f"w1_raw{e}_{i}", align_bytes=64)
+                tag = f"w1_raw{e}" if i == n_parts - 1 else f"w1_head{e}"
+                t_ = keep.tile([P, PACK, width], F32, name=tag, align_bytes=64)
                 nc.sync.dma_start(out=t_[:], in_=w1[e].rearrange("(p j) c -> p j c", j=PACK)[:, :, i * width : (i + 1) * width])
                 parts.append(t_)
             w1_raw.append(parts)
@@ -67,16 +64,21 @@ def tile_moe_tk_mlp_relu2_kernel(tc, xT, w1, w2, gate, offs, pos1, pos2, pos3, p
             t_ = keep.tile([P, T // 16], U16, name=f"pos_t{r}")
             nc.sync.dma_start(t_[:], pos[r])
             pos_t.append(t_)
-        gates = keep.tile([P, TOP, T], F32, name="gates", align_bytes=64)
-        nc.sync.dma_start(out=gates[:], in_=gate[:, :P, :].rearrange("r p t -> p r t"))
+        gates = []
+        for r in range(TOP):
+            t_ = keep.tile([P, T], F32, name=f"gate{r}", align_bytes=64)
+            nc.sync.dma_start(out=t_[:], in_=gate[r, :P, :])
+            gates.append(t_)
 
         for c in range(2):
             xg = keep.tile([P, T // 2, PACK], BF16, name=f"xg{c}", align_bytes=64)
-            nc.vector.tensor_copy(
-                out=xg[:].rearrange("p (c i) j -> p c j i", i=2),
-                in_=x_raw[c][:].rearrange("p j (c i) -> p c j i", i=2),
-            )
             cols = slice(c * (T // 2), (c + 1) * (T // 2))
+            dst = xg[:].rearrange("p (c i) j -> p c j i", i=2)
+            src = x_raw[:, :, cols].rearrange("p j (c i) -> p c j i", i=2)
+            if c == 0:
+                nc.vector.tensor_copy(out=dst, in_=src)
+            else:
+                nc.scalar.copy(out=dst, in_=src)
             nc.vector.quantize_mx(out=xw[:, cols].bitcast(FP8X4), scales=xs[:, cols], in_=xg[:].rearrange("p c j -> p (c j)"))
 
         w1_grouped, slot_words, slot_scales, banks, y_banks = {}, {}, {}, {}, {}
@@ -102,12 +104,12 @@ def tile_moe_tk_mlp_relu2_kernel(tc, xT, w1, w2, gate, offs, pos1, pos2, pos3, p
             return offs_t[:, 2 * q * C // 16 : (2 * q + 2) * C // 16]
 
         def gather_words(q):
-            tag = "slot_words0" if q == 0 else ("w1_raw0_1" if q == 1 else f"w1_raw{2 * q - 2}_0")
+            tag = f"slot_words{q}" if q < 1 else f"w1_raw{2 * q - 2}"
             slot_words[q] = keep.tile([P, 2 * C], U32, name=f"slot_words{q}", tag=tag, align_bytes=64)
             nc.vector.tensor_copy(slot_words[q][:], xw[:].bitcast(U32).indirect(pair_list(q)))
 
         def gather_scales(q):
-            tag = "slot_scales0" if q == 0 else ("w1_raw1_1" if q == 1 else f"w1_raw{2 * q - 1}_0")
+            tag = "slot_scales0" if q == 0 else f"w1_raw{2 * q - 1}"
             slot_scales[q] = keep.tile([P, 2 * C], U8, name=f"slot_scales{q}", tag=tag, align_bytes=64)
             nc.vector.tensor_copy(slot_scales[q][:], xs[:].indirect(pair_list(q)))
 
@@ -175,7 +177,7 @@ def tile_moe_tk_mlp_relu2_kernel(tc, xT, w1, w2, gate, offs, pos1, pos2, pos3, p
 
         def fetch(h, r, tag):
             prod = keep.tile([P, T], F32, name=f"prod{h}_{r}", tag=tag, align_bytes=64)
-            nc.vector.tensor_tensor(prod[:], y[h][:].indirect(pos_t[r][:]), gates[:, r, :], MULT)
+            nc.vector.tensor_tensor(prod[:], y[h][:].indirect(pos_t[r][:]), gates[r][:], MULT)
             return prod
 
         def add_turned(acc, prod, first, last):
@@ -213,21 +215,22 @@ def tile_moe_tk_mlp_relu2_kernel(tc, xT, w1, w2, gate, offs, pos1, pos2, pos3, p
             elif e % 2 == 1 and e < E - 1:
                 quantise_h(e - 1, e + 1, f"h_codes{e - 1}")
         quantise_w2(0, 0, E // 2, True, stage, "w1_grouped")
-        quantise_w2(0, E // 2, E, True, keep, "w2_last")
+        quantise_w2(0, E // 2, E - 2, True, keep, "w2_third")
+        quantise_w2(0, E - 2, E, True, keep, "w2_last")
         quantise_h(E - 1, E, "w2_last")
         for q in range(PAIRS):
             second_product(0, q)
         for q in range(PAIRS):
             y_copy(q, 0)
         quantise_w2(1, 0, E // 2, True, keep, "h_bf3")
-        quantise_w2(1, E // 2, E, False, keep, "w2_codes0_4")
+        quantise_w2(1, E // 2, E, False, keep, "w2_codes0_6")
         for q in range(PAIRS):
             second_product(1, q)
         for q in range(PAIRS):
             y_copy(q, 1)
 
         acc = [psum.tile([P, P], F32, name="bank") for c in range(T // P)]
-        for r, tag in enumerate(("prod0_0", "prod0_1", "w2_codes0_4", "prod0_3")):
+        for r, tag in enumerate(("prod0_0", "prod0_1", "w2_codes0_6", "prod0_3")):
             add_turned(acc, fetch(0, r, tag), r == 0, r == TOP - 1)
         back0 = turn_back(acc, "w2_codes1_4")
         res0 = keep.tile([P, T], F32, name="res0")
@@ -240,10 +243,11 @@ def tile_moe_tk_mlp_relu2_kernel(tc, xT, w1, w2, gate, offs, pos1, pos2, pos3, p
         back1 = turn_back(acc, "turned1")
         prod2 = fetch(1, 2, "prod1_2")
         prod3 = fetch(1, 3, "prod1_3")
-        s23 = keep.tile([P, T], F32, name="s23")
+        partial = keep.tile([P, T], F32, name="partial")
         res1 = keep.tile([P, T], F32, name="res1")
-        nc.vector.tensor_tensor(s23[:], prod2[:], prod3[:], ADD)
-        for c in range(2):
-            cols = slice(c * (T // 2), (c + 1) * (T // 2))
-            nc.vector.tensor_tensor(res1[:, cols], back1[:, cols], s23[:, cols], ADD)
+        halves = [slice(c * (T // 2), (c + 1) * (T // 2)) for c in range(2)]
+        for cols in halves:
+            nc.vector.tensor_tensor(partial[:, cols], back1[:, cols], prod2[:, cols], ADD)
+        for cols in halves:
+            nc.vector.tensor_tensor(res1[:, cols], partial[:, cols], prod3[:, cols], ADD)
             nc.sync.dma_start(out[P:, cols], res1[:, cols])

@@ -89,14 +89,14 @@ def tile_moe_tk_mlp_relu2_kernel(tc, xT, w1, w2, gate, offs, pos1, pos2, pos3, p
         def w1_copy(e):
             g = stage.tile([P, PACK * H], BF16, name="w1_grouped", align_bytes=64)
             w1_grouped[e] = g
-            dst = g[:].rearrange("p (t m j) -> p m j t", t=4, j=PACK)
+            dst = g[:].rearrange("p (t m a b) -> p m a t b", t=4, a=2, b=2)
             if e < 2:
                 for i in range(2):
                     nc.scalar.copy(
-                        out=dst[:, i * P // 2 : (i + 1) * P // 2], in_=w1_raw[e][i][:].rearrange("p j (m t) -> p m j t", t=4)
+                        out=dst[:, i * P // 2 : (i + 1) * P // 2], in_=w1_raw[e][i][:].rearrange("p (a b) (m t) -> p m a t b", t=4, b=2)
                     )
                 return
-            src = w1_raw[e][0][:].rearrange("p j (m t) -> p m j t", t=4)
+            src = w1_raw[e][0][:].rearrange("p (a b) (m t) -> p m a t b", t=4, b=2)
             nc.scalar.copy(out=dst[:, :W1_SCALAR], in_=src[:, :W1_SCALAR])
             nc.vector.tensor_copy(out=dst[:, W1_SCALAR:], in_=src[:, W1_SCALAR:])
 

@@ -22,7 +22,7 @@ ADD = mybir.AluOpType.add
 RELU = mybir.ActivationFunctionType.Relu
 SQUARE = mybir.ActivationFunctionType.Square
 
-W1_SCALAR = 40
+W1_SCALAR = 48
 
 
 def tile_moe_tk_mlp_relu2_kernel(tc, xT, w1, w2, gate, offs, pos1, pos2, pos3, pos4, out):
@@ -230,7 +230,7 @@ def tile_moe_tk_mlp_relu2_kernel(tc, xT, w1, w2, gate, offs, pos1, pos2, pos3, p
             y_copy(q, 1)
 
         acc = [psum.tile([P, P], F32, name="bank") for c in range(T // P)]
-        for r, tag in enumerate(("prod0_0", "prod0_1", "w2_codes0_6", "prod0_3")):
+        for r, tag in enumerate(("prod0_0", "prod0_1", "w2_raw", "prod0_3")):
             add_turned(acc, fetch(0, r, tag), r == 0, r == TOP - 1)
         back0 = turn_back(acc, "w2_codes1_4")
         res0 = keep.tile([P, T], F32, name="res0")

@@ -181,15 +181,15 @@ def tile_moe_tk_mlp_relu2_kernel(tc, xT, w1, w2, gate, offs, pos1, pos2, pos3, p
             return prod
 
         def add_turned(acc, prod, first, last):
-            for c in range(T // P):
+            for c in range(len(acc)):
                 nc.tensor.matmul(
                     acc[c][:], lhsT=prod[:, c * P : (c + 1) * P], rhs=ident[:], is_transpose=True, start=first, stop=last
                 )
 
         def turn_back(acc, tag):
-            turned = keep.tile([P, T // P, P], F32, name="turned", tag=tag, align_bytes=64)
-            back = psum.tile([P, T // P, P], F32, name="bank")
-            for c in range(T // P):
+            turned = keep.tile([P, len(acc), P], F32, name="turned", tag=tag, align_bytes=64)
+            back = psum.tile([P, len(acc), P], F32, name="bank")
+            for c in range(len(acc)):
                 nc.scalar.copy(out=turned[:, c, :], in_=acc[c][:])
                 nc.tensor.transpose(back[:, c, :], turned[:, c, :], ident[:])
             return back[:].rearrange("p c t -> p (c t)")
@@ -239,15 +239,22 @@ def tile_moe_tk_mlp_relu2_kernel(tc, xT, w1, w2, gate, offs, pos1, pos2, pos3, p
 
         acc = [psum.tile([P, P], F32, name="bank") for c in range(T // P)]
         for r in range(2):
-            add_turned(acc, fetch(1, r, f"prod1_{r}"), r == 0, r == 1)
-        back1 = turn_back(acc, "turned1")
-        prod2 = fetch(1, 2, "prod1_2")
-        prod3 = fetch(1, 3, "prod1_3")
-        partial = keep.tile([P, T], F32, name="partial")
-        res1 = keep.tile([P, T], F32, name="res1")
+            add_turned(acc, fetch(1, r, f"prod1_{r}"), r == 0, False)
         halves = [slice(c * (T // 2), (c + 1) * (T // 2)) for c in range(2)]
-        for cols in halves:
-            nc.vector.tensor_tensor(partial[:, cols], back1[:, cols], prod2[:, cols], ADD)
-        for cols in halves:
-            nc.vector.tensor_tensor(res1[:, cols], partial[:, cols], prod3[:, cols], ADD)
-            nc.sync.dma_start(out[P:, cols], res1[:, cols])
+
+        def fetch_half(r, c):
+            cols = halves[c]
+            prod = keep.tile([P, T // 2], F32, name=f"prod1_{r}_{c}", align_bytes=64)
+            lst = pos_t[r][:, cols.start // 16 : cols.stop // 16]
+            nc.vector.tensor_tensor(prod[:], y[1][:].indirect(lst), gates[r][:, cols], MULT)
+            return prod
+
+        backs = []
+        for c in range(2):
+            add_turned(acc[2 * c : 2 * c + 2], fetch_half(2, c), False, True)
+            backs.append(turn_back(acc[2 * c : 2 * c + 2], f"turned1_{c}"))
+        lasts = [fetch_half(3, c) for c in range(2)]
+        for c in range(2):
+            res1 = keep.tile([P, T // 2], F32, name=f"res1_{c}")
+            nc.vector.tensor_tensor(res1[:], backs[c], lasts[c][:], ADD)
+            nc.sync.dma_start(out[P:, halves[c]], res1[:])

@@ -22,7 +22,8 @@ ADD = mybir.AluOpType.add
 RELU = mybir.ActivationFunctionType.Relu
 SQUARE = mybir.ActivationFunctionType.Square
 
-W1_SCALAR = 48
+W1_SCALAR = 112
+RAW = PACK * H * 4
 
 
 def tile_moe_tk_mlp_relu2_kernel(tc, xT, w1, w2, gate, offs, pos1, pos2, pos3, pos4, out):
@@ -31,6 +32,7 @@ def tile_moe_tk_mlp_relu2_kernel(tc, xT, w1, w2, gate, offs, pos1, pos2, pos3, p
     with ExitStack() as ctx:
         keep = ctx.enter_context(tc.tile_pool(name="keep", bufs=1))
         stage = ctx.enter_context(tc.tile_pool(name="stage", bufs=2))
+        placed = ctx.enter_context(tc.tile_pool(name="placed", bufs=1))
         psum = ctx.enter_context(tc.psum_pool(name="psum", bufs=8))
 
         xs = keep.tile([P, 2 * T], U8, name="xs", align_bytes=64)
@@ -44,21 +46,29 @@ def tile_moe_tk_mlp_relu2_kernel(tc, xT, w1, w2, gate, offs, pos1, pos2, pos3, p
         offs_t = keep.tile([P, E * C // 16], U16, name="offs_t")
         nc.sync.dma_start(offs_t[:], offs)
         w1_raw = []
+        w2_at = (E + 2) * RAW + 3 * RAW // 2
+        w2_raw = placed.tile([P, E, PACK, N], F32, name="w2_raw", align_bytes=64, offset=w2_at)
+
+        def load_w2(q):
+            nc.sync.dma_start(
+                out=w2_raw[:, 2 * q : 2 * q + 2], in_=w2[2 * q : 2 * q + 2].rearrange("i (p j) n -> p i j n", j=PACK)
+            )
+
         for e in range(E):
             n_parts = 2 if e < 2 else 1
             width = H // n_parts
             parts = []
             for i in range(n_parts):
-                tag = f"w1_raw{e}" if i == n_parts - 1 else f"w1_head{e}"
-                t_ = keep.tile([P, PACK, width], F32, name=tag, align_bytes=64)
+                t_ = placed.tile(
+                    [P, PACK, width], F32, name=f"w1_raw{e}_{i}", align_bytes=64, offset=(e + 1) * RAW - (n_parts - i) * (RAW // n_parts)
+                )
                 nc.sync.dma_start(out=t_[:], in_=w1[e].rearrange("(p j) c -> p j c", j=PACK)[:, :, i * width : (i + 1) * width])
                 parts.append(t_)
             w1_raw.append(parts)
-        w2_raw = keep.tile([P, E, PACK, N], F32, name="w2_raw", align_bytes=64)
-        for q in range(PAIRS):
-            nc.sync.dma_start(
-                out=w2_raw[:, 2 * q : 2 * q + 2], in_=w2[2 * q : 2 * q + 2].rearrange("i (p j) n -> p i j n", j=PACK)
-            )
+            if e == 3:
+                load_w2(0)
+        for q in range(1, PAIRS):
+            load_w2(q)
         pos_t = []
         for r in range(TOP):
             t_ = keep.tile([P, T // 16], U16, name=f"pos_t{r}")
@@ -73,50 +83,69 @@ def tile_moe_tk_mlp_relu2_kernel(tc, xT, w1, w2, gate, offs, pos1, pos2, pos3, p
         for c in range(2):
             xg = keep.tile([P, T // 2, PACK], BF16, name=f"xg{c}", align_bytes=64)
             cols = slice(c * (T // 2), (c + 1) * (T // 2))
-            dst = xg[:].rearrange("p (c i) j -> p c j i", i=2)
-            src = x_raw[:, :, cols].rearrange("p j (c i) -> p c j i", i=2)
+            dst = xg[:].rearrange("p (c i) (a b) -> p c a i b", i=4, b=2)
+            src = x_raw[:, :, cols].rearrange("p (a b) (c i) -> p c a i b", i=4, b=2)
             if c == 0:
                 nc.vector.tensor_copy(out=dst, in_=src)
             else:
                 nc.scalar.copy(out=dst, in_=src)
             nc.vector.quantize_mx(out=xw[:, cols].bitcast(FP8X4), scales=xs[:, cols], in_=xg[:].rearrange("p c j -> p (c j)"))
 
+        w2_grouped = {}
         w1_grouped, slot_words, slot_scales, banks, y_banks = {}, {}, {}, {}, {}
         h_codes, h_scales, w2_codes, w2_scales = {}, {}, {}, {}
         h_bf = [keep.tile([P, 2 * C * PACK], BF16, name=f"h_bf{q}", align_bytes=64) for q in range(PAIRS)]
-        y = [keep.tile([P, E * C], F32, name=f"y{h}") for h in range(2)]
+        y = [
+            placed.tile([P, E * C], F32, name="y0", align_bytes=64, offset=(E + 2) * RAW + RAW // 2),
+            placed.tile([P, E * C], F32, name="y1", align_bytes=64, offset=w2_at),
+        ]
+
+        def grouped_at(e):
+            return (e - 2) * RAW if e >= 2 else (E + 1) * RAW + e * RAW // 2
 
         def w1_copy(e):
-            g = stage.tile([P, PACK * H], BF16, name="w1_grouped", align_bytes=64)
-            w1_grouped[e] = g
-            dst = g[:].rearrange("p (t m a b) -> p m a t b", t=4, a=2, b=2)
             if e < 2:
+                g = placed.tile([P, PACK * H], BF16, name=f"w1_grouped{e}", align_bytes=64, offset=grouped_at(e))
+                w1_grouped[e] = [g]
+                dst = g[:].rearrange("p (t m a b) -> p m a t b", t=4, a=2, b=2)
                 for i in range(2):
                     nc.scalar.copy(
                         out=dst[:, i * P // 2 : (i + 1) * P // 2], in_=w1_raw[e][i][:].rearrange("p (a b) (m t) -> p m a t b", t=4, b=2)
                     )
                 return
-            src = w1_raw[e][0][:].rearrange("p (a b) (m t) -> p m a t b", t=4, b=2)
-            nc.scalar.copy(out=dst[:, :W1_SCALAR], in_=src[:, :W1_SCALAR])
-            nc.vector.tensor_copy(out=dst[:, W1_SCALAR:], in_=src[:, W1_SCALAR:])
+            src = w1_raw[e][0][:].rearrange("p (a b) (m u v) -> p u m a v b", u=2, v=2, b=2)
+            tiles = [
+                placed.tile([P, 2 * H], BF16, name=f"w1_grouped{e}_{u}", align_bytes=64, offset=grouped_at(e) + u * RAW // 4)
+                for u in range(2)
+            ]
+            w1_grouped[e] = tiles
+            dst = [g[:].rearrange("p (v m a b) -> p m a v b", v=2, a=2, b=2) for g in tiles]
+            share = W1_SCALAR if e < 4 else 0
+            if share:
+                nc.scalar.copy(out=dst[1][:, :share], in_=src[:, 1, :share])
+            nc.vector.tensor_copy(out=dst[0], in_=src[:, 0])
+            nc.vector.tensor_copy(out=dst[1][:, share:], in_=src[:, 1, share:])
 
         def pair_list(q):
             return offs_t[:, 2 * q * C // 16 : (2 * q + 2) * C // 16]
 
         def gather_words(q):
-            tag = f"slot_words{q}" if q < 1 else f"w1_raw{2 * q - 2}"
-            slot_words[q] = keep.tile([P, 2 * C], U32, name=f"slot_words{q}", tag=tag, align_bytes=64)
+            end = (2 * q - 1 if q > 0 else E + 1) * RAW
+            slot_words[q] = placed.tile([P, 2 * C], U32, name=f"slot_words{q}", align_bytes=64, offset=end - 8 * C)
             nc.vector.tensor_copy(slot_words[q][:], xw[:].bitcast(U32).indirect(pair_list(q)))
 
         def gather_scales(q):
-            tag = "slot_scales0" if q == 0 else f"w1_raw{2 * q - 1}"
-            slot_scales[q] = keep.tile([P, 2 * C], U8, name=f"slot_scales{q}", tag=tag, align_bytes=64)
+            end = (2 * q if q > 0 else E + 1) * RAW
+            slot_scales[q] = placed.tile([P, 2 * C], U8, name=f"slot_scales{q}", align_bytes=64, offset=end - 10 * C)
             nc.vector.tensor_copy(slot_scales[q][:], xs[:].indirect(pair_list(q)))
 
         def first_product(e):
             wc = stage.tile([P, H], U32, name="w1_codes", align_bytes=64)
             ws = stage.tile([P, H], U8, name="w1_scales", align_bytes=64)
-            nc.vector.quantize_mx(out=wc[:].bitcast(FP8X4), scales=ws[:], in_=w1_grouped[e][:])
+            width = H // len(w1_grouped[e])
+            for u, g in enumerate(w1_grouped[e]):
+                cols = slice(u * width, (u + 1) * width)
+                nc.vector.quantize_mx(out=wc[:, cols].bitcast(FP8X4), scales=ws[:, cols], in_=g[:])
             banks[e] = []
             for b in range(2):
                 ps = psum.tile([P, PACK, P], F32, name="bank")
@@ -131,14 +160,17 @@ def tile_moe_tk_mlp_relu2_kernel(tc, xT, w1, w2, gate, offs, pos1, pos2, pos3, p
                 banks[e].append(ps)
 
         def squared_relu(e):
-            pos_part = stage.tile([P, C, PACK], F32, name="pos_part", align_bytes=64)
+            pos_part = placed.tile([P, C, PACK], F32, name=f"pos_part{e}", align_bytes=64, offset=(E + 2) * RAW + (e % 2) * RAW // 2)
             for b in range(2):
                 nc.scalar.activation(pos_part[:, b * P : (b + 1) * P, :], banks[e][b][:].rearrange("p t n -> p n t"), RELU)
-            mine = slice((e % 2) * C * PACK, (e % 2 + 1) * C * PACK)
-            nc.scalar.activation(h_bf[e // 2][:, mine], pos_part[:].rearrange("p n t -> p (n t)"), SQUARE)
+            for b in range(2):
+                first = ((e % 2) * C + b * P) * PACK
+                nc.scalar.activation(
+                    h_bf[e // 2][:, first : first + P * PACK], pos_part[:, b * P : (b + 1) * P, :].rearrange("p n t -> p (n t)"), SQUARE
+                )
 
-        def quantise_h(e0, e1, tag):
-            hc = keep.tile([P, (e1 - e0) * C], U32, name=f"h_codes{e0}", tag=tag, align_bytes=64)
+        def quantise_h(e0, e1, pool, **place):
+            hc = pool.tile([P, (e1 - e0) * C], U32, name=f"h_codes{e0}", align_bytes=64, **place)
             hs = keep.tile([P, (e1 - e0) * C], U8, name=f"h_scales{e0}", align_bytes=64)
             first = (e0 % 2) * C * PACK
             nc.vector.quantize_mx(
@@ -147,18 +179,24 @@ def tile_moe_tk_mlp_relu2_kernel(tc, xT, w1, w2, gate, offs, pos1, pos2, pos3, p
             for e in range(e0, e1):
                 h_codes[e], h_scales[e] = hc[:, (e - e0) * C : (e - e0 + 1) * C], hs[:, (e - e0) * C : (e - e0 + 1) * C]
 
-        def quantise_w2(h, e0, e1, on_vector, layout_pool, layout_tag):
+        def w2_copy(h, e0, e1, on_vector, pool, **place):
+            g = pool.tile([P, e1 - e0, P, PACK], BF16, name=f"w2_grouped{h}_{e0}", align_bytes=64, **place)
+            w2_grouped[h, e0] = g
+            for e in range(e0, e1):
+                dst = g[:, e - e0].rearrange("p (c i) (a b) -> p c a i b", i=4, b=2)
+                src = w2_raw[:, e, :, h * P : (h + 1) * P].rearrange("p (a b) (c i) -> p c a i b", i=4, b=2)
+                if on_vector:
+                    nc.vector.tensor_copy(out=dst, in_=src)
+                else:
+                    nc.scalar.copy(out=dst, in_=src)
+
+        def quantise_w2(h, e0, e1, pool=keep, **place):
             n_e = e1 - e0
-            g = layout_pool.tile([P, n_e, P, PACK], BF16, name="w2_grouped", tag=layout_tag, align_bytes=64)
-            dst = g[:].rearrange("p e (c i) j -> p e c j i", i=2)
-            src = w2_raw[:, e0:e1, :, h * P : (h + 1) * P].rearrange("p e j (c i) -> p e c j i", i=2)
-            if on_vector:
-                nc.vector.tensor_copy(out=dst, in_=src)
-            else:
-                nc.scalar.copy(out=dst, in_=src)
-            wc = keep.tile([P, n_e * P], U32, name=f"w2_codes{h}_{e0}", align_bytes=64)
+            wc = pool.tile([P, n_e * P], U32, name=f"w2_codes{h}_{e0}", align_bytes=64, **place)
             ws = keep.tile([P, n_e * P], U8, name=f"w2_scales{h}_{e0}", align_bytes=64)
-            nc.vector.quantize_mx(out=wc[:].bitcast(FP8X4), scales=ws[:], in_=g[:].rearrange("p i c j -> p (i c j)"))
+            nc.vector.quantize_mx(
+                out=wc[:].bitcast(FP8X4), scales=ws[:], in_=w2_grouped[h, e0][:].rearrange("p i c j -> p (i c j)")
+            )
             for e in range(e0, e1):
                 w2_codes[h, e], w2_scales[h, e] = wc[:, (e - e0) * P : (e - e0 + 1) * P], ws[:, (e - e0) * P : (e - e0 + 1) * P]
 
@@ -175,8 +213,8 @@ def tile_moe_tk_mlp_relu2_kernel(tc, xT, w1, w2, gate, offs, pos1, pos2, pos3, p
         def y_copy(q, h):
             nc.scalar.copy(out=y[h][:, 2 * q * C : (2 * q + 2) * C], in_=y_banks[q, h][:].rearrange("p i c -> p (i c)"))
 
-        def fetch(h, r, tag):
-            prod = keep.tile([P, T], F32, name=f"prod{h}_{r}", tag=tag, align_bytes=64)
+        def fetch(h, r, pool=keep, **place):
+            prod = pool.tile([P, T], F32, name=f"prod{h}_{r}", align_bytes=64, **place)
             nc.vector.tensor_tensor(prod[:], y[h][:].indirect(pos_t[r][:]), gates[r][:], MULT)
             return prod
 
@@ -210,28 +248,44 @@ def tile_moe_tk_mlp_relu2_kernel(tc, xT, w1, w2, gate, offs, pos1, pos2, pos3, p
                 gather_words(e // 2 + 2)
             if e + 2 < E:
                 w1_copy(e + 2)
-            if e == E - 2:
-                quantise_h(e, e + 1, "h_codes6")
-            elif e % 2 == 1 and e < E - 1:
-                quantise_h(e - 1, e + 1, f"h_codes{e - 1}")
-        quantise_w2(0, 0, E // 2, True, stage, "w1_grouped")
-        quantise_w2(0, E // 2, E - 2, True, keep, "w2_third")
-        quantise_w2(0, E - 2, E, True, keep, "w2_last")
-        quantise_h(E - 1, E, "w2_last")
+            if e in (2, 3):
+                w2_copy(e - 2, 0, 2, False, keep)
+        KB = 1024
+        at6, at7 = 6 * RAW, 7 * RAW
+        quantise_h(0, 2, placed, offset=grouped_at(7))
+        w2_copy(0, 2, 4, True, placed, offset=at6 + 6 * KB)
+        quantise_h(2, 4, placed, offset=grouped_at(7) + RAW // 4)
+        quantise_w2(0, 0, 2, placed, offset=grouped_at(6))
+        quantise_w2(0, 2, 4)
+        w2_copy(0, 4, 5, True, placed, offset=at6 + 2 * KB)
+        w2_copy(0, 5, 6, True, placed, offset=at6 + 4 * KB)
+        quantise_w2(0, 4, 5)
+        quantise_w2(0, 5, 6)
+        quantise_h(4, 6, placed, offset=at6 + KB // 2)
+        quantise_h(6, 7, placed, offset=at6 + 3 * KB + KB // 2)
+        w2_copy(0, 6, 7, True, placed, offset=at7)
+        w2_copy(0, 7, 8, True, placed, offset=at7 + 3 * KB)
+        quantise_w2(0, 6, 7)
+        quantise_w2(0, 7, 8)
+        quantise_h(7, 8, placed, offset=at7)
+        w2_copy(1, 2, 4, True, placed, offset=at7 + 3 * KB)
         for q in range(PAIRS):
             second_product(0, q)
         for q in range(PAIRS):
             y_copy(q, 0)
-        quantise_w2(1, 0, E // 2, True, keep, "h_bf3")
-        quantise_w2(1, E // 2, E, False, keep, "w2_codes0_6")
+        quantise_w2(1, 2, 4)
+        quantise_w2(1, 0, 2, placed, offset=at7 + 3 * KB)
+        w2_copy(1, 4, 8, False, keep, tag="w2_codes0_7")
+        quantise_w2(1, 4, 8)
         for q in range(PAIRS):
             second_product(1, q)
         for q in range(PAIRS):
             y_copy(q, 1)
 
         acc = [psum.tile([P, P], F32, name="bank") for c in range(T // P)]
-        for r, tag in enumerate(("prod0_0", "prod0_1", "w2_raw", "prod0_3")):
-            add_turned(acc, fetch(0, r, tag), r == 0, r == TOP - 1)
+        for r in range(TOP):
+            prod = fetch(0, r, placed, offset=w2_at + RAW + (r - 2) * 4 * T) if r >= 2 else fetch(0, r)
+            add_turned(acc, prod, r == 0, r == TOP - 1)
         back0 = turn_back(acc, "w2_codes1_4")
         res0 = keep.tile([P, T], F32, name="res0")
         nc.scalar.copy(out=res0[:], in_=back0)
@@ -239,7 +293,7 @@ def tile_moe_tk_mlp_relu2_kernel(tc, xT, w1, w2, gate, offs, pos1, pos2, pos3, p
 
         acc = [psum.tile([P, P], F32, name="bank") for c in range(T // P)]
         for r in range(2):
-            add_turned(acc, fetch(1, r, f"prod1_{r}"), r == 0, False)
+            add_turned(acc, fetch(1, r), r == 0, False)
         halves = [slice(c * (T // 2), (c + 1) * (T // 2)) for c in range(2)]
 
         def fetch_half(r, c):

@@ -23,6 +23,7 @@ RELU = mybir.ActivationFunctionType.Relu
 SQUARE = mybir.ActivationFunctionType.Square
 
 W1_SCALAR = 112
+X_SCALAR = 192
 RAW = PACK * H * 4
 
 
@@ -41,13 +42,22 @@ def tile_moe_tk_mlp_relu2_kernel(tc, xT, w1, w2, gate, offs, pos1, pos2, pos3, p
         nc.vector.memset(xw[:, T:], 0)
         ident = keep.tile([P, P], F32, name="ident")
         make_identity(nc, ident[:])
-        x_raw = keep.tile([P, PACK, T], F32, name="x_raw", align_bytes=64)
+        x_raw = keep.tile([P, PACK, T], F32, name="x_raw", align_bytes=256)
         nc.sync.dma_start(out=x_raw[:], in_=xT.rearrange("(p j) t -> p j t", j=PACK))
         offs_t = keep.tile([P, E * C // 16], U16, name="offs_t")
         nc.sync.dma_start(offs_t[:], offs)
         w1_raw = []
         w2_at = (E + 2) * RAW + 3 * RAW // 2
-        w2_raw = placed.tile([P, E, PACK, N], F32, name="w2_raw", align_bytes=64, offset=w2_at)
+        w2_raw = placed.tile([P, E // 2, PACK, N], F32, name="w2_raw", align_bytes=64, offset=w2_at)
+        w2_late = [
+            placed.tile([P, E // 2, PACK, P], F32, name=f"w2_late{h}", align_bytes=64, offset=w2_at + (2 + h) * RAW) for h in range(2)
+        ]
+
+        def load_w2_half(h):
+            for e in range(E // 2, E):
+                nc.sync.dma_start(
+                    out=w2_late[h][:, e - E // 2], in_=w2[e].rearrange("(p j) n -> p j n", j=PACK)[:, :, h * P : (h + 1) * P]
+                )
 
         def load_w2(q):
             nc.sync.dma_start(
@@ -60,15 +70,15 @@ def tile_moe_tk_mlp_relu2_kernel(tc, xT, w1, w2, gate, offs, pos1, pos2, pos3, p
             parts = []
             for i in range(n_parts):
                 t_ = placed.tile(
-                    [P, PACK, width], F32, name=f"w1_raw{e}_{i}", align_bytes=64, offset=(e + 1) * RAW - (n_parts - i) * (RAW // n_parts)
+                    [P, PACK, width], F32, name=f"w1_raw{e}_{i}", align_bytes=256, offset=(e + 1) * RAW - (n_parts - i) * (RAW // n_parts)
                 )
                 nc.sync.dma_start(out=t_[:], in_=w1[e].rearrange("(p j) c -> p j c", j=PACK)[:, :, i * width : (i + 1) * width])
                 parts.append(t_)
             w1_raw.append(parts)
             if e == 3:
                 load_w2(0)
-        for q in range(1, PAIRS):
-            load_w2(q)
+        load_w2(1)
+        load_w2_half(0)
         pos_t = []
         for r in range(TOP):
             t_ = keep.tile([P, T // 16], U16, name=f"pos_t{r}")
@@ -76,20 +86,28 @@ def tile_moe_tk_mlp_relu2_kernel(tc, xT, w1, w2, gate, offs, pos1, pos2, pos3, p
             pos_t.append(t_)
         gates = []
         for r in range(TOP):
-            t_ = keep.tile([P, T], F32, name=f"gate{r}", align_bytes=64)
+            t_ = keep.tile([P, T], F32, name=f"gate{r}", align_bytes=256)
             nc.sync.dma_start(out=t_[:], in_=gate[r, :P, :])
             gates.append(t_)
+            if r == 0:
+                load_w2_half(1)
 
-        for c in range(2):
-            xg = keep.tile([P, T // 2, PACK], BF16, name=f"xg{c}", align_bytes=64)
-            cols = slice(c * (T // 2), (c + 1) * (T // 2))
-            dst = xg[:].rearrange("p (c i) (a b) -> p c a i b", i=4, b=2)
-            src = x_raw[:, :, cols].rearrange("p (a b) (c i) -> p c a i b", i=4, b=2)
-            if c == 0:
-                nc.vector.tensor_copy(out=dst, in_=src)
-            else:
-                nc.scalar.copy(out=dst, in_=src)
-            nc.vector.quantize_mx(out=xw[:, cols].bitcast(FP8X4), scales=xs[:, cols], in_=xg[:].rearrange("p c j -> p (c j)"))
+        x_parts = ((0, P), (P, 2 * P), (2 * P, T))
+        xg = [keep.tile([P, t1 - t0, PACK], BF16, name=f"xg{t0}", align_bytes=64) for t0, t1 in x_parts]
+
+        def x_copy(copy, i, t0, t1):
+            first = x_parts[i][0]
+            copy(
+                out=xg[i][:, t0 - first : t1 - first].rearrange("p (c i) (a b) -> p c a i b", i=4, b=2),
+                in_=x_raw[:, :, t0:t1].rearrange("p (a b) (c i) -> p c a i b", i=4, b=2),
+            )
+
+        x_copy(nc.scalar.copy, 2, T - X_SCALAR, T)
+        x_copy(nc.vector.tensor_copy, 0, 0, P)
+        x_copy(nc.vector.tensor_copy, 1, P, 2 * P)
+        x_copy(nc.vector.tensor_copy, 2, 2 * P, T - X_SCALAR)
+        for i, (t0, t1) in enumerate(x_parts):
+            nc.vector.quantize_mx(out=xw[:, t0:t1].bitcast(FP8X4), scales=xs[:, t0:t1], in_=xg[i][:].rearrange("p c j -> p (c j)"))
 
         w2_grouped = {}
         w1_grouped, slot_words, slot_scales, banks, y_banks = {}, {}, {}, {}, {}
@@ -97,7 +115,7 @@ def tile_moe_tk_mlp_relu2_kernel(tc, xT, w1, w2, gate, offs, pos1, pos2, pos3, p
         h_bf = [keep.tile([P, 2 * C * PACK], BF16, name=f"h_bf{q}", align_bytes=64) for q in range(PAIRS)]
         y = [
             placed.tile([P, E * C], F32, name="y0", align_bytes=64, offset=(E + 2) * RAW + RAW // 2),
-            placed.tile([P, E * C], F32, name="y1", align_bytes=64, offset=w2_at),
+            placed.tile([P, E * C], F32, name="y1", align_bytes=64, offset=w2_at + 5 * RAW // 2),
         ]
 
         def grouped_at(e):
@@ -184,7 +202,8 @@ def tile_moe_tk_mlp_relu2_kernel(tc, xT, w1, w2, gate, offs, pos1, pos2, pos3, p
             w2_grouped[h, e0] = g
             for e in range(e0, e1):
                 dst = g[:, e - e0].rearrange("p (c i) (a b) -> p c a i b", i=4, b=2)
-                src = w2_raw[:, e, :, h * P : (h + 1) * P].rearrange("p (a b) (c i) -> p c a i b", i=4, b=2)
+                rows = w2_raw[:, e, :, h * P : (h + 1) * P] if e < E // 2 else w2_late[h][:, e - E // 2]
+                src = rows.rearrange("p (a b) (c i) -> p c a i b", i=4, b=2)
                 if on_vector:
                     nc.vector.tensor_copy(out=dst, in_=src)
                 else:
@@ -284,7 +303,7 @@ def tile_moe_tk_mlp_relu2_kernel(tc, xT, w1, w2, gate, offs, pos1, pos2, pos3, p
 
         acc = [psum.tile([P, P], F32, name="bank") for c in range(T // P)]
         for r in range(TOP):
-            prod = fetch(0, r, placed, offset=w2_at + RAW + (r - 2) * 4 * T) if r >= 2 else fetch(0, r)
+            prod = fetch(0, r, placed, offset=w2_at + 7 * RAW // 2 + (r - 2) * 4 * T) if r >= 2 else fetch(0, r)
             add_turned(acc, prod, r == 0, r == TOP - 1)
         back0 = turn_back(acc, "w2_codes1_4")
         res0 = keep.tile([P, T], F32, name="res0")

@@ -53,8 +53,8 @@ def tile_moe_tk_mlp_relu2_kernel(tc, xT, w1, w2, gate, offs, pos1, pos2, pos3, p
             placed.tile([P, E // 2, PACK, P], F32, name=f"w2_late{h}", align_bytes=64, offset=w2_at + (2 + h) * RAW) for h in range(2)
         ]
 
-        def load_w2_half(h):
-            for e in range(E // 2, E):
+        def load_w2_half(h, e0, e1):
+            for e in range(e0, e1):
                 nc.sync.dma_start(
                     out=w2_late[h][:, e - E // 2], in_=w2[e].rearrange("(p j) n -> p j n", j=PACK)[:, :, h * P : (h + 1) * P]
                 )
@@ -78,7 +78,7 @@ def tile_moe_tk_mlp_relu2_kernel(tc, xT, w1, w2, gate, offs, pos1, pos2, pos3, p
             if e == 3:
                 load_w2(0)
         load_w2(1)
-        load_w2_half(0)
+        load_w2_half(0, E // 2, E)
         pos_t = []
         for r in range(TOP):
             t_ = keep.tile([P, T // 16], U16, name=f"pos_t{r}")
@@ -89,8 +89,8 @@ def tile_moe_tk_mlp_relu2_kernel(tc, xT, w1, w2, gate, offs, pos1, pos2, pos3, p
             t_ = keep.tile([P, T], F32, name=f"gate{r}", align_bytes=256)
             nc.sync.dma_start(out=t_[:], in_=gate[r, :P, :])
             gates.append(t_)
-            if r == 0:
-                load_w2_half(1)
+            if r < 2:
+                load_w2_half(1, E // 2 + 2 * r, E // 2 + 2 * r + 2)
 
         x_parts = ((0, P), (P, 2 * P), (2 * P, T))
         xg = [keep.tile([P, t1 - t0, PACK], BF16, name=f"xg{t0}", align_bytes=64) for t0, t1 in x_parts]
@@ -219,18 +219,17 @@ def tile_moe_tk_mlp_relu2_kernel(tc, xT, w1, w2, gate, offs, pos1, pos2, pos3, p
             for e in range(e0, e1):
                 w2_codes[h, e], w2_scales[h, e] = wc[:, (e - e0) * P : (e - e0 + 1) * P], ws[:, (e - e0) * P : (e - e0 + 1) * P]
 
-        def second_product(h, q):
-            ps = psum.tile([P, 2, C], F32, name="bank")
-            for i in range(2):
-                e = 2 * q + i
+        def second_product(h, e0, e1):
+            ps = psum.tile([P, e1 - e0, C], F32, name="bank")
+            for e in range(e0, e1):
                 nc.tensor.matmul_mx(
-                    out=ps[:, i, :], lhsT=w2_codes[h, e].bitcast(FP8X4), lhsT_scale=w2_scales[h, e],
+                    out=ps[:, e - e0, :], lhsT=w2_codes[h, e].bitcast(FP8X4), lhsT_scale=w2_scales[h, e],
                     rhs=h_codes[e].bitcast(FP8X4), rhs_scale=h_scales[e], start=True, stop=True,
                 )
-            y_banks[q, h] = ps
+            y_banks[h, e0] = ps
 
-        def y_copy(q, h):
-            nc.scalar.copy(out=y[h][:, 2 * q * C : (2 * q + 2) * C], in_=y_banks[q, h][:].rearrange("p i c -> p (i c)"))
+        def y_copy(h, e0, e1):
+            nc.scalar.copy(out=y[h][:, e0 * C : e1 * C], in_=y_banks[h, e0][:].rearrange("p i c -> p (i c)"))
 
         def fetch(h, r, pool=keep, **place):
             prod = pool.tile([P, T], F32, name=f"prod{h}_{r}", align_bytes=64, **place)
@@ -288,18 +287,19 @@ def tile_moe_tk_mlp_relu2_kernel(tc, xT, w1, w2, gate, offs, pos1, pos2, pos3, p
         quantise_w2(0, 7, 8)
         quantise_h(7, 8, placed, offset=at7)
         w2_copy(1, 2, 4, True, placed, offset=at7 + 3 * KB)
-        for q in range(PAIRS):
-            second_product(0, q)
-        for q in range(PAIRS):
-            y_copy(q, 0)
+        groups = ((0, 2), (2, 4), (4, 6), (6, 7), (7, 8))
+        for e0, e1 in groups:
+            second_product(0, e0, e1)
+        for e0, e1 in groups:
+            y_copy(0, e0, e1)
         quantise_w2(1, 2, 4)
         quantise_w2(1, 0, 2, placed, offset=at7 + 3 * KB)
         w2_copy(1, 4, 8, False, keep, tag="w2_codes0_7")
         quantise_w2(1, 4, 8)
-        for q in range(PAIRS):
-            second_product(1, q)
-        for q in range(PAIRS):
-            y_copy(q, 1)
+        for e0 in range(0, E, 2):
+            second_product(1, e0, e0 + 2)
+        for e0 in range(0, E, 2):
+            y_copy(1, e0, e0 + 2)
 
         acc = [psum.tile([P, P], F32, name="bank") for c in range(T // P)]
         for r in range(TOP):
@@ -315,19 +315,26 @@ def tile_moe_tk_mlp_relu2_kernel(tc, xT, w1, w2, gate, offs, pos1, pos2, pos3, p
             add_turned(acc, fetch(1, r), r == 0, False)
         halves = [slice(c * (T // 2), (c + 1) * (T // 2)) for c in range(2)]
 
-        def fetch_half(r, c):
-            cols = halves[c]
-            prod = keep.tile([P, T // 2], F32, name=f"prod1_{r}_{c}", align_bytes=64)
+        def fetch_part(r, cols):
+            prod = keep.tile([P, cols.stop - cols.start], F32, name=f"prod1_{r}_{cols.start}", align_bytes=64)
             lst = pos_t[r][:, cols.start // 16 : cols.stop // 16]
             nc.vector.tensor_tensor(prod[:], y[1][:].indirect(lst), gates[r][:, cols], MULT)
             return prod
 
         backs = []
         for c in range(2):
-            add_turned(acc[2 * c : 2 * c + 2], fetch_half(2, c), False, True)
+            add_turned(acc[2 * c : 2 * c + 2], fetch_part(2, halves[c]), False, True)
             backs.append(turn_back(acc[2 * c : 2 * c + 2], f"turned1_{c}"))
-        lasts = [fetch_half(3, c) for c in range(2)]
-        for c in range(2):
-            res1 = keep.tile([P, T // 2], F32, name=f"res1_{c}")
-            nc.vector.tensor_tensor(res1[:], backs[c], lasts[c][:], ADD)
-            nc.sync.dma_start(out[P:, halves[c]], res1[:])
+        parts = (slice(0, 2 * P), slice(2 * P, 3 * P), slice(3 * P, T))
+        sums = (backs[0], backs[1][:, :P], backs[1][:, P:])
+
+        def finish(i, last):
+            res1 = keep.tile([P, parts[i].stop - parts[i].start], F32, name=f"res1_{i}")
+            nc.vector.tensor_tensor(res1[:], sums[i], last[:], ADD)
+            nc.sync.dma_start(out[P:, parts[i]], res1[:])
+
+        lasts = [fetch_part(3, parts[i]) for i in range(2)]
+        finish(0, lasts[0])
+        lasts.append(fetch_part(3, parts[2]))
+        finish(1, lasts[1])
+        finish(2, lasts[2])

@@ -22,7 +22,6 @@ ADD = mybir.AluOpType.add
 RELU = mybir.ActivationFunctionType.Relu
 SQUARE = mybir.ActivationFunctionType.Square
 
-W1_SCALAR = 112
 X_SCALAR = 192
 RAW = PACK * H * 4
 
@@ -49,14 +48,18 @@ def tile_moe_tk_mlp_relu2_kernel(tc, xT, w1, w2, gate, offs, pos1, pos2, pos3, p
         w1_raw = []
         w2_at = (E + 2) * RAW + 3 * RAW // 2
         w2_raw = placed.tile([P, E // 2, PACK, N], F32, name="w2_raw", align_bytes=64, offset=w2_at)
-        w2_late = [
-            placed.tile([P, E // 2, PACK, P], F32, name=f"w2_late{h}", align_bytes=64, offset=w2_at + (2 + h) * RAW) for h in range(2)
-        ]
+        w2_late = {
+            (h, q): placed.tile(
+                [P, 2, PACK, P], F32, name=f"w2_late{h}_{q}", align_bytes=64, offset=w2_at + (2 + h) * RAW + (q - 2) * RAW // 2
+            )
+            for h in range(2)
+            for q in (2, 3)
+        }
 
         def load_w2_half(h, e0, e1):
             for e in range(e0, e1):
                 nc.sync.dma_start(
-                    out=w2_late[h][:, e - E // 2], in_=w2[e].rearrange("(p j) n -> p j n", j=PACK)[:, :, h * P : (h + 1) * P]
+                    out=w2_late[h, e // 2][:, e % 2], in_=w2[e].rearrange("(p j) n -> p j n", j=PACK)[:, :, h * P : (h + 1) * P]
                 )
 
         def load_w2(q):
@@ -65,16 +68,9 @@ def tile_moe_tk_mlp_relu2_kernel(tc, xT, w1, w2, gate, offs, pos1, pos2, pos3, p
             )
 
         for e in range(E):
-            n_parts = 2 if e < 2 else 1
-            width = H // n_parts
-            parts = []
-            for i in range(n_parts):
-                t_ = placed.tile(
-                    [P, PACK, width], F32, name=f"w1_raw{e}_{i}", align_bytes=256, offset=(e + 1) * RAW - (n_parts - i) * (RAW // n_parts)
-                )
-                nc.sync.dma_start(out=t_[:], in_=w1[e].rearrange("(p j) c -> p j c", j=PACK)[:, :, i * width : (i + 1) * width])
-                parts.append(t_)
-            w1_raw.append(parts)
+            t_ = placed.tile([P, PACK, H], F32, name=f"w1_raw{e}", align_bytes=256, offset=e * RAW)
+            nc.sync.dma_start(out=t_[:], in_=w1[e].rearrange("(p j) c -> p j c", j=PACK))
+            w1_raw.append(t_)
             if e == 3:
                 load_w2(0)
         load_w2(1)
@@ -89,8 +85,8 @@ def tile_moe_tk_mlp_relu2_kernel(tc, xT, w1, w2, gate, offs, pos1, pos2, pos3, p
             t_ = keep.tile([P, T], F32, name=f"gate{r}", align_bytes=256)
             nc.sync.dma_start(out=t_[:], in_=gate[r, :P, :])
             gates.append(t_)
-            if r < 2:
-                load_w2_half(1, E // 2 + 2 * r, E // 2 + 2 * r + 2)
+            if r == 1:
+                load_w2_half(1, E // 2, E)
 
         x_parts = ((0, P), (P, 2 * P), (2 * P, T))
         xg = [keep.tile([P, t1 - t0, PACK], BF16, name=f"xg{t0}", align_bytes=64) for t0, t1 in x_parts]
@@ -115,7 +111,7 @@ def tile_moe_tk_mlp_relu2_kernel(tc, xT, w1, w2, gate, offs, pos1, pos2, pos3, p
         h_bf = [keep.tile([P, 2 * C * PACK], BF16, name=f"h_bf{q}", align_bytes=64) for q in range(PAIRS)]
         y = [
             placed.tile([P, E * C], F32, name="y0", align_bytes=64, offset=(E + 2) * RAW + RAW // 2),
-            placed.tile([P, E * C], F32, name="y1", align_bytes=64, offset=w2_at + 5 * RAW // 2),
+            placed.tile([P, E * C], F32, name="y1", align_bytes=64, offset=w2_at + 31 * RAW // 8),
         ]
 
         def grouped_at(e):
@@ -126,34 +122,28 @@ def tile_moe_tk_mlp_relu2_kernel(tc, xT, w1, w2, gate, offs, pos1, pos2, pos3, p
                 g = placed.tile([P, PACK * H], BF16, name=f"w1_grouped{e}", align_bytes=64, offset=grouped_at(e))
                 w1_grouped[e] = [g]
                 dst = g[:].rearrange("p (t m a b) -> p m a t b", t=4, a=2, b=2)
-                for i in range(2):
-                    nc.scalar.copy(
-                        out=dst[:, i * P // 2 : (i + 1) * P // 2], in_=w1_raw[e][i][:].rearrange("p (a b) (m t) -> p m a t b", t=4, b=2)
-                    )
+                nc.scalar.copy(out=dst, in_=w1_raw[e][:].rearrange("p (a b) (m t) -> p m a t b", t=4, b=2))
                 return
-            src = w1_raw[e][0][:].rearrange("p (a b) (m u v) -> p u m a v b", u=2, v=2, b=2)
+            src = w1_raw[e][:].rearrange("p (a b) (m u v) -> p u m a v b", u=2, v=2, b=2)
             tiles = [
                 placed.tile([P, 2 * H], BF16, name=f"w1_grouped{e}_{u}", align_bytes=64, offset=grouped_at(e) + u * RAW // 4)
                 for u in range(2)
             ]
             w1_grouped[e] = tiles
             dst = [g[:].rearrange("p (v m a b) -> p m a v b", v=2, a=2, b=2) for g in tiles]
-            share = W1_SCALAR if e < 4 else 0
-            if share:
-                nc.scalar.copy(out=dst[1][:, :share], in_=src[:, 1, :share])
-            nc.vector.tensor_copy(out=dst[0], in_=src[:, 0])
-            nc.vector.tensor_copy(out=dst[1][:, share:], in_=src[:, 1, share:])
+            for u in range(2):
+                nc.vector.tensor_copy(out=dst[u], in_=src[:, u])
 
         def pair_list(q):
             return offs_t[:, 2 * q * C // 16 : (2 * q + 2) * C // 16]
 
         def gather_words(q):
-            end = (2 * q - 1 if q > 0 else E + 1) * RAW
+            end = (2 * q - 1) * RAW if q > 1 else (E + 1) * RAW - q * RAW // 2
             slot_words[q] = placed.tile([P, 2 * C], U32, name=f"slot_words{q}", align_bytes=64, offset=end - 8 * C)
             nc.vector.tensor_copy(slot_words[q][:], xw[:].bitcast(U32).indirect(pair_list(q)))
 
         def gather_scales(q):
-            end = (2 * q if q > 0 else E + 1) * RAW
+            end = (E + 1, 1, 4, 6)[q] * RAW
             slot_scales[q] = placed.tile([P, 2 * C], U8, name=f"slot_scales{q}", align_bytes=64, offset=end - 10 * C)
             nc.vector.tensor_copy(slot_scales[q][:], xs[:].indirect(pair_list(q)))
 
@@ -202,7 +192,7 @@ def tile_moe_tk_mlp_relu2_kernel(tc, xT, w1, w2, gate, offs, pos1, pos2, pos3, p
             w2_grouped[h, e0] = g
             for e in range(e0, e1):
                 dst = g[:, e - e0].rearrange("p (c i) (a b) -> p c a i b", i=4, b=2)
-                rows = w2_raw[:, e, :, h * P : (h + 1) * P] if e < E // 2 else w2_late[h][:, e - E // 2]
+                rows = w2_raw[:, e, :, h * P : (h + 1) * P] if e < E // 2 else w2_late[h, e // 2][:, e % 2]
                 src = rows.rearrange("p (a b) (c i) -> p c a i b", i=4, b=2)
                 if on_vector:
                     nc.vector.tensor_copy(out=dst, in_=src)
@@ -252,15 +242,16 @@ def tile_moe_tk_mlp_relu2_kernel(tc, xT, w1, w2, gate, offs, pos1, pos2, pos3, p
 
         gather_words(0)
         gather_scales(0)
+        gather_words(1)
         w1_copy(0)
         first_product(0)
+        gather_scales(1)
         w1_copy(1)
-        gather_words(1)
         for e in range(E):
             squared_relu(e)
             if e + 1 < E:
                 first_product(e + 1)
-            if e % 2 == 0 and e + 2 < E:
+            if e in (2, 4):
                 gather_scales(e // 2 + 1)
             if e % 2 == 1 and e + 3 < E:
                 gather_words(e // 2 + 2)
@@ -294,8 +285,10 @@ def tile_moe_tk_mlp_relu2_kernel(tc, xT, w1, w2, gate, offs, pos1, pos2, pos3, p
             y_copy(0, e0, e1)
         quantise_w2(1, 2, 4)
         quantise_w2(1, 0, 2, placed, offset=at7 + 3 * KB)
-        w2_copy(1, 4, 8, False, keep, tag="w2_codes0_7")
-        quantise_w2(1, 4, 8)
+        w2_copy(1, 4, 6, False, keep, tag="w2_codes0_7")
+        quantise_w2(1, 4, 6)
+        w2_copy(1, 6, 8, False, keep, tag="w2_codes0_6")
+        quantise_w2(1, 6, 8)
         for e0 in range(0, E, 2):
             second_product(1, e0, e0 + 2)
         for e0 in range(0, E, 2):
@@ -303,9 +296,9 @@ def tile_moe_tk_mlp_relu2_kernel(tc, xT, w1, w2, gate, offs, pos1, pos2, pos3, p
 
         acc = [psum.tile([P, P], F32, name="bank") for c in range(T // P)]
         for r in range(TOP):
-            prod = fetch(0, r, placed, offset=w2_at + 7 * RAW // 2 + (r - 2) * 4 * T) if r >= 2 else fetch(0, r)
+            prod = fetch(0, r, placed, offset=w2_at + (24, 27, 29)[r - 1] * RAW // 8) if r >= 1 else fetch(0, r)
             add_turned(acc, prod, r == 0, r == TOP - 1)
-        back0 = turn_back(acc, "w2_codes1_4")
+        back0 = turn_back(acc, "w2_codes1_6")
         res0 = keep.tile([P, T], F32, name="res0")
         nc.scalar.copy(out=res0[:], in_=back0)
         nc.sync.dma_start(out[:P, :], res0[:])

@@ -7,7 +7,6 @@ K, T, E, C, H, N = 512, 512, 8, 256, 512, 256
 TOP = 4
 P = 128
 PACK = 4
-PAIRS = E // 2
 FLOPS = 2 * E * C * (K * H + H * N)
 
 F32 = mybir.dt.float32
@@ -23,7 +22,19 @@ RELU = mybir.ActivationFunctionType.Relu
 SQUARE = mybir.ActivationFunctionType.Square
 
 X_SCALAR = 192
+W1_ON_SCALAR = 2
+W2_WHOLE = 4
+
+KB = 1024
 RAW = PACK * H * 4
+FIRST_SLOTS_END = (E + 1) * RAW
+FIRST_GROUPED_AT = (E + 1) * RAW
+RELU_AT = (E + 2) * RAW
+Y0_AT = RELU_AT + 4 * KB
+W2_AT = Y0_AT + 8 * KB
+W2_LATE_AT = W2_AT + 16 * KB
+PAIR2_SECOND_AT = W2_LATE_AT + 8 * KB
+PAIR3_SECOND_AT = PAIR2_SECOND_AT + 4 * KB
 
 
 def tile_moe_tk_mlp_relu2_kernel(tc, xT, w1, w2, gate, offs, pos1, pos2, pos3, pos4, out):
@@ -41,110 +52,105 @@ def tile_moe_tk_mlp_relu2_kernel(tc, xT, w1, w2, gate, offs, pos1, pos2, pos3, p
         nc.vector.memset(xw[:, T:], 0)
         ident = keep.tile([P, P], F32, name="ident")
         make_identity(nc, ident[:])
+
         x_raw = keep.tile([P, PACK, T], F32, name="x_raw", align_bytes=256)
         nc.sync.dma_start(out=x_raw[:], in_=xT.rearrange("(p j) t -> p j t", j=PACK))
         offs_t = keep.tile([P, E * C // 16], U16, name="offs_t")
         nc.sync.dma_start(offs_t[:], offs)
-        w1_raw = []
-        w2_at = (E + 2) * RAW + 3 * RAW // 2
-        w2_raw = placed.tile([P, E // 2, PACK, N], F32, name="w2_raw", align_bytes=64, offset=w2_at)
+        w2_raw = placed.tile([P, W2_WHOLE, PACK, N], F32, name="w2_raw", align_bytes=64, offset=W2_AT)
         w2_late = {
             (h, q): placed.tile(
-                [P, 2, PACK, P], F32, name=f"w2_late{h}_{q}", align_bytes=64, offset=w2_at + (2 + h) * RAW + (q - 2) * RAW // 2
+                [P, 2, PACK, P], F32, name=f"w2_late{h}_{q}", align_bytes=64, offset=W2_LATE_AT + (2 * h + q - 2) * 4 * KB
             )
             for h in range(2)
             for q in (2, 3)
         }
 
-        def load_w2_half(h, e0, e1):
-            for e in range(e0, e1):
-                nc.sync.dma_start(
-                    out=w2_late[h, e // 2][:, e % 2], in_=w2[e].rearrange("(p j) n -> p j n", j=PACK)[:, :, h * P : (h + 1) * P]
-                )
-
-        def load_w2(q):
+        def load_w2_pair(q):
             nc.sync.dma_start(
                 out=w2_raw[:, 2 * q : 2 * q + 2], in_=w2[2 * q : 2 * q + 2].rearrange("i (p j) n -> p i j n", j=PACK)
             )
 
+        def load_w2_late(h):
+            for e in range(W2_WHOLE, E):
+                nc.sync.dma_start(
+                    out=w2_late[h, e // 2][:, e % 2], in_=w2[e].rearrange("(p j) n -> p j n", j=PACK)[:, :, h * P : (h + 1) * P]
+                )
+
+        w1_raw = []
         for e in range(E):
-            t_ = placed.tile([P, PACK, H], F32, name=f"w1_raw{e}", align_bytes=256, offset=e * RAW)
-            nc.sync.dma_start(out=t_[:], in_=w1[e].rearrange("(p j) c -> p j c", j=PACK))
-            w1_raw.append(t_)
-            if e == 3:
-                load_w2(0)
-        load_w2(1)
-        load_w2_half(0, E // 2, E)
+            raw = placed.tile([P, PACK, H], F32, name=f"w1_raw{e}", align_bytes=256, offset=e * RAW)
+            nc.sync.dma_start(out=raw[:], in_=w1[e].rearrange("(p j) c -> p j c", j=PACK))
+            w1_raw.append(raw)
+            if e == E // 2 - 1:
+                load_w2_pair(0)
+        load_w2_pair(1)
+        load_w2_late(0)
         pos_t = []
         for r in range(TOP):
-            t_ = keep.tile([P, T // 16], U16, name=f"pos_t{r}")
-            nc.sync.dma_start(t_[:], pos[r])
-            pos_t.append(t_)
+            lst = keep.tile([P, T // 16], U16, name=f"pos_t{r}")
+            nc.sync.dma_start(lst[:], pos[r])
+            pos_t.append(lst)
         gates = []
         for r in range(TOP):
-            t_ = keep.tile([P, T], F32, name=f"gate{r}", align_bytes=256)
-            nc.sync.dma_start(out=t_[:], in_=gate[r, :P, :])
-            gates.append(t_)
+            rows = keep.tile([P, T], F32, name=f"gate{r}", align_bytes=256)
+            nc.sync.dma_start(out=rows[:], in_=gate[r, :P, :])
+            gates.append(rows)
             if r == 1:
-                load_w2_half(1, E // 2, E)
+                load_w2_late(1)
 
         x_parts = ((0, P), (P, 2 * P), (2 * P, T))
         xg = [keep.tile([P, t1 - t0, PACK], BF16, name=f"xg{t0}", align_bytes=64) for t0, t1 in x_parts]
 
-        def x_copy(copy, i, t0, t1):
-            first = x_parts[i][0]
+        def x_copy(copy, part, t0, t1):
+            first = x_parts[part][0]
             copy(
-                out=xg[i][:, t0 - first : t1 - first].rearrange("p (c i) (a b) -> p c a i b", i=4, b=2),
-                in_=x_raw[:, :, t0:t1].rearrange("p (a b) (c i) -> p c a i b", i=4, b=2),
+                out=xg[part][:, t0 - first : t1 - first].rearrange("p (c i) j -> p c j i", i=2),
+                in_=x_raw[:, :, t0:t1].rearrange("p j (c i) -> p c j i", i=2),
             )
 
         x_copy(nc.scalar.copy, 2, T - X_SCALAR, T)
         x_copy(nc.vector.tensor_copy, 0, 0, P)
         x_copy(nc.vector.tensor_copy, 1, P, 2 * P)
         x_copy(nc.vector.tensor_copy, 2, 2 * P, T - X_SCALAR)
-        for i, (t0, t1) in enumerate(x_parts):
-            nc.vector.quantize_mx(out=xw[:, t0:t1].bitcast(FP8X4), scales=xs[:, t0:t1], in_=xg[i][:].rearrange("p c j -> p (c j)"))
+        for part, (t0, t1) in enumerate(x_parts):
+            nc.vector.quantize_mx(out=xw[:, t0:t1].bitcast(FP8X4), scales=xs[:, t0:t1], in_=xg[part][:].rearrange("p c j -> p (c j)"))
 
-        w2_grouped = {}
-        w1_grouped, slot_words, slot_scales, banks, y_banks = {}, {}, {}, {}, {}
+        w1_grouped, w2_grouped, slot_words, slot_scales, banks, y_banks = {}, {}, {}, {}, {}, {}
         h_codes, h_scales, w2_codes, w2_scales = {}, {}, {}, {}
-        h_bf = [keep.tile([P, 2 * C * PACK], BF16, name=f"h_bf{q}", align_bytes=64) for q in range(PAIRS)]
+        h_bf = [keep.tile([P, 2 * C * PACK], BF16, name=f"h_bf{q}", align_bytes=64) for q in range(E // 2)]
         y = [
-            placed.tile([P, E * C], F32, name="y0", align_bytes=64, offset=(E + 2) * RAW + RAW // 2),
-            placed.tile([P, E * C], F32, name="y1", align_bytes=64, offset=w2_at + 31 * RAW // 8),
+            placed.tile([P, E * C], F32, name="y0", align_bytes=64, offset=Y0_AT),
+            placed.tile([P, E * C], F32, name="y1", align_bytes=64, offset=PAIR3_SECOND_AT + 3 * KB),
         ]
 
         def grouped_at(e):
-            return (e - 2) * RAW if e >= 2 else (E + 1) * RAW + e * RAW // 2
+            return (e - 2) * RAW if e >= 2 else FIRST_GROUPED_AT + e * 4 * KB
 
         def w1_copy(e):
-            if e < 2:
+            if e < W1_ON_SCALAR:
                 g = placed.tile([P, PACK * H], BF16, name=f"w1_grouped{e}", align_bytes=64, offset=grouped_at(e))
                 w1_grouped[e] = [g]
                 dst = g[:].rearrange("p (t m a b) -> p m a t b", t=4, a=2, b=2)
                 nc.scalar.copy(out=dst, in_=w1_raw[e][:].rearrange("p (a b) (m t) -> p m a t b", t=4, b=2))
                 return
-            src = w1_raw[e][:].rearrange("p (a b) (m u v) -> p u m a v b", u=2, v=2, b=2)
-            tiles = [
-                placed.tile([P, 2 * H], BF16, name=f"w1_grouped{e}_{u}", align_bytes=64, offset=grouped_at(e) + u * RAW // 4)
+            src = w1_raw[e][:].rearrange("p j (m u v) -> p u m j v", u=2, v=2)
+            w1_grouped[e] = [
+                placed.tile([P, 2 * H], BF16, name=f"w1_grouped{e}_{u}", align_bytes=64, offset=grouped_at(e) + u * 2 * KB)
                 for u in range(2)
             ]
-            w1_grouped[e] = tiles
-            dst = [g[:].rearrange("p (v m a b) -> p m a v b", v=2, a=2, b=2) for g in tiles]
-            for u in range(2):
-                nc.vector.tensor_copy(out=dst[u], in_=src[:, u])
+            for u, g in enumerate(w1_grouped[e]):
+                nc.vector.tensor_copy(out=g[:].rearrange("p (v m j) -> p m j v", v=2, j=PACK), in_=src[:, u])
 
         def pair_list(q):
             return offs_t[:, 2 * q * C // 16 : (2 * q + 2) * C // 16]
 
-        def gather_words(q):
-            end = (2 * q - 1) * RAW if q > 1 else (E + 1) * RAW - q * RAW // 2
-            slot_words[q] = placed.tile([P, 2 * C], U32, name=f"slot_words{q}", align_bytes=64, offset=end - 8 * C)
+        def gather_words(q, end):
+            slot_words[q] = placed.tile([P, 2 * C], U32, name=f"slot_words{q}", align_bytes=64, offset=end - 2 * KB)
             nc.vector.tensor_copy(slot_words[q][:], xw[:].bitcast(U32).indirect(pair_list(q)))
 
-        def gather_scales(q):
-            end = (E + 1, 1, 4, 6)[q] * RAW
-            slot_scales[q] = placed.tile([P, 2 * C], U8, name=f"slot_scales{q}", align_bytes=64, offset=end - 10 * C)
+        def gather_scales(q, end):
+            slot_scales[q] = placed.tile([P, 2 * C], U8, name=f"slot_scales{q}", align_bytes=64, offset=end - 2 * KB - 2 * C)
             nc.vector.tensor_copy(slot_scales[q][:], xs[:].indirect(pair_list(q)))
 
         def first_product(e):
@@ -155,30 +161,30 @@ def tile_moe_tk_mlp_relu2_kernel(tc, xT, w1, w2, gate, offs, pos1, pos2, pos3, p
                 cols = slice(u * width, (u + 1) * width)
                 nc.vector.quantize_mx(out=wc[:, cols].bitcast(FP8X4), scales=ws[:, cols], in_=g[:])
             banks[e] = []
-            for b in range(2):
+            for s in range(2):
                 ps = psum.tile([P, PACK, P], F32, name="bank")
-                part = slice((e % 2) * C + b * P, (e % 2) * C + (b + 1) * P)
+                slots = slice((e % 2) * C + s * P, (e % 2) * C + (s + 1) * P)
                 for t in range(PACK):
-                    m = slice(t * P, (t + 1) * P)
+                    cols = slice(t * P, (t + 1) * P)
                     nc.tensor.matmul_mx(
-                        out=ps[:, t, :], lhsT=wc[:, m].bitcast(FP8X4), lhsT_scale=ws[:, m],
-                        rhs=slot_words[e // 2][:, part].bitcast(FP8X4), rhs_scale=slot_scales[e // 2][:, part],
+                        out=ps[:, t, :], lhsT=wc[:, cols].bitcast(FP8X4), lhsT_scale=ws[:, cols],
+                        rhs=slot_words[e // 2][:, slots].bitcast(FP8X4), rhs_scale=slot_scales[e // 2][:, slots],
                         start=True, stop=True,
                     )
                 banks[e].append(ps)
 
         def squared_relu(e):
-            pos_part = placed.tile([P, C, PACK], F32, name=f"pos_part{e}", align_bytes=64, offset=(E + 2) * RAW + (e % 2) * RAW // 2)
-            for b in range(2):
-                nc.scalar.activation(pos_part[:, b * P : (b + 1) * P, :], banks[e][b][:].rearrange("p t n -> p n t"), RELU)
-            for b in range(2):
-                first = ((e % 2) * C + b * P) * PACK
+            relu = placed.tile([P, C, PACK], F32, name=f"pos_part{e}", align_bytes=64, offset=RELU_AT + (e % 2) * 4 * KB)
+            for s in range(2):
+                nc.scalar.activation(relu[:, s * P : (s + 1) * P, :], banks[e][s][:].rearrange("p t n -> p n t"), RELU)
+            for s in range(2):
+                first = ((e % 2) * C + s * P) * PACK
                 nc.scalar.activation(
-                    h_bf[e // 2][:, first : first + P * PACK], pos_part[:, b * P : (b + 1) * P, :].rearrange("p n t -> p (n t)"), SQUARE
+                    h_bf[e // 2][:, first : first + P * PACK], relu[:, s * P : (s + 1) * P, :].rearrange("p n t -> p (n t)"), SQUARE
                 )
 
-        def quantise_h(e0, e1, pool, **place):
-            hc = pool.tile([P, (e1 - e0) * C], U32, name=f"h_codes{e0}", align_bytes=64, **place)
+        def quantise_h(e0, e1, at):
+            hc = placed.tile([P, (e1 - e0) * C], U32, name=f"h_codes{e0}", align_bytes=64, offset=at)
             hs = keep.tile([P, (e1 - e0) * C], U8, name=f"h_scales{e0}", align_bytes=64)
             first = (e0 % 2) * C * PACK
             nc.vector.quantize_mx(
@@ -187,22 +193,19 @@ def tile_moe_tk_mlp_relu2_kernel(tc, xT, w1, w2, gate, offs, pos1, pos2, pos3, p
             for e in range(e0, e1):
                 h_codes[e], h_scales[e] = hc[:, (e - e0) * C : (e - e0 + 1) * C], hs[:, (e - e0) * C : (e - e0 + 1) * C]
 
-        def w2_copy(h, e0, e1, on_vector, pool, **place):
+        def w2_copy(copy, h, e0, e1, pool, **place):
             g = pool.tile([P, e1 - e0, P, PACK], BF16, name=f"w2_grouped{h}_{e0}", align_bytes=64, **place)
             w2_grouped[h, e0] = g
             for e in range(e0, e1):
-                dst = g[:, e - e0].rearrange("p (c i) (a b) -> p c a i b", i=4, b=2)
-                rows = w2_raw[:, e, :, h * P : (h + 1) * P] if e < E // 2 else w2_late[h, e // 2][:, e % 2]
-                src = rows.rearrange("p (a b) (c i) -> p c a i b", i=4, b=2)
-                if on_vector:
-                    nc.vector.tensor_copy(out=dst, in_=src)
-                else:
-                    nc.scalar.copy(out=dst, in_=src)
+                rows = w2_raw[:, e, :, h * P : (h + 1) * P] if e < W2_WHOLE else w2_late[h, e // 2][:, e % 2]
+                copy(
+                    out=g[:, e - e0].rearrange("p (c i) j -> p c j i", i=2),
+                    in_=rows.rearrange("p j (c i) -> p c j i", i=2),
+                )
 
         def quantise_w2(h, e0, e1, pool=keep, **place):
-            n_e = e1 - e0
-            wc = pool.tile([P, n_e * P], U32, name=f"w2_codes{h}_{e0}", align_bytes=64, **place)
-            ws = keep.tile([P, n_e * P], U8, name=f"w2_scales{h}_{e0}", align_bytes=64)
+            wc = pool.tile([P, (e1 - e0) * P], U32, name=f"w2_codes{h}_{e0}", align_bytes=64, **place)
+            ws = keep.tile([P, (e1 - e0) * P], U8, name=f"w2_scales{h}_{e0}", align_bytes=64)
             nc.vector.quantize_mx(
                 out=wc[:].bitcast(FP8X4), scales=ws[:], in_=w2_grouped[h, e0][:].rearrange("p i c j -> p (i c j)")
             )
@@ -240,54 +243,54 @@ def tile_moe_tk_mlp_relu2_kernel(tc, xT, w1, w2, gate, offs, pos1, pos2, pos3, p
                 nc.tensor.transpose(back[:, c, :], turned[:, c, :], ident[:])
             return back[:].rearrange("p c t -> p (c t)")
 
-        gather_words(0)
-        gather_scales(0)
-        gather_words(1)
+        gather_words(0, FIRST_SLOTS_END)
+        gather_scales(0, FIRST_SLOTS_END)
+        gather_words(1, FIRST_SLOTS_END - 4 * KB)
         w1_copy(0)
         first_product(0)
-        gather_scales(1)
+        gather_scales(1, RAW)
         w1_copy(1)
         for e in range(E):
             squared_relu(e)
             if e + 1 < E:
                 first_product(e + 1)
-            if e in (2, 4):
-                gather_scales(e // 2 + 1)
-            if e % 2 == 1 and e + 3 < E:
-                gather_words(e // 2 + 2)
+            if 1 <= e <= 4:
+                gather = gather_words if e % 2 == 1 else gather_scales
+                gather((e + 3) // 2, (e + 2) * RAW)
             if e + 2 < E:
                 w1_copy(e + 2)
             if e in (2, 3):
-                w2_copy(e - 2, 0, 2, False, keep)
-        KB = 1024
+                w2_copy(nc.scalar.copy, e - 2, 0, 2, keep)
+
         at6, at7 = 6 * RAW, 7 * RAW
-        quantise_h(0, 2, placed, offset=grouped_at(7))
-        w2_copy(0, 2, 4, True, placed, offset=at6 + 6 * KB)
-        quantise_h(2, 4, placed, offset=grouped_at(7) + RAW // 4)
+        quantise_h(0, 2, grouped_at(7))
+        w2_copy(nc.vector.tensor_copy, 0, 2, 4, placed, offset=at6 + 6 * KB)
+        quantise_h(2, 4, grouped_at(7) + 2 * KB)
         quantise_w2(0, 0, 2, placed, offset=grouped_at(6))
         quantise_w2(0, 2, 4)
-        w2_copy(0, 4, 5, True, placed, offset=at6 + 2 * KB)
-        w2_copy(0, 5, 6, True, placed, offset=at6 + 4 * KB)
+        w2_copy(nc.vector.tensor_copy, 0, 4, 5, placed, offset=at6 + 2 * KB)
+        w2_copy(nc.vector.tensor_copy, 0, 5, 6, placed, offset=at6 + 4 * KB)
         quantise_w2(0, 4, 5)
         quantise_w2(0, 5, 6)
-        quantise_h(4, 6, placed, offset=at6 + KB // 2)
-        quantise_h(6, 7, placed, offset=at6 + 3 * KB + KB // 2)
-        w2_copy(0, 6, 7, True, placed, offset=at7)
-        w2_copy(0, 7, 8, True, placed, offset=at7 + 3 * KB)
+        quantise_h(4, 6, at6 + KB // 2)
+        quantise_h(6, 7, at6 + 3 * KB + KB // 2)
+        w2_copy(nc.vector.tensor_copy, 0, 6, 7, placed, offset=at7)
+        w2_copy(nc.vector.tensor_copy, 0, 7, 8, placed, offset=at7 + 3 * KB)
         quantise_w2(0, 6, 7)
         quantise_w2(0, 7, 8)
-        quantise_h(7, 8, placed, offset=at7)
-        w2_copy(1, 2, 4, True, placed, offset=at7 + 3 * KB)
+        quantise_h(7, 8, at7)
+        w2_copy(nc.vector.tensor_copy, 1, 2, 4, placed, offset=at7 + 3 * KB)
         groups = ((0, 2), (2, 4), (4, 6), (6, 7), (7, 8))
         for e0, e1 in groups:
             second_product(0, e0, e1)
         for e0, e1 in groups:
             y_copy(0, e0, e1)
+
         quantise_w2(1, 2, 4)
         quantise_w2(1, 0, 2, placed, offset=at7 + 3 * KB)
-        w2_copy(1, 4, 6, False, keep, tag="w2_codes0_7")
+        w2_copy(nc.scalar.copy, 1, 4, 6, keep, tag="w2_codes0_7")
         quantise_w2(1, 4, 6)
-        w2_copy(1, 6, 8, False, keep, tag="w2_codes0_6")
+        w2_copy(nc.scalar.copy, 1, 6, 8, keep, tag="w2_codes0_6")
         quantise_w2(1, 6, 8)
         for e0 in range(0, E, 2):
             second_product(1, e0, e0 + 2)
@@ -295,9 +298,10 @@ def tile_moe_tk_mlp_relu2_kernel(tc, xT, w1, w2, gate, offs, pos1, pos2, pos3, p
             y_copy(1, e0, e0 + 2)
 
         acc = [psum.tile([P, P], F32, name="bank") for c in range(T // P)]
-        for r in range(TOP):
-            prod = fetch(0, r, placed, offset=w2_at + (24, 27, 29)[r - 1] * RAW // 8) if r >= 1 else fetch(0, r)
-            add_turned(acc, prod, r == 0, r == TOP - 1)
+        add_turned(acc, fetch(0, 0), True, False)
+        add_turned(acc, fetch(0, 1, placed, offset=PAIR2_SECOND_AT), False, False)
+        add_turned(acc, fetch(0, 2, placed, offset=PAIR3_SECOND_AT - KB), False, False)
+        add_turned(acc, fetch(0, 3, placed, offset=PAIR3_SECOND_AT + KB), False, True)
         back0 = turn_back(acc, "w2_codes1_6")
         res0 = keep.tile([P, T], F32, name="res0")
         nc.scalar.copy(out=res0[:], in_=back0)
@@ -306,7 +310,6 @@ def tile_moe_tk_mlp_relu2_kernel(tc, xT, w1, w2, gate, offs, pos1, pos2, pos3, p
         acc = [psum.tile([P, P], F32, name="bank") for c in range(T // P)]
         for r in range(2):
             add_turned(acc, fetch(1, r), r == 0, False)
-        halves = [slice(c * (T // 2), (c + 1) * (T // 2)) for c in range(2)]
 
         def fetch_part(r, cols):
             prod = keep.tile([P, cols.stop - cols.start], F32, name=f"prod1_{r}_{cols.start}", align_bytes=64)
@@ -316,18 +319,18 @@ def tile_moe_tk_mlp_relu2_kernel(tc, xT, w1, w2, gate, offs, pos1, pos2, pos3, p
 
         backs = []
         for c in range(2):
-            add_turned(acc[2 * c : 2 * c + 2], fetch_part(2, halves[c]), False, True)
+            add_turned(acc[2 * c : 2 * c + 2], fetch_part(2, slice(c * 2 * P, (c + 1) * 2 * P)), False, True)
             backs.append(turn_back(acc[2 * c : 2 * c + 2], f"turned1_{c}"))
         parts = (slice(0, 2 * P), slice(2 * P, 3 * P), slice(3 * P, T))
         sums = (backs[0], backs[1][:, :P], backs[1][:, P:])
 
-        def finish(i, last):
-            res1 = keep.tile([P, parts[i].stop - parts[i].start], F32, name=f"res1_{i}")
-            nc.vector.tensor_tensor(res1[:], sums[i], last[:], ADD)
-            nc.sync.dma_start(out[P:, parts[i]], res1[:])
+        def finish(part, fourth):
+            res1 = keep.tile([P, parts[part].stop - parts[part].start], F32, name=f"res1_{part}")
+            nc.vector.tensor_tensor(res1[:], sums[part], fourth[:], ADD)
+            nc.sync.dma_start(out[P:, parts[part]], res1[:])
 
-        lasts = [fetch_part(3, parts[i]) for i in range(2)]
-        finish(0, lasts[0])
-        lasts.append(fetch_part(3, parts[2]))
-        finish(1, lasts[1])
-        finish(2, lasts[2])
+        fourths = [fetch_part(3, parts[part]) for part in range(2)]
+        finish(0, fourths[0])
+        fourths.append(fetch_part(3, parts[2]))
+        finish(1, fourths[1])
+        finish(2, fourths[2])

@@ -23,6 +23,8 @@ SQUARE = mybir.ActivationFunctionType.Square
 
 X_SCALAR = 192
 W1_ON_SCALAR = 2
+ON_GPSIMD = (4, 6)
+M_VECTOR = 96
 W2_WHOLE = 4
 
 KB = 1024
@@ -82,7 +84,7 @@ def tile_moe_tk_mlp_relu2_kernel(tc, xT, w1, w2, gate, offs, pos1, pos2, pos3, p
             raw = placed.tile([P, PACK, H], F32, name=f"w1_raw{e}", align_bytes=256, offset=e * RAW)
             nc.sync.dma_start(out=raw[:], in_=w1[e].rearrange("(p j) c -> p j c", j=PACK))
             w1_raw.append(raw)
-            if e == E // 2 - 1:
+            if e == E // 2:
                 load_w2_pair(0)
         load_w2_pair(1)
         load_w2_late(0)
@@ -124,23 +126,36 @@ def tile_moe_tk_mlp_relu2_kernel(tc, xT, w1, w2, gate, offs, pos1, pos2, pos3, p
             placed.tile([P, E * C], F32, name="y1", align_bytes=64, offset=PAIR3_SECOND_AT + 3 * KB),
         ]
 
-        def grouped_at(e):
-            return (e - 2) * RAW if e >= 2 else FIRST_GROUPED_AT + e * 4 * KB
+        def grouped_at(e, u=0):
+            if u == 1 and e in ON_GPSIMD:
+                return grouped_at(e - 1) + 64
+            return (e - 2) * RAW + 2 * KB + u * 5 * KB // 2 if e >= 2 else FIRST_GROUPED_AT + e * 4 * KB
 
         def w1_copy(e):
             if e < W1_ON_SCALAR:
                 g = placed.tile([P, PACK * H], BF16, name=f"w1_grouped{e}", align_bytes=64, offset=grouped_at(e))
-                w1_grouped[e] = [g]
+                w1_grouped[e] = [(0, g)]
                 dst = g[:].rearrange("p (t m a b) -> p m a t b", t=4, a=2, b=2)
                 nc.scalar.copy(out=dst, in_=w1_raw[e][:].rearrange("p (a b) (m t) -> p m a t b", t=4, b=2))
                 return
             src = w1_raw[e][:].rearrange("p j (m u v) -> p u m j v", u=2, v=2)
-            w1_grouped[e] = [
-                placed.tile([P, 2 * H], BF16, name=f"w1_grouped{e}_{u}", align_bytes=64, offset=grouped_at(e) + u * 2 * KB)
+            tiles = [
+                placed.tile([P, 2 * H], BF16, name=f"w1_grouped{e}_{u}", align_bytes=64, offset=grouped_at(e, u))
                 for u in range(2)
             ]
-            for u, g in enumerate(w1_grouped[e]):
-                nc.vector.tensor_copy(out=g[:].rearrange("p (v m j) -> p m j v", v=2, j=PACK), in_=src[:, u])
+            dst = [g[:].rearrange("p (v m j) -> p m j v", v=2, j=PACK) for g in tiles]
+            w1_grouped[e] = list(enumerate(tiles))
+            if e not in ON_GPSIMD:
+                for u in range(2):
+                    nc.vector.tensor_copy(out=dst[u], in_=src[:, u])
+                return
+            for u, first in ((1, 0), (0, M_VECTOR)):
+                nc.gpsimd.tensor_scalar(
+                    dst[u][:, first:].rearrange("p m j v -> p m v j"), src[:, u, first:].rearrange("p m j v -> p m v j"),
+                    1.0, 0.0, MULT, ADD,
+                )
+            nc.vector.tensor_copy(out=dst[0][:, :M_VECTOR], in_=src[:, 0, :M_VECTOR])
+            w1_grouped[e].reverse()
 
         def pair_list(q):
             return offs_t[:, 2 * q * C // 16 : (2 * q + 2) * C // 16]
@@ -157,7 +172,7 @@ def tile_moe_tk_mlp_relu2_kernel(tc, xT, w1, w2, gate, offs, pos1, pos2, pos3, p
             wc = stage.tile([P, H], U32, name="w1_codes", align_bytes=64)
             ws = stage.tile([P, H], U8, name="w1_scales", align_bytes=64)
             width = H // len(w1_grouped[e])
-            for u, g in enumerate(w1_grouped[e]):
+            for u, g in w1_grouped[e]:
                 cols = slice(u * width, (u + 1) * width)
                 nc.vector.quantize_mx(out=wc[:, cols].bitcast(FP8X4), scales=ws[:, cols], in_=g[:])
             banks[e] = []
@@ -248,25 +263,26 @@ def tile_moe_tk_mlp_relu2_kernel(tc, xT, w1, w2, gate, offs, pos1, pos2, pos3, p
         gather_words(1, FIRST_SLOTS_END - 4 * KB)
         w1_copy(0)
         first_product(0)
-        gather_scales(1, RAW)
+        gather_scales(1, RAW + 2 * KB)
         w1_copy(1)
         for e in range(E):
             squared_relu(e)
             if e + 1 < E:
                 first_product(e + 1)
-            if 1 <= e <= 4:
-                gather = gather_words if e % 2 == 1 else gather_scales
-                gather((e + 3) // 2, (e + 2) * RAW)
+            if e in (2, 4):
+                gather_words(e // 2 + 1, grouped_at(e + 1) + 64)
+                gather_scales(e // 2 + 1, grouped_at(e + 1, 1) + 4 * KB)
+            if e == 3:
+                quantise_h(0, 2, grouped_at(4, 1) + 2 * KB - 64)
             if e + 2 < E:
                 w1_copy(e + 2)
             if e in (2, 3):
                 w2_copy(nc.scalar.copy, e - 2, 0, 2, keep)
 
         at6, at7 = 6 * RAW, 7 * RAW
-        quantise_h(0, 2, grouped_at(7))
+        quantise_h(2, 4, grouped_at(7))
         w2_copy(nc.vector.tensor_copy, 0, 2, 4, placed, offset=at6 + 6 * KB)
-        quantise_h(2, 4, grouped_at(7) + 2 * KB)
-        quantise_w2(0, 0, 2, placed, offset=grouped_at(6))
+        quantise_w2(0, 0, 2, placed, offset=grouped_at(7, 1))
         quantise_w2(0, 2, 4)
         w2_copy(nc.vector.tensor_copy, 0, 4, 5, placed, offset=at6 + 2 * KB)
         w2_copy(nc.vector.tensor_copy, 0, 5, 6, placed, offset=at6 + 4 * KB)

@@ -276,8 +276,8 @@ def tile_moe_tk_mlp_relu2_kernel(tc, xT, w1, w2, gate, offs, pos1, pos2, pos3, p
                 quantise_h(0, 2, grouped_at(4, 1) + 2 * KB - 64)
             if e + 2 < E:
                 w1_copy(e + 2)
-            if e in (2, 3):
-                w2_copy(nc.scalar.copy, e - 2, 0, 2, keep)
+            if e == 2:
+                w2_copy(nc.scalar.copy, 0, 0, 2, keep)
 
         at6, at7 = 6 * RAW, 7 * RAW
         quantise_h(2, 4, grouped_at(7))
@@ -295,15 +295,16 @@ def tile_moe_tk_mlp_relu2_kernel(tc, xT, w1, w2, gate, offs, pos1, pos2, pos3, p
         quantise_w2(0, 6, 7)
         quantise_w2(0, 7, 8)
         quantise_h(7, 8, at7)
-        w2_copy(nc.vector.tensor_copy, 1, 2, 4, placed, offset=at7 + 3 * KB)
+        w2_copy(nc.vector.tensor_copy, 1, 0, 2, placed, offset=at7 + KB + 64)
+        w2_copy(nc.vector.tensor_copy, 1, 2, 4, placed, offset=at7 + 3 * KB + 64)
         groups = ((0, 2), (2, 4), (4, 6), (6, 7), (7, 8))
         for e0, e1 in groups:
             second_product(0, e0, e1)
         for e0, e1 in groups:
             y_copy(0, e0, e1)
 
+        quantise_w2(1, 0, 2)
         quantise_w2(1, 2, 4)
-        quantise_w2(1, 0, 2, placed, offset=at7 + 3 * KB)
         w2_copy(nc.scalar.copy, 1, 4, 6, keep, tag="w2_codes0_7")
         quantise_w2(1, 4, 6)
         w2_copy(nc.scalar.copy, 1, 6, 8, keep, tag="w2_codes0_6")

@@ -24,10 +24,11 @@ SQUARE = mybir.ActivationFunctionType.Square
 X_SCALAR = 192
 W1_ON_SCALAR = 2
 ON_GPSIMD = (4, 6)
-M_VECTOR = 96
+M_VECTOR = 120
 W2_WHOLE = 4
 
 KB = 1024
+OVERLAP = 64
 RAW = PACK * H * 4
 FIRST_SLOTS_END = (E + 1) * RAW
 FIRST_GROUPED_AT = (E + 1) * RAW
@@ -89,12 +90,11 @@ def tile_moe_tk_mlp_relu2_kernel(tc, xT, w1, w2, gate, offs, pos1, pos2, pos3, p
         load_w2_pair(1)
         load_w2_late(0)
         pos_t = []
+        gates = []
         for r in range(TOP):
             lst = keep.tile([P, T // 16], U16, name=f"pos_t{r}")
             nc.sync.dma_start(lst[:], pos[r])
             pos_t.append(lst)
-        gates = []
-        for r in range(TOP):
             rows = keep.tile([P, T], F32, name=f"gate{r}", align_bytes=256)
             nc.sync.dma_start(out=rows[:], in_=gate[r, :P, :])
             gates.append(rows)
@@ -128,7 +128,7 @@ def tile_moe_tk_mlp_relu2_kernel(tc, xT, w1, w2, gate, offs, pos1, pos2, pos3, p
 
         def grouped_at(e, u=0):
             if u == 1 and e in ON_GPSIMD:
-                return grouped_at(e - 1) + 64
+                return grouped_at(e - 1) + OVERLAP
             return (e - 2) * RAW + 2 * KB + u * 5 * KB // 2 if e >= 2 else FIRST_GROUPED_AT + e * 4 * KB
 
         def w1_copy(e):
@@ -269,19 +269,20 @@ def tile_moe_tk_mlp_relu2_kernel(tc, xT, w1, w2, gate, offs, pos1, pos2, pos3, p
             squared_relu(e)
             if e + 1 < E:
                 first_product(e + 1)
-            if e in (2, 4):
-                gather_words(e // 2 + 1, grouped_at(e + 1) + 64)
+            if e + 2 in ON_GPSIMD:
+                gather_words(e // 2 + 1, grouped_at(e + 1) + OVERLAP)
                 gather_scales(e // 2 + 1, grouped_at(e + 1, 1) + 4 * KB)
-            if e == 3:
-                quantise_h(0, 2, grouped_at(4, 1) + 2 * KB - 64)
+            if e + 1 == ON_GPSIMD[0]:
+                quantise_h(0, 2, grouped_at(e + 1, 1) + 2 * KB - OVERLAP)
             if e + 2 < E:
                 w1_copy(e + 2)
-            if e == 2:
+            if e + 2 == E // 2:
                 w2_copy(nc.scalar.copy, 0, 0, 2, keep)
 
         at6, at7 = 6 * RAW, 7 * RAW
         quantise_h(2, 4, grouped_at(7))
         w2_copy(nc.vector.tensor_copy, 0, 2, 4, placed, offset=at6 + 6 * KB)
+        w2_copy(nc.vector.tensor_copy, 1, 0, 2, placed, offset=grouped_at(7, 1) + KB)
         quantise_w2(0, 0, 2, placed, offset=grouped_at(7, 1))
         quantise_w2(0, 2, 4)
         w2_copy(nc.vector.tensor_copy, 0, 4, 5, placed, offset=at6 + 2 * KB)
@@ -295,15 +296,14 @@ def tile_moe_tk_mlp_relu2_kernel(tc, xT, w1, w2, gate, offs, pos1, pos2, pos3, p
         quantise_w2(0, 6, 7)
         quantise_w2(0, 7, 8)
         quantise_h(7, 8, at7)
-        w2_copy(nc.vector.tensor_copy, 1, 0, 2, placed, offset=at7 + KB + 64)
-        w2_copy(nc.vector.tensor_copy, 1, 2, 4, placed, offset=at7 + 3 * KB + 64)
+        w2_copy(nc.vector.tensor_copy, 1, 2, 4, placed, offset=at7 + 3 * KB + OVERLAP)
         groups = ((0, 2), (2, 4), (4, 6), (6, 7), (7, 8))
         for e0, e1 in groups:
             second_product(0, e0, e1)
         for e0, e1 in groups:
             y_copy(0, e0, e1)
 
-        quantise_w2(1, 0, 2)
+        quantise_w2(1, 0, 2, placed, offset=at7 + 2 * KB + OVERLAP)
         quantise_w2(1, 2, 4)
         w2_copy(nc.scalar.copy, 1, 4, 6, keep, tag="w2_codes0_7")
         quantise_w2(1, 4, 6)

@@ -20,24 +20,23 @@ MULT = mybir.AluOpType.mult
 ADD = mybir.AluOpType.add
 RELU = mybir.ActivationFunctionType.Relu
 SQUARE = mybir.ActivationFunctionType.Square
+COPY = mybir.ActivationFunctionType.Copy
 
-X_SCALAR = 192
-W1_ON_SCALAR = 2
-ON_GPSIMD = (4, 6)
-M_VECTOR = 120
-W2_WHOLE = 4
+X_SCALAR = 80
+M_VECTOR = 96
 
 KB = 1024
-OVERLAP = 64
+BANK = 2 * KB
+SHIFT = 64
 RAW = PACK * H * 4
-FIRST_SLOTS_END = (E + 1) * RAW
-FIRST_GROUPED_AT = (E + 1) * RAW
-RELU_AT = (E + 2) * RAW
-Y0_AT = RELU_AT + 4 * KB
-W2_AT = Y0_AT + 8 * KB
-W2_LATE_AT = W2_AT + 16 * KB
-PAIR2_SECOND_AT = W2_LATE_AT + 8 * KB
-PAIR3_SECOND_AT = PAIR2_SECOND_AT + 4 * KB
+LAY_A, LAY_B, LAY_C = 64 * KB, 66 * KB, 68 * KB
+RELU_AT = 70 * KB
+H_LAST_AT = 78 * KB
+LATE_AT = 82 * KB
+Y1_AT = LATE_AT + 12 * KB - SHIFT
+LAY6_AT, LAY7_AT = 102 * KB, 104 * KB
+CODES7_AT = 108 * KB
+PICKED_AT = 111 * KB
 
 
 def tile_moe_tk_mlp_relu2_kernel(tc, xT, w1, w2, gate, offs, pos1, pos2, pos3, pos4, out):
@@ -47,149 +46,132 @@ def tile_moe_tk_mlp_relu2_kernel(tc, xT, w1, w2, gate, offs, pos1, pos2, pos3, p
         keep = ctx.enter_context(tc.tile_pool(name="keep", bufs=1))
         stage = ctx.enter_context(tc.tile_pool(name="stage", bufs=2))
         placed = ctx.enter_context(tc.tile_pool(name="placed", bufs=1))
-        psum = ctx.enter_context(tc.psum_pool(name="psum", bufs=8))
+        psum = ctx.enter_context(tc.psum_pool(name="psum", bufs=1))
 
-        xs = keep.tile([P, 2 * T], U8, name="xs", align_bytes=64)
+        def sb(shape, dtype, name, at=None):
+            if at is None:
+                return keep.tile(shape, dtype, name=name, align_bytes=64)
+            return placed.tile(shape, dtype, name=name, align_bytes=64, offset=at)
+
+        def bank(shape, name, b):
+            return psum.tile(shape, F32, name=name, offset=b * BANK)
+
+        xs = sb([P, 2 * T], U8, "xs")
         nc.gpsimd.memset(xs[:].bitcast(I32), 0)
-        xw = keep.tile([P, 2 * T], I32, name="xw", align_bytes=64)
+        xw = sb([P, 2 * T], I32, "xw")
         nc.vector.memset(xw[:, T:], 0)
         ident = keep.tile([P, P], F32, name="ident")
         make_identity(nc, ident[:])
 
-        x_raw = keep.tile([P, PACK, T], F32, name="x_raw", align_bytes=256)
-        nc.sync.dma_start(out=x_raw[:], in_=xT.rearrange("(p j) t -> p j t", j=PACK))
+        x_rows = xT.rearrange("(p j) t -> p j t", j=PACK)
+        x_raw = []
+        for half in range(2):
+            raw = keep.tile([P, PACK, T // 2], F32, name=f"x_raw{half}", align_bytes=256)
+            nc.sync.dma_start(out=raw[:], in_=x_rows[:, :, half * T // 2 : (half + 1) * T // 2])
+            x_raw.append(raw)
         offs_t = keep.tile([P, E * C // 16], U16, name="offs_t")
         nc.sync.dma_start(offs_t[:], offs)
-        w2_raw = placed.tile([P, W2_WHOLE, PACK, N], F32, name="w2_raw", align_bytes=64, offset=W2_AT)
-        w2_late = {
-            (h, q): placed.tile(
-                [P, 2, PACK, P], F32, name=f"w2_late{h}_{q}", align_bytes=64, offset=W2_LATE_AT + (2 * h + q - 2) * 4 * KB
-            )
-            for h in range(2)
-            for q in (2, 3)
-        }
+        w2_raw = {}
 
-        def load_w2_pair(q):
-            nc.sync.dma_start(
-                out=w2_raw[:, 2 * q : 2 * q + 2], in_=w2[2 * q : 2 * q + 2].rearrange("i (p j) n -> p i j n", j=PACK)
-            )
-
-        def load_w2_late(h):
-            for e in range(W2_WHOLE, E):
-                nc.sync.dma_start(
-                    out=w2_late[h, e // 2][:, e % 2], in_=w2[e].rearrange("(p j) n -> p j n", j=PACK)[:, :, h * P : (h + 1) * P]
-                )
+        def load_w2(h, q):
+            at = LATE_AT + (q - 1) * 4 * KB if h == 1 and q > 0 else None
+            w2_raw[h, q] = sb([P, 2, PACK, P], F32, f"w2_raw{h}_{q}", at)
+            for i in range(2):
+                rows = w2[2 * q + i].rearrange("(p j) n -> p j n", j=PACK)
+                nc.sync.dma_start(out=w2_raw[h, q][:, i], in_=rows[:, :, h * P : (h + 1) * P])
 
         w1_raw = []
         for e in range(E):
             raw = placed.tile([P, PACK, H], F32, name=f"w1_raw{e}", align_bytes=256, offset=e * RAW)
             nc.sync.dma_start(out=raw[:], in_=w1[e].rearrange("(p j) c -> p j c", j=PACK))
             w1_raw.append(raw)
-            if e == E // 2:
-                load_w2_pair(0)
-        load_w2_pair(1)
-        load_w2_late(0)
-        pos_t = []
-        gates = []
+            if e == 5:
+                load_w2(0, 0)
+        for q in range(1, E // 2):
+            load_w2(0, q)
+        pos_t, gates = [], []
         for r in range(TOP):
+            load_w2(1, r)
             lst = keep.tile([P, T // 16], U16, name=f"pos_t{r}")
             nc.sync.dma_start(lst[:], pos[r])
             pos_t.append(lst)
             rows = keep.tile([P, T], F32, name=f"gate{r}", align_bytes=256)
             nc.sync.dma_start(out=rows[:], in_=gate[r, :P, :])
             gates.append(rows)
-            if r == 1:
-                load_w2_late(1)
 
-        x_parts = ((0, P), (P, 2 * P), (2 * P, T))
-        xg = [keep.tile([P, t1 - t0, PACK], BF16, name=f"xg{t0}", align_bytes=64) for t0, t1 in x_parts]
+        def interleave(copy, dst, src):
+            copy(out=dst.rearrange("p (c i) j -> p c j i", i=2), in_=src.rearrange("p j (c i) -> p c j i", i=2))
 
-        def x_copy(copy, part, t0, t1):
-            first = x_parts[part][0]
-            copy(
-                out=xg[part][:, t0 - first : t1 - first].rearrange("p (c i) j -> p c j i", i=2),
-                in_=x_raw[:, :, t0:t1].rearrange("p j (c i) -> p c j i", i=2),
-            )
+        xg = [sb([P, T // 2, PACK], BF16, f"xg{half}") for half in range(2)]
+        cut = T // 2 - X_SCALAR
+        interleave(nc.scalar.copy, xg[1][:, cut:], x_raw[1][:, :, cut:])
+        for half in range(2):
+            upto = cut if half else T // 2
+            interleave(nc.vector.tensor_copy, xg[half][:, :upto], x_raw[half][:, :, :upto])
+            cols = slice(half * T // 2, (half + 1) * T // 2)
+            nc.vector.quantize_mx(out=xw[:, cols].bitcast(FP8X4), scales=xs[:, cols], in_=xg[half][:].rearrange("p c j -> p (c j)"))
 
-        x_copy(nc.scalar.copy, 2, T - X_SCALAR, T)
-        x_copy(nc.vector.tensor_copy, 0, 0, P)
-        x_copy(nc.vector.tensor_copy, 1, P, 2 * P)
-        x_copy(nc.vector.tensor_copy, 2, 2 * P, T - X_SCALAR)
-        for part, (t0, t1) in enumerate(x_parts):
-            nc.vector.quantize_mx(out=xw[:, t0:t1].bitcast(FP8X4), scales=xs[:, t0:t1], in_=xg[part][:].rearrange("p c j -> p (c j)"))
+        laid, slot_words, slot_scales, banks, y_banks = {}, {}, {}, {}, {}
+        w2_laid, h_codes, h_scales, w2_codes, w2_scales = {}, {}, {}, {}, {}
+        h_bf = [sb([P, 2 * C * PACK], BF16, f"h_bf{q}", H_LAST_AT if q == 3 else None) for q in range(E // 2)]
+        y = [sb([P, E * C], F32, "y0", RAW), sb([P, E * C], F32, "y1", Y1_AT)]
 
-        w1_grouped, w2_grouped, slot_words, slot_scales, banks, y_banks = {}, {}, {}, {}, {}, {}
-        h_codes, h_scales, w2_codes, w2_scales = {}, {}, {}, {}
-        h_bf = [keep.tile([P, 2 * C * PACK], BF16, name=f"h_bf{q}", align_bytes=64) for q in range(E // 2)]
-        y = [
-            placed.tile([P, E * C], F32, name="y0", align_bytes=64, offset=Y0_AT),
-            placed.tile([P, E * C], F32, name="y1", align_bytes=64, offset=PAIR3_SECOND_AT + 3 * KB),
-        ]
+        def on_gpsimd(dst, src):
+            nc.gpsimd.tensor_scalar(dst.rearrange("p m j v -> p m v j"), src.rearrange("p m j v -> p m v j"), 1.0, 0.0, MULT, ADD)
 
-        def grouped_at(e, u=0):
-            if u == 1 and e in ON_GPSIMD:
-                return grouped_at(e - 1) + OVERLAP
-            return (e - 2) * RAW + 2 * KB + u * 5 * KB // 2 if e >= 2 else FIRST_GROUPED_AT + e * 4 * KB
-
-        def w1_copy(e):
-            if e < W1_ON_SCALAR:
-                g = placed.tile([P, PACK * H], BF16, name=f"w1_grouped{e}", align_bytes=64, offset=grouped_at(e))
-                w1_grouped[e] = [(0, g)]
-                dst = g[:].rearrange("p (t m a b) -> p m a t b", t=4, a=2, b=2)
-                nc.scalar.copy(out=dst, in_=w1_raw[e][:].rearrange("p (a b) (m t) -> p m a t b", t=4, b=2))
-                return
+        def w1_layout(e):
             src = w1_raw[e][:].rearrange("p j (m u v) -> p u m j v", u=2, v=2)
-            tiles = [
-                placed.tile([P, 2 * H], BF16, name=f"w1_grouped{e}_{u}", align_bytes=64, offset=grouped_at(e, u))
-                for u in range(2)
-            ]
+            at = {
+                0: (LAY_B, LAY_C), 4: (LAY_A + SHIFT, LAY_B + SHIFT), 5: (LAY_B + SHIFT, LAY_A + SHIFT), 7: (LAY_B, LAY_A),
+            }.get(e, (LAY_A, LAY_B))
+            tiles = [sb([P, 2 * H], BF16, f"w1_laid{e}_{u}", at[u]) for u in range(2)]
             dst = [g[:].rearrange("p (v m j) -> p m j v", v=2, j=PACK) for g in tiles]
-            w1_grouped[e] = list(enumerate(tiles))
-            if e not in ON_GPSIMD:
+            laid[e] = list(enumerate(tiles))
+            if e < 2:
+                nc.scalar.copy(out=dst[0], in_=src[:, 0])
+                on_gpsimd(dst[1], src[:, 1])
+            elif e in (4, 6):
+                on_gpsimd(dst[1], src[:, 1])
+                on_gpsimd(dst[0][:, M_VECTOR:], src[:, 0, M_VECTOR:])
+                nc.vector.tensor_copy(out=dst[0][:, :M_VECTOR], in_=src[:, 0, :M_VECTOR])
+                laid[e].reverse()
+            else:
                 for u in range(2):
                     nc.vector.tensor_copy(out=dst[u], in_=src[:, u])
-                return
-            for u, first in ((1, 0), (0, M_VECTOR)):
-                nc.gpsimd.tensor_scalar(
-                    dst[u][:, first:].rearrange("p m j v -> p m v j"), src[:, u, first:].rearrange("p m j v -> p m v j"),
-                    1.0, 0.0, MULT, ADD,
-                )
-            nc.vector.tensor_copy(out=dst[0][:, :M_VECTOR], in_=src[:, 0, :M_VECTOR])
-            w1_grouped[e].reverse()
 
-        def pair_list(q):
-            return offs_t[:, 2 * q * C // 16 : (2 * q + 2) * C // 16]
+        def gather(window, dtype, into, e0, e1, name, at=None):
+            g = sb([P, (e1 - e0) * C], dtype, f"{name}{e0}", at)
+            nc.vector.tensor_copy(g[:], window.indirect(offs_t[:, e0 * C // 16 : e1 * C // 16]))
+            for e in range(e0, e1):
+                into[e] = g[:, (e - e0) * C : (e - e0 + 1) * C]
 
-        def gather_words(q, end):
-            slot_words[q] = placed.tile([P, 2 * C], U32, name=f"slot_words{q}", align_bytes=64, offset=end - 2 * KB)
-            nc.vector.tensor_copy(slot_words[q][:], xw[:].bitcast(U32).indirect(pair_list(q)))
+        def gather_words(e0, e1, at=None):
+            gather(xw[:].bitcast(U32), U32, slot_words, e0, e1, "slot_words", at)
 
-        def gather_scales(q, end):
-            slot_scales[q] = placed.tile([P, 2 * C], U8, name=f"slot_scales{q}", align_bytes=64, offset=end - 2 * KB - 2 * C)
-            nc.vector.tensor_copy(slot_scales[q][:], xs[:].indirect(pair_list(q)))
+        def gather_scales(e0, e1, at=None):
+            gather(xs[:], U8, slot_scales, e0, e1, "slot_scales", at)
 
         def first_product(e):
             wc = stage.tile([P, H], U32, name="w1_codes", align_bytes=64)
             ws = stage.tile([P, H], U8, name="w1_scales", align_bytes=64)
-            width = H // len(w1_grouped[e])
-            for u, g in w1_grouped[e]:
-                cols = slice(u * width, (u + 1) * width)
+            for u, g in laid[e]:
+                cols = slice(u * H // 2, (u + 1) * H // 2)
                 nc.vector.quantize_mx(out=wc[:, cols].bitcast(FP8X4), scales=ws[:, cols], in_=g[:])
             banks[e] = []
             for s in range(2):
-                ps = psum.tile([P, PACK, P], F32, name="bank")
-                slots = slice((e % 2) * C + s * P, (e % 2) * C + (s + 1) * P)
-                for t in range(PACK):
+                ps = bank([P, PACK, P], f"a{e}_{s}", (2 * e + s) % 8)
+                slots = slice(s * P, (s + 1) * P)
+                for t in [2 * u + v for u, g in laid[e] for v in range(2)]:
                     cols = slice(t * P, (t + 1) * P)
                     nc.tensor.matmul_mx(
                         out=ps[:, t, :], lhsT=wc[:, cols].bitcast(FP8X4), lhsT_scale=ws[:, cols],
-                        rhs=slot_words[e // 2][:, slots].bitcast(FP8X4), rhs_scale=slot_scales[e // 2][:, slots],
+                        rhs=slot_words[e][:, slots].bitcast(FP8X4), rhs_scale=slot_scales[e][:, slots],
                         start=True, stop=True,
                     )
                 banks[e].append(ps)
 
         def squared_relu(e):
-            relu = placed.tile([P, C, PACK], F32, name=f"pos_part{e}", align_bytes=64, offset=RELU_AT + (e % 2) * 4 * KB)
+            relu = sb([P, C, PACK], F32, f"relu{e}", RELU_AT + (e % 2) * 4 * KB)
             for s in range(2):
                 nc.scalar.activation(relu[:, s * P : (s + 1) * P, :], banks[e][s][:].rearrange("p t n -> p n t"), RELU)
             for s in range(2):
@@ -199,8 +181,8 @@ def tile_moe_tk_mlp_relu2_kernel(tc, xT, w1, w2, gate, offs, pos1, pos2, pos3, p
                 )
 
         def quantise_h(e0, e1, at):
-            hc = placed.tile([P, (e1 - e0) * C], U32, name=f"h_codes{e0}", align_bytes=64, offset=at)
-            hs = keep.tile([P, (e1 - e0) * C], U8, name=f"h_scales{e0}", align_bytes=64)
+            hc = sb([P, (e1 - e0) * C], U32, f"h_codes{e0}", at)
+            hs = sb([P, (e1 - e0) * C], U8, f"h_scales{e0}")
             first = (e0 % 2) * C * PACK
             nc.vector.quantize_mx(
                 out=hc[:].bitcast(FP8X4), scales=hs[:], in_=h_bf[e0 // 2][:, first : first + (e1 - e0) * C * PACK]
@@ -208,27 +190,23 @@ def tile_moe_tk_mlp_relu2_kernel(tc, xT, w1, w2, gate, offs, pos1, pos2, pos3, p
             for e in range(e0, e1):
                 h_codes[e], h_scales[e] = hc[:, (e - e0) * C : (e - e0 + 1) * C], hs[:, (e - e0) * C : (e - e0 + 1) * C]
 
-        def w2_copy(copy, h, e0, e1, pool, **place):
-            g = pool.tile([P, e1 - e0, P, PACK], BF16, name=f"w2_grouped{h}_{e0}", align_bytes=64, **place)
-            w2_grouped[h, e0] = g
+        def w2_layout(copy, h, e0, e1, at=None):
+            g = sb([P, e1 - e0, P, PACK], BF16, f"w2_laid{h}_{e0}", at)
+            w2_laid[h, e0] = g
             for e in range(e0, e1):
-                rows = w2_raw[:, e, :, h * P : (h + 1) * P] if e < W2_WHOLE else w2_late[h, e // 2][:, e % 2]
-                copy(
-                    out=g[:, e - e0].rearrange("p (c i) j -> p c j i", i=2),
-                    in_=rows.rearrange("p j (c i) -> p c j i", i=2),
-                )
+                interleave(copy, g[:, e - e0], w2_raw[h, e // 2][:, e % 2])
 
-        def quantise_w2(h, e0, e1, pool=keep, **place):
-            wc = pool.tile([P, (e1 - e0) * P], U32, name=f"w2_codes{h}_{e0}", align_bytes=64, **place)
-            ws = keep.tile([P, (e1 - e0) * P], U8, name=f"w2_scales{h}_{e0}", align_bytes=64)
+        def quantise_w2(h, e0, e1, at=None):
+            wc = sb([P, (e1 - e0) * P], U32, f"w2_codes{h}_{e0}", at)
+            ws = sb([P, (e1 - e0) * P], U8, f"w2_scales{h}_{e0}")
             nc.vector.quantize_mx(
-                out=wc[:].bitcast(FP8X4), scales=ws[:], in_=w2_grouped[h, e0][:].rearrange("p i c j -> p (i c j)")
+                out=wc[:].bitcast(FP8X4), scales=ws[:], in_=w2_laid[h, e0][:].rearrange("p i c j -> p (i c j)")
             )
             for e in range(e0, e1):
                 w2_codes[h, e], w2_scales[h, e] = wc[:, (e - e0) * P : (e - e0 + 1) * P], ws[:, (e - e0) * P : (e - e0 + 1) * P]
 
-        def second_product(h, e0, e1):
-            ps = psum.tile([P, e1 - e0, C], F32, name="bank")
+        def second_product(h, e0, e1, b):
+            ps = bank([P, e1 - e0, C], f"y{h}_{e0}", b)
             for e in range(e0, e1):
                 nc.tensor.matmul_mx(
                     out=ps[:, e - e0, :], lhsT=w2_codes[h, e].bitcast(FP8X4), lhsT_scale=w2_scales[h, e],
@@ -239,115 +217,114 @@ def tile_moe_tk_mlp_relu2_kernel(tc, xT, w1, w2, gate, offs, pos1, pos2, pos3, p
         def y_copy(h, e0, e1):
             nc.scalar.copy(out=y[h][:, e0 * C : e1 * C], in_=y_banks[h, e0][:].rearrange("p i c -> p (i c)"))
 
-        def fetch(h, r, pool=keep, **place):
-            prod = pool.tile([P, T], F32, name=f"prod{h}_{r}", align_bytes=64, **place)
-            nc.vector.tensor_tensor(prod[:], y[h][:].indirect(pos_t[r][:]), gates[r][:], MULT)
+        def fetch(h, r, t0, t1, at=None):
+            prod = sb([P, t1 - t0], F32, f"prod{h}_{r}_{t0}", at)
+            nc.vector.tensor_tensor(prod[:], y[h][:].indirect(pos_t[r][:, t0 // 16 : t1 // 16]), gates[r][:, t0:t1], MULT)
             return prod
 
-        def add_turned(acc, prod, first, last):
-            for c in range(len(acc)):
-                nc.tensor.matmul(
-                    acc[c][:], lhsT=prod[:, c * P : (c + 1) * P], rhs=ident[:], is_transpose=True, start=first, stop=last
-                )
+        def turn(dst, src, first, last):
+            nc.tensor.matmul(dst, lhsT=src, rhs=ident[:], is_transpose=True, start=first, stop=last)
 
-        def turn_back(acc, tag):
-            turned = keep.tile([P, len(acc), P], F32, name="turned", tag=tag, align_bytes=64)
-            back = psum.tile([P, len(acc), P], F32, name="bank")
-            for c in range(len(acc)):
-                nc.scalar.copy(out=turned[:, c, :], in_=acc[c][:])
-                nc.tensor.transpose(back[:, c, :], turned[:, c, :], ident[:])
-            return back[:].rearrange("p c t -> p (c t)")
-
-        gather_words(0, FIRST_SLOTS_END)
-        gather_scales(0, FIRST_SLOTS_END)
-        gather_words(1, FIRST_SLOTS_END - 4 * KB)
-        w1_copy(0)
+        gather_words(0, 2)
+        gather_scales(0, 2)
+        gather_words(2, 3)
+        w1_layout(0)
         first_product(0)
-        gather_scales(1, RAW + 2 * KB)
-        w1_copy(1)
+        gather_words(3, 4, 0)
+        gather_scales(2, 4, KB)
+        w1_layout(1)
         for e in range(E):
             squared_relu(e)
             if e + 1 < E:
                 first_product(e + 1)
-            if e + 2 in ON_GPSIMD:
-                gather_words(e // 2 + 1, grouped_at(e + 1) + OVERLAP)
-                gather_scales(e // 2 + 1, grouped_at(e + 1, 1) + 4 * KB)
-            if e + 1 == ON_GPSIMD[0]:
-                quantise_h(0, 2, grouped_at(e + 1, 1) + 2 * KB - OVERLAP)
+            if e in (2, 4):
+                quantise_h(e - 2, e, (e + 1) * RAW + 3 * KB)
+                gather_words(e + 2, e + 4, (e + 1) * RAW)
+                gather_scales(e + 2, e + 4, (e + 1) * RAW + 2 * KB)
+            if e == 3:
+                w2_layout(nc.scalar.copy, 0, 0, 2)
             if e + 2 < E:
-                w1_copy(e + 2)
-            if e + 2 == E // 2:
-                w2_copy(nc.scalar.copy, 0, 0, 2, keep)
+                w1_layout(e + 2)
 
-        at6, at7 = 6 * RAW, 7 * RAW
-        quantise_h(2, 4, grouped_at(7))
-        w2_copy(nc.vector.tensor_copy, 0, 2, 4, placed, offset=at6 + 6 * KB)
-        w2_copy(nc.vector.tensor_copy, 1, 0, 2, placed, offset=grouped_at(7, 1) + KB)
-        quantise_w2(0, 0, 2, placed, offset=grouped_at(7, 1))
-        quantise_w2(0, 2, 4)
-        w2_copy(nc.vector.tensor_copy, 0, 4, 5, placed, offset=at6 + 2 * KB)
-        w2_copy(nc.vector.tensor_copy, 0, 5, 6, placed, offset=at6 + 4 * KB)
-        quantise_w2(0, 4, 5)
-        quantise_w2(0, 5, 6)
-        quantise_h(4, 6, at6 + KB // 2)
-        quantise_h(6, 7, at6 + 3 * KB + KB // 2)
-        w2_copy(nc.vector.tensor_copy, 0, 6, 7, placed, offset=at7)
-        w2_copy(nc.vector.tensor_copy, 0, 7, 8, placed, offset=at7 + 3 * KB)
-        quantise_w2(0, 6, 7)
-        quantise_w2(0, 7, 8)
-        quantise_h(7, 8, at7)
-        w2_copy(nc.vector.tensor_copy, 1, 2, 4, placed, offset=at7 + 3 * KB + OVERLAP)
-        groups = ((0, 2), (2, 4), (4, 6), (6, 7), (7, 8))
-        for e0, e1 in groups:
-            second_product(0, e0, e1)
-        for e0, e1 in groups:
+        quantise_h(4, 6, 7 * RAW)
+        quantise_w2(0, 0, 2, 7 * RAW + 2 * KB)
+        for q in range(1, E // 2):
+            for e in (2 * q, 2 * q + 1):
+                w2_layout(nc.vector.tensor_copy, 0, e, e + 1, {6: LAY6_AT, 7: LAY7_AT}.get(e))
+            for e in (2 * q, 2 * q + 1):
+                quantise_w2(0, e, e + 1, CODES7_AT if e == 7 else None)
+        quantise_h(6, 7, LAY6_AT)
+        quantise_h(7, 8, LAY7_AT)
+        groups = ((0, 2, 6), (2, 4, 7), (4, 6, 4), (6, 7, 5), (7, 8, 0))
+        for e0, e1, b in groups:
+            second_product(0, e0, e1, b)
+        for e0, e1, b in groups:
             y_copy(0, e0, e1)
 
-        quantise_w2(1, 0, 2, placed, offset=at7 + 2 * KB + OVERLAP)
-        quantise_w2(1, 2, 4)
-        w2_copy(nc.scalar.copy, 1, 4, 6, keep, tag="w2_codes0_7")
-        quantise_w2(1, 4, 6)
-        w2_copy(nc.scalar.copy, 1, 6, 8, keep, tag="w2_codes0_6")
-        quantise_w2(1, 6, 8)
-        for e0 in range(0, E, 2):
-            second_product(1, e0, e0 + 2)
-        for e0 in range(0, E, 2):
-            y_copy(1, e0, e0 + 2)
+        gate_ps = bank([P, T // P, P], "gate_ps", 0)
+        for c in range(T // P):
+            turn(gate_ps[:, c, :], gates[0][:, c * P : (c + 1) * P], True, True)
+        gate_cols = sb([P, T // P], F32, "gate_cols")
+        nc.scalar.copy(out=gate_cols[:], in_=gate_ps[:, :, 0])
 
-        acc = [psum.tile([P, P], F32, name="bank") for c in range(T // P)]
-        add_turned(acc, fetch(0, 0), True, False)
-        add_turned(acc, fetch(0, 1, placed, offset=PAIR2_SECOND_AT), False, False)
-        add_turned(acc, fetch(0, 2, placed, offset=PAIR3_SECOND_AT - KB), False, False)
-        add_turned(acc, fetch(0, 3, placed, offset=PAIR3_SECOND_AT + KB), False, True)
-        back0 = turn_back(acc, "w2_codes1_6")
-        res0 = keep.tile([P, T], F32, name="res0")
-        nc.scalar.copy(out=res0[:], in_=back0)
-        nc.sync.dma_start(out[:P, :], res0[:])
+        for e in range(3):
+            w2_layout(nc.vector.tensor_copy, 1, e, e + 1, H_LAST_AT + e * KB)
+        for e in range(3):
+            quantise_w2(1, e, e + 1)
+        for e0, e1, at in ((3, 4, CODES7_AT - KB + SHIFT), (4, 6, CODES7_AT + SHIFT), (6, 8, LATE_AT + 2 * KB)):
+            w2_layout(nc.scalar.copy, 1, e0, e1, at)
+            quantise_w2(1, e0, e1)
+        for q, b in enumerate((2, 3, 0, 1)):
+            second_product(1, 2 * q, 2 * q + 2, b)
+        for q in range(E // 2):
+            y_copy(1, 2 * q, 2 * q + 2)
 
-        acc = [psum.tile([P, P], F32, name="bank") for c in range(T // P)]
-        for r in range(2):
-            add_turned(acc, fetch(1, r), r == 0, False)
+        acc = [bank([P, P], f"acc{c}", 4 + c) for c in range(T // P)]
+        for r in range(TOP):
+            prod = fetch(0, r, 0, T, (None, LATE_AT, LATE_AT + 7 * KB, LATE_AT + 9 * KB)[r])
+            for c in range(T // P):
+                turn(acc[c][:], prod[:, c * P : (c + 1) * P], r == 0, r == TOP - 1)
 
-        def fetch_part(r, cols):
-            prod = keep.tile([P, cols.stop - cols.start], F32, name=f"prod1_{r}_{cols.start}", align_bytes=64)
-            lst = pos_t[r][:, cols.start // 16 : cols.stop // 16]
-            nc.vector.tensor_tensor(prod[:], y[1][:].indirect(lst), gates[r][:, cols], MULT)
-            return prod
-
+        halves = (0, 1)
+        picked_ps = []
+        for a in halves:
+            picked = sb([P, 2 * P], F32, f"picked{a}", None if a else PICKED_AT)
+            nc.scalar.activation(picked[:], y[1][:].indirect(pos_t[0][:, a * 16 : (a + 1) * 16]), COPY)
+            ps = bank([P, 2, P], f"picked_ps{a}", 2 + a)
+            for c in range(2):
+                turn(ps[:, c, :], picked[:, c * P : (c + 1) * P], True, True)
+            picked_ps.append(ps)
+        turned0 = sb([P, T // P, P], F32, "turned0", PICKED_AT)
+        for c in range(T // P):
+            nc.scalar.copy(out=turned0[:, c, :], in_=acc[c][:])
+        back0 = bank([P, T // P, P], "back0", 4)
+        for c in range(T // P):
+            turn(back0[:, c, :], turned0[:, c, :], True, True)
+        gated = sb([P, T // P, P], F32, "gated")
+        for c in range(T // P):
+            nc.scalar.activation(gated[:, c, :], picked_ps[c // 2][:, c % 2, :], COPY, scale=gate_cols[:, c : c + 1])
+        second = fetch(1, 1, 0, T)
         backs = []
-        for c in range(2):
-            add_turned(acc[2 * c : 2 * c + 2], fetch_part(2, slice(c * 2 * P, (c + 1) * 2 * P)), False, True)
-            backs.append(turn_back(acc[2 * c : 2 * c + 2], f"turned1_{c}"))
-        parts = (slice(0, 2 * P), slice(2 * P, 3 * P), slice(3 * P, T))
-        sums = (backs[0], backs[1][:, :P], backs[1][:, P:])
-
-        def finish(part, fourth):
-            res1 = keep.tile([P, parts[part].stop - parts[part].start], F32, name=f"res1_{part}")
-            nc.vector.tensor_tensor(res1[:], sums[part], fourth[:], ADD)
-            nc.sync.dma_start(out[P:, parts[part]], res1[:])
-
-        fourths = [fetch_part(3, parts[part]) for part in range(2)]
-        finish(0, fourths[0])
-        fourths.append(fetch_part(3, parts[2]))
-        finish(1, fourths[1])
-        finish(2, fourths[2])
+        for a in halves:
+            third = fetch(1, 2, a * 2 * P, (a + 1) * 2 * P)
+            ps = bank([P, 2, P], f"sum_ps{a}", a)
+            for c in range(2):
+                turn(ps[:, c, :], second[:, (2 * a + c) * P : (2 * a + c + 1) * P], True, False)
+                turn(ps[:, c, :], third[:, c * P : (c + 1) * P], False, True)
+            turned1 = sb([P, 2, P], F32, f"turned1_{a}")
+            nc.scalar.copy(out=turned1[:], in_=ps[:])
+            back = bank([P, 2, P], f"back1_{a}", 5 + a)
+            for c in range(2):
+                turn(back[:, c, :], gated[:, 2 * a + c, :], True, False)
+                turn(back[:, c, :], turned1[:, c, :], False, True)
+            backs.append(back)
+        res0 = sb([P, T], F32, "res0")
+        nc.scalar.copy(out=res0[:], in_=back0[:].rearrange("p c t -> p (c t)"))
+        nc.sync.dma_start(out[:P, :], res0[:])
+        fourths = [fetch(1, 3, a * 2 * P, (a + 1) * 2 * P) for a in halves]
+        for a, c0, c1 in ((0, 0, 2), (1, 0, 1), (1, 1, 2)):
+            res1 = sb([P, (c1 - c0) * P], F32, f"res1_{a}_{c0}")
+            nc.vector.tensor_tensor(
+                res1[:], backs[a][:, c0:c1, :].rearrange("p c t -> p (c t)"), fourths[a][:, c0 * P : c1 * P], ADD
+            )
+            nc.sync.dma_start(out[P:, (2 * a + c0) * P : (2 * a + c1) * P], res1[:])

@@ -20,10 +20,9 @@ MULT = mybir.AluOpType.mult
 ADD = mybir.AluOpType.add
 RELU = mybir.ActivationFunctionType.Relu
 SQUARE = mybir.ActivationFunctionType.Square
-COPY = mybir.ActivationFunctionType.Copy
 
 X_SCALAR = 80
-M_VECTOR = 96
+M_VECTOR = 120
 
 KB = 1024
 BANK = 2 * KB
@@ -37,6 +36,10 @@ Y1_AT = LATE_AT + 12 * KB - SHIFT
 LAY6_AT, LAY7_AT = 102 * KB, 104 * KB
 CODES7_AT = 108 * KB
 PICKED_AT = 111 * KB
+LAY_D = 113 * KB
+FIRST_AT = 115 * KB
+LAY5_AT = 123 * KB
+EARLY_AT = 124 * KB
 
 
 def tile_moe_tk_mlp_relu2_kernel(tc, xT, w1, w2, gate, offs, pos1, pos2, pos3, pos4, out):
@@ -73,31 +76,47 @@ def tile_moe_tk_mlp_relu2_kernel(tc, xT, w1, w2, gate, offs, pos1, pos2, pos3, p
         nc.sync.dma_start(offs_t[:], offs)
         w2_raw = {}
 
-        def load_w2(h, q):
-            at = LATE_AT + (q - 1) * 4 * KB if h == 1 and q > 0 else None
-            w2_raw[h, q] = sb([P, 2, PACK, P], F32, f"w2_raw{h}_{q}", at)
-            for i in range(2):
-                rows = w2[2 * q + i].rearrange("(p j) n -> p j n", j=PACK)
-                nc.sync.dma_start(out=w2_raw[h, q][:, i], in_=rows[:, :, h * P : (h + 1) * P])
+        def load_whole(e0, e1, at=None):
+            raw = sb([P, e1 - e0, PACK, N], F32, f"w2_whole{e0}", at)
+            nc.sync.dma_start(out=raw[:], in_=w2[e0:e1].rearrange("i (p j) n -> p i j n", j=PACK))
+            for e in range(e0, e1):
+                for h in range(2):
+                    w2_raw[h, e] = raw[:, e - e0, :, h * P : (h + 1) * P]
+
+        def load_half(h, q):
+            raw = sb([P, 2, PACK, P], F32, f"w2_raw{h}_{q}", LATE_AT + (q - 1) * 4 * KB if h else None)
+            for e in (2 * q, 2 * q + 1):
+                rows = w2[e].rearrange("(p j) n -> p j n", j=PACK)
+                nc.sync.dma_start(out=raw[:, e % 2], in_=rows[:, :, h * P : (h + 1) * P])
+                w2_raw[h, e] = raw[:, e % 2]
 
         w1_raw = []
         for e in range(E):
-            raw = placed.tile([P, PACK, H], F32, name=f"w1_raw{e}", align_bytes=256, offset=e * RAW)
-            nc.sync.dma_start(out=raw[:], in_=w1[e].rearrange("(p j) c -> p j c", j=PACK))
+            rows = w1[e].rearrange("(p j) c -> p j c", j=PACK)
+            parts = 2 if e < 2 else 1
+            raw = []
+            for i in range(parts):
+                at = e * RAW + i * RAW // parts
+                raw.append(placed.tile([P, PACK, H // parts], F32, name=f"w1_raw{e}_{i}", align_bytes=256, offset=at))
+                nc.sync.dma_start(out=raw[i][:], in_=rows[:, :, i * H // parts : (i + 1) * H // parts])
             w1_raw.append(raw)
-            if e == 5:
-                load_w2(0, 0)
-        for q in range(1, E // 2):
-            load_w2(0, q)
+            if e == 6:
+                load_whole(0, 1, EARLY_AT)
+                load_whole(1, 2)
+        load_whole(2, 4)
+        for q in (2, 3):
+            load_half(0, q)
         pos_t, gates = [], []
         for r in range(TOP):
-            load_w2(1, r)
             lst = keep.tile([P, T // 16], U16, name=f"pos_t{r}")
             nc.sync.dma_start(lst[:], pos[r])
             pos_t.append(lst)
             rows = keep.tile([P, T], F32, name=f"gate{r}", align_bytes=256)
             nc.sync.dma_start(out=rows[:], in_=gate[r, :P, :])
             gates.append(rows)
+            if r == 1:
+                for q in (2, 3):
+                    load_half(1, q)
 
         def interleave(copy, dst, src):
             copy(out=dst.rearrange("p (c i) j -> p c j i", i=2), in_=src.rearrange("p j (c i) -> p c j i", i=2))
@@ -120,17 +139,24 @@ def tile_moe_tk_mlp_relu2_kernel(tc, xT, w1, w2, gate, offs, pos1, pos2, pos3, p
             nc.gpsimd.tensor_scalar(dst.rearrange("p m j v -> p m v j"), src.rearrange("p m j v -> p m v j"), 1.0, 0.0, MULT, ADD)
 
         def w1_layout(e):
-            src = w1_raw[e][:].rearrange("p j (m u v) -> p u m j v", u=2, v=2)
-            at = {
-                0: (LAY_B, LAY_C), 4: (LAY_A + SHIFT, LAY_B + SHIFT), 5: (LAY_B + SHIFT, LAY_A + SHIFT), 7: (LAY_B, LAY_A),
-            }.get(e, (LAY_A, LAY_B))
+            if e < 2:
+                tiles = [sb([P, 2 * H], BF16, f"w1_laid{e}_{u}", FIRST_AT + (2 * e + u) * 2 * KB) for u in range(2)]
+                laid[e] = list(enumerate(tiles))
+                for i in range(2):
+                    src = w1_raw[e][i][:].rearrange("p j (m u v) -> p u m j v", u=2, v=2)
+                    for u in range(2):
+                        dst = tiles[u][:].rearrange("p (v m j) -> p m j v", v=2, j=PACK)[:, i * P // 2 : (i + 1) * P // 2]
+                        if u and (e, i) != (1, 0):
+                            on_gpsimd(dst, src[:, u])
+                        else:
+                            nc.scalar.copy(out=dst, in_=src[:, u])
+                return
+            src = w1_raw[e][0][:].rearrange("p j (m u v) -> p u m j v", u=2, v=2)
+            at = {2: (RAW + 4 * KB + SHIFT, LAY_C), 3: (LAY_A, LAY_B), 4: (LAY_C, LAY_A), 5: (LAY_A, LAY_D), 6: (LAY_C, LAY_A), 7: (LAY_A, LAY_D)}[e]
             tiles = [sb([P, 2 * H], BF16, f"w1_laid{e}_{u}", at[u]) for u in range(2)]
             dst = [g[:].rearrange("p (v m j) -> p m j v", v=2, j=PACK) for g in tiles]
             laid[e] = list(enumerate(tiles))
-            if e < 2:
-                nc.scalar.copy(out=dst[0], in_=src[:, 0])
-                on_gpsimd(dst[1], src[:, 1])
-            elif e in (4, 6):
+            if e in (4, 6):
                 on_gpsimd(dst[1], src[:, 1])
                 on_gpsimd(dst[0][:, M_VECTOR:], src[:, 0, M_VECTOR:])
                 nc.vector.tensor_copy(out=dst[0][:, :M_VECTOR], in_=src[:, 0, :M_VECTOR])
@@ -154,14 +180,15 @@ def tile_moe_tk_mlp_relu2_kernel(tc, xT, w1, w2, gate, offs, pos1, pos2, pos3, p
         def first_product(e):
             wc = stage.tile([P, H], U32, name="w1_codes", align_bytes=64)
             ws = stage.tile([P, H], U8, name="w1_scales", align_bytes=64)
+            width = H // len(laid[e])
             for u, g in laid[e]:
-                cols = slice(u * H // 2, (u + 1) * H // 2)
+                cols = slice(u * width, (u + 1) * width)
                 nc.vector.quantize_mx(out=wc[:, cols].bitcast(FP8X4), scales=ws[:, cols], in_=g[:])
             banks[e] = []
             for s in range(2):
                 ps = bank([P, PACK, P], f"a{e}_{s}", (2 * e + s) % 8)
                 slots = slice(s * P, (s + 1) * P)
-                for t in [2 * u + v for u, g in laid[e] for v in range(2)]:
+                for t in [u * width // P + v for u, g in laid[e] for v in range(width // P)]:
                     cols = slice(t * P, (t + 1) * P)
                     nc.tensor.matmul_mx(
                         out=ps[:, t, :], lhsT=wc[:, cols].bitcast(FP8X4), lhsT_scale=ws[:, cols],
@@ -171,7 +198,7 @@ def tile_moe_tk_mlp_relu2_kernel(tc, xT, w1, w2, gate, offs, pos1, pos2, pos3, p
                 banks[e].append(ps)
 
         def squared_relu(e):
-            relu = sb([P, C, PACK], F32, f"relu{e}", RELU_AT + (e % 2) * 4 * KB)
+            relu = sb([P, C, PACK], F32, f"relu{e}", {0: RAW + SHIFT, 6: EARLY_AT}.get(e, RELU_AT + (e % 2) * 4 * KB))
             for s in range(2):
                 nc.scalar.activation(relu[:, s * P : (s + 1) * P, :], banks[e][s][:].rearrange("p t n -> p n t"), RELU)
             for s in range(2):
@@ -194,7 +221,7 @@ def tile_moe_tk_mlp_relu2_kernel(tc, xT, w1, w2, gate, offs, pos1, pos2, pos3, p
             g = sb([P, e1 - e0, P, PACK], BF16, f"w2_laid{h}_{e0}", at)
             w2_laid[h, e0] = g
             for e in range(e0, e1):
-                interleave(copy, g[:, e - e0], w2_raw[h, e // 2][:, e % 2])
+                interleave(copy, g[:, e - e0], w2_raw[h, e])
 
         def quantise_w2(h, e0, e1, at=None):
             wc = sb([P, (e1 - e0) * P], U32, f"w2_codes{h}_{e0}", at)
@@ -225,55 +252,66 @@ def tile_moe_tk_mlp_relu2_kernel(tc, xT, w1, w2, gate, offs, pos1, pos2, pos3, p
         def turn(dst, src, first, last):
             nc.tensor.matmul(dst, lhsT=src, rhs=ident[:], is_transpose=True, start=first, stop=last)
 
+        def turn_back(acc, name, b, at=None):
+            turned = sb([P, len(acc), P], F32, name, at)
+            back = bank([P, len(acc), P], f"back_{name}", b)
+            for c in range(len(acc)):
+                nc.scalar.copy(out=turned[:, c, :], in_=acc[c][:])
+                turn(back[:, c, :], turned[:, c, :], True, True)
+            return back[:].rearrange("p c t -> p (c t)")
+
+        def add_turned(acc, prod, first, last):
+            for c in range(len(acc)):
+                turn(acc[c][:], prod[:, c * P : (c + 1) * P], first, last)
+
         gather_words(0, 2)
         gather_scales(0, 2)
-        gather_words(2, 3)
         w1_layout(0)
         first_product(0)
-        gather_words(3, 4, 0)
-        gather_scales(2, 4, KB)
+        gather_words(2, 4, 4 * KB)
+        gather_scales(2, 4, 6 * KB)
         w1_layout(1)
         for e in range(E):
             squared_relu(e)
             if e + 1 < E:
                 first_product(e + 1)
             if e in (2, 4):
-                quantise_h(e - 2, e, (e + 1) * RAW + 3 * KB)
                 gather_words(e + 2, e + 4, (e + 1) * RAW)
                 gather_scales(e + 2, e + 4, (e + 1) * RAW + 2 * KB)
-            if e == 3:
+            if e == 5:
+                w2_layout(nc.scalar.copy, 1, 0, 1)
                 w2_layout(nc.scalar.copy, 0, 0, 2)
             if e + 2 < E:
                 w1_layout(e + 2)
 
-        quantise_h(4, 6, 7 * RAW)
-        quantise_w2(0, 0, 2, 7 * RAW + 2 * KB)
-        for q in range(1, E // 2):
+        at7 = 7 * RAW
+        w2_last_at = PICKED_AT
+        quantise_h(0, 2, at7 - 2 * KB + SHIFT)
+        quantise_h(2, 4, at7 + SHIFT)
+        w2_layout(nc.vector.tensor_copy, 0, 2, 4)
+        w2_layout(nc.vector.tensor_copy, 1, 1, 2, at7 + 6 * KB)
+        quantise_w2(0, 0, 2, at7 + 3 * KB)
+        quantise_w2(0, 2, 4)
+        quantise_h(4, 6, at7 + 4 * KB)
+        for q in (2, 3):
             for e in (2 * q, 2 * q + 1):
-                w2_layout(nc.vector.tensor_copy, 0, e, e + 1, {6: LAY6_AT, 7: LAY7_AT}.get(e))
+                w2_layout(nc.vector.tensor_copy, 0, e, e + 1, {5: LAY5_AT, 7: LAY7_AT}.get(e))
             for e in (2 * q, 2 * q + 1):
                 quantise_w2(0, e, e + 1, CODES7_AT if e == 7 else None)
-        quantise_h(6, 7, LAY6_AT)
-        quantise_h(7, 8, LAY7_AT)
+            quantise_h(q + 4, q + 5, LAY5_AT if q == 2 else LAY7_AT + KB - SHIFT)
         groups = ((0, 2, 6), (2, 4, 7), (4, 6, 4), (6, 7, 5), (7, 8, 0))
         for e0, e1, b in groups:
             second_product(0, e0, e1, b)
         for e0, e1, b in groups:
             y_copy(0, e0, e1)
 
-        gate_ps = bank([P, T // P, P], "gate_ps", 0)
-        for c in range(T // P):
-            turn(gate_ps[:, c, :], gates[0][:, c * P : (c + 1) * P], True, True)
-        gate_cols = sb([P, T // P], F32, "gate_cols")
-        nc.scalar.copy(out=gate_cols[:], in_=gate_ps[:, :, 0])
-
-        for e in range(3):
-            w2_layout(nc.vector.tensor_copy, 1, e, e + 1, H_LAST_AT + e * KB)
-        for e in range(3):
-            quantise_w2(1, e, e + 1)
-        for e0, e1, at in ((3, 4, CODES7_AT - KB + SHIFT), (4, 6, CODES7_AT + SHIFT), (6, 8, LATE_AT + 2 * KB)):
+        w2_layout(nc.vector.tensor_copy, 1, 2, 4, LAY7_AT - 2 * KB + SHIFT)
+        quantise_w2(1, 0, 1, LAY7_AT + SHIFT)
+        quantise_w2(1, 1, 2)
+        quantise_w2(1, 2, 4)
+        for e0, e1, at in ((4, 6, CODES7_AT - 2 * KB + SHIFT), (6, 8, CODES7_AT + SHIFT)):
             w2_layout(nc.scalar.copy, 1, e0, e1, at)
-            quantise_w2(1, e0, e1)
+            quantise_w2(1, e0, e1, w2_last_at if e0 == 6 else None)
         for q, b in enumerate((2, 3, 0, 1)):
             second_product(1, 2 * q, 2 * q + 2, b)
         for q in range(E // 2):
@@ -281,50 +319,31 @@ def tile_moe_tk_mlp_relu2_kernel(tc, xT, w1, w2, gate, offs, pos1, pos2, pos3, p
 
         acc = [bank([P, P], f"acc{c}", 4 + c) for c in range(T // P)]
         for r in range(TOP):
-            prod = fetch(0, r, 0, T, (None, LATE_AT, LATE_AT + 7 * KB, LATE_AT + 9 * KB)[r])
-            for c in range(T // P):
-                turn(acc[c][:], prod[:, c * P : (c + 1) * P], r == 0, r == TOP - 1)
-
-        halves = (0, 1)
-        picked_ps = []
-        for a in halves:
-            picked = sb([P, 2 * P], F32, f"picked{a}", None if a else PICKED_AT)
-            nc.scalar.activation(picked[:], y[1][:].indirect(pos_t[0][:, a * 16 : (a + 1) * 16]), COPY)
-            ps = bank([P, 2, P], f"picked_ps{a}", 2 + a)
-            for c in range(2):
-                turn(ps[:, c, :], picked[:, c * P : (c + 1) * P], True, True)
-            picked_ps.append(ps)
-        turned0 = sb([P, T // P, P], F32, "turned0", PICKED_AT)
-        for c in range(T // P):
-            nc.scalar.copy(out=turned0[:, c, :], in_=acc[c][:])
-        back0 = bank([P, T // P, P], "back0", 4)
-        for c in range(T // P):
-            turn(back0[:, c, :], turned0[:, c, :], True, True)
-        gated = sb([P, T // P, P], F32, "gated")
-        for c in range(T // P):
-            nc.scalar.activation(gated[:, c, :], picked_ps[c // 2][:, c % 2, :], COPY, scale=gate_cols[:, c : c + 1])
-        second = fetch(1, 1, 0, T)
-        backs = []
-        for a in halves:
-            third = fetch(1, 2, a * 2 * P, (a + 1) * 2 * P)
-            ps = bank([P, 2, P], f"sum_ps{a}", a)
-            for c in range(2):
-                turn(ps[:, c, :], second[:, (2 * a + c) * P : (2 * a + c + 1) * P], True, False)
-                turn(ps[:, c, :], third[:, c * P : (c + 1) * P], False, True)
-            turned1 = sb([P, 2, P], F32, f"turned1_{a}")
-            nc.scalar.copy(out=turned1[:], in_=ps[:])
-            back = bank([P, 2, P], f"back1_{a}", 5 + a)
-            for c in range(2):
-                turn(back[:, c, :], gated[:, 2 * a + c, :], True, False)
-                turn(back[:, c, :], turned1[:, c, :], False, True)
-            backs.append(back)
+            prod = fetch(0, r, 0, T, (None, LATE_AT + 4 * KB, LATE_AT + 7 * KB, LATE_AT + 9 * KB)[r])
+            add_turned(acc, prod, r == 0, r == TOP - 1)
+        back0 = turn_back(acc, "turned0", 4, w2_last_at)
         res0 = sb([P, T], F32, "res0")
-        nc.scalar.copy(out=res0[:], in_=back0[:].rearrange("p c t -> p (c t)"))
+        nc.scalar.copy(out=res0[:], in_=back0)
         nc.sync.dma_start(out[:P, :], res0[:])
-        fourths = [fetch(1, 3, a * 2 * P, (a + 1) * 2 * P) for a in halves]
-        for a, c0, c1 in ((0, 0, 2), (1, 0, 1), (1, 1, 2)):
-            res1 = sb([P, (c1 - c0) * P], F32, f"res1_{a}_{c0}")
-            nc.vector.tensor_tensor(
-                res1[:], backs[a][:, c0:c1, :].rearrange("p c t -> p (c t)"), fourths[a][:, c0 * P : c1 * P], ADD
-            )
-            nc.sync.dma_start(out[P:, (2 * a + c0) * P : (2 * a + c1) * P], res1[:])
+
+        acc = [bank([P, P], f"sum{c}", b) for c, b in enumerate((2, 3, 0, 1))]
+        for r in range(2):
+            add_turned(acc, fetch(1, r, 0, T), r == 0, False)
+        backs = []
+        for a in range(2):
+            add_turned(acc[2 * a : 2 * a + 2], fetch(1, 2, a * 2 * P, (a + 1) * 2 * P), False, True)
+            backs.append(turn_back(acc[2 * a : 2 * a + 2], f"turned1_{a}", 5 + a))
+        parts = ((0, 2 * P), (2 * P, 3 * P), (3 * P, T))
+        sums = (backs[0], backs[1][:, :P], backs[1][:, P:])
+
+        def finish(part, fourth):
+            t0, t1 = parts[part]
+            res1 = sb([P, t1 - t0], F32, f"res1_{part}")
+            nc.vector.tensor_tensor(res1[:], sums[part], fourth[:], ADD)
+            nc.sync.dma_start(out[P:, t0:t1], res1[:])
+
+        fourths = [fetch(1, 3, *parts[part]) for part in range(2)]
+        finish(0, fourths[0])
+        fourths.append(fetch(1, 3, *parts[2]))
+        finish(1, fourths[1])
+        finish(2, fourths[2])

@@ -20,6 +20,7 @@ MULT = mybir.AluOpType.mult
 ADD = mybir.AluOpType.add
 RELU = mybir.ActivationFunctionType.Relu
 SQUARE = mybir.ActivationFunctionType.Square
+COPY = mybir.ActivationFunctionType.Copy
 
 X_SCALAR = 80
 M_VECTOR = 120
@@ -40,6 +41,7 @@ LAY_D = 113 * KB
 FIRST_AT = 115 * KB
 LAY5_AT = 123 * KB
 EARLY_AT = 124 * KB
+FETCHED_AT = 128 * KB
 
 
 def tile_moe_tk_mlp_relu2_kernel(tc, xT, w1, w2, gate, offs, pos1, pos2, pos3, pos4, out):
@@ -321,18 +323,26 @@ def tile_moe_tk_mlp_relu2_kernel(tc, xT, w1, w2, gate, offs, pos1, pos2, pos3, p
         for r in range(TOP):
             prod = fetch(0, r, 0, T, (None, LATE_AT + 4 * KB, LATE_AT + 7 * KB, LATE_AT + 9 * KB)[r])
             add_turned(acc, prod, r == 0, r == TOP - 1)
+        fetched = [sb([P, T // 2], F32, f"fetched{a}", FETCHED_AT + a * KB) for a in range(2)]
+        for a in range(2):
+            nc.scalar.activation(fetched[a][:], y[1][:].indirect(pos_t[0][:, a * 16 : (a + 1) * 16]), COPY)
         back0 = turn_back(acc, "turned0", 4, w2_last_at)
         res0 = sb([P, T], F32, "res0")
         nc.scalar.copy(out=res0[:], in_=back0)
         nc.sync.dma_start(out[:P, :], res0[:])
 
         acc = [bank([P, P], f"sum{c}", b) for c, b in enumerate((2, 3, 0, 1))]
-        for r in range(2):
-            add_turned(acc, fetch(1, r, 0, T), r == 0, False)
+        add_turned(acc, fetch(1, 1, 0, T), True, False)
+        add_turned(acc[:2], fetch(1, 2, 0, 2 * P), False, False)
         backs = []
         for a in range(2):
-            add_turned(acc[2 * a : 2 * a + 2], fetch(1, 2, a * 2 * P, (a + 1) * 2 * P), False, True)
-            backs.append(turn_back(acc[2 * a : 2 * a + 2], f"turned1_{a}", 5 + a))
+            gated = sb([P, T // 2], F32, f"gated{a}")
+            nc.vector.tensor_tensor(gated[:], fetched[a][:], gates[0][:, a * 2 * P : (a + 1) * 2 * P], MULT)
+            add_turned(acc[2 * a : 2 * a + 2], gated, False, a == 0)
+            if a == 0:
+                backs.append(turn_back(acc[:2], "turned1_0", 5))
+        add_turned(acc[2:], fetch(1, 2, 2 * P, T, FETCHED_AT), False, True)
+        backs.append(turn_back(acc[2:], "turned1_1", 6))
         parts = ((0, 2 * P), (2 * P, 3 * P), (3 * P, T))
         sums = (backs[0], backs[1][:, :P], backs[1][:, P:])
 

@@ -41,7 +41,6 @@ LAY_D = 113 * KB
 FIRST_AT = 115 * KB
 LAY5_AT = 123 * KB
 EARLY_AT = 124 * KB
-FETCHED_AT = 128 * KB
 
 
 def tile_moe_tk_mlp_relu2_kernel(tc, xT, w1, w2, gate, offs, pos1, pos2, pos3, pos4, out):
@@ -323,37 +322,28 @@ def tile_moe_tk_mlp_relu2_kernel(tc, xT, w1, w2, gate, offs, pos1, pos2, pos3, p
         for r in range(TOP):
             prod = fetch(0, r, 0, T, (None, LATE_AT + 4 * KB, LATE_AT + 7 * KB, LATE_AT + 9 * KB)[r])
             add_turned(acc, prod, r == 0, r == TOP - 1)
-        fetched = [sb([P, T // 2], F32, f"fetched{a}", FETCHED_AT + a * KB) for a in range(2)]
-        for a in range(2):
-            nc.scalar.activation(fetched[a][:], y[1][:].indirect(pos_t[0][:, a * 16 : (a + 1) * 16]), COPY)
+
+        def fetch_plain(r, t0, t1):
+            values = sb([P, t1 - t0], F32, f"fetched{r}_{t0}")
+            nc.scalar.activation(values[:], y[1][:].indirect(pos_t[r][:, t0 // 16 : t1 // 16]), COPY)
+            return values
+
+        halves = (slice(0, T // 2), slice(T // 2, T))
+        fetched0 = fetch_plain(0, 0, T)
         back0 = turn_back(acc, "turned0", 4, w2_last_at)
+        fetched1 = [fetch_plain(1, half.start, half.stop) for half in halves]
         res0 = sb([P, T], F32, "res0")
         nc.scalar.copy(out=res0[:], in_=back0)
         nc.sync.dma_start(out[:P, :], res0[:])
 
-        acc = [bank([P, P], f"sum{c}", b) for c, b in enumerate((2, 3, 0, 1))]
-        add_turned(acc, fetch(1, 1, 0, T), True, False)
-        add_turned(acc[:2], fetch(1, 2, 0, 2 * P), False, False)
-        backs = []
-        for a in range(2):
-            gated = sb([P, T // 2], F32, f"gated{a}")
-            nc.vector.tensor_tensor(gated[:], fetched[a][:], gates[0][:, a * 2 * P : (a + 1) * 2 * P], MULT)
-            add_turned(acc[2 * a : 2 * a + 2], gated, False, a == 0)
-            if a == 0:
-                backs.append(turn_back(acc[:2], "turned1_0", 5))
-        add_turned(acc[2:], fetch(1, 2, 2 * P, T, FETCHED_AT), False, True)
-        backs.append(turn_back(acc[2:], "turned1_1", 6))
-        parts = ((0, 2 * P), (2 * P, 3 * P), (3 * P, T))
-        sums = (backs[0], backs[1][:, :P], backs[1][:, P:])
-
-        def finish(part, fourth):
-            t0, t1 = parts[part]
-            res1 = sb([P, t1 - t0], F32, f"res1_{part}")
-            nc.vector.tensor_tensor(res1[:], sums[part], fourth[:], ADD)
-            nc.sync.dma_start(out[P:, t0:t1], res1[:])
-
-        fourths = [fetch(1, 3, *parts[part]) for part in range(2)]
-        finish(0, fourths[0])
-        fourths.append(fetch(1, 3, *parts[2]))
-        finish(1, fourths[1])
-        finish(2, fourths[2])
+        third, fourth = fetch(1, 2, 0, T), fetch(1, 3, 0, T)
+        first, second, two, three = (sb([P, T], F32, name) for name in ("first", "second", "two", "three"))
+        nc.vector.tensor_tensor(first[:], fetched0[:], gates[0][:], MULT)
+        nc.vector.tensor_tensor(two[:], third[:], fourth[:], ADD)
+        nc.vector.tensor_tensor(second[:, halves[0]], fetched1[0][:], gates[1][:, halves[0]], MULT)
+        nc.vector.tensor_tensor(three[:], two[:], first[:], ADD)
+        nc.vector.tensor_tensor(second[:, halves[1]], fetched1[1][:], gates[1][:, halves[1]], MULT)
+        for a, half in enumerate(halves):
+            res1 = sb([P, T // 2], F32, f"res1_{a}")
+            nc.vector.tensor_tensor(res1[:], three[:, half], second[:, half], ADD)
+            nc.sync.dma_start(out[P:, half], res1[:])

@@ -23,24 +23,23 @@ SQUARE = mybir.ActivationFunctionType.Square
 COPY = mybir.ActivationFunctionType.Copy
 
 X_SCALAR = 80
-M_VECTOR = 120
+M_GPSIMD = 32
+N_SCALAR = 80
 
 KB = 1024
 BANK = 2 * KB
-SHIFT = 64
+EDGE = 64
 RAW = PACK * H * 4
-LAY_A, LAY_B, LAY_C = 64 * KB, 66 * KB, 68 * KB
-RELU_AT = 70 * KB
-H_LAST_AT = 78 * KB
-LATE_AT = 82 * KB
-Y1_AT = LATE_AT + 12 * KB - SHIFT
-LAY6_AT, LAY7_AT = 102 * KB, 104 * KB
-CODES7_AT = 108 * KB
-PICKED_AT = 111 * KB
-LAY_D = 113 * KB
-FIRST_AT = 115 * KB
-LAY5_AT = 123 * KB
-EARLY_AT = 124 * KB
+LAID = [64 * KB + 2 * KB * i for i in range(4)]
+FIRST_AT = 72 * KB
+RELU_AT = 80 * KB
+LATE_AT = 88 * KB
+Y1_AT = LATE_AT + 8 * KB - EDGE
+LAID5_AT = 104 * KB
+LAID7_AT = 108 * KB
+CODES7_AT = 112 * KB
+CODES_LAST_AT = 115 * KB
+GATED_AT = 118 * KB
 
 
 def tile_moe_tk_mlp_relu2_kernel(tc, xT, w1, w2, gate, offs, pos1, pos2, pos3, pos4, out):
@@ -52,298 +51,305 @@ def tile_moe_tk_mlp_relu2_kernel(tc, xT, w1, w2, gate, offs, pos1, pos2, pos3, p
         placed = ctx.enter_context(tc.tile_pool(name="placed", bufs=1))
         psum = ctx.enter_context(tc.psum_pool(name="psum", bufs=1))
 
-        def sb(shape, dtype, name, at=None):
+        def sb(shape, dtype, name, at=None, align=64):
             if at is None:
-                return keep.tile(shape, dtype, name=name, align_bytes=64)
-            return placed.tile(shape, dtype, name=name, align_bytes=64, offset=at)
+                return keep.tile(shape, dtype, name=name, align_bytes=align)
+            return placed.tile(shape, dtype, name=name, align_bytes=align, offset=at)
 
         def bank(shape, name, b):
             return psum.tile(shape, F32, name=name, offset=b * BANK)
 
-        xs = sb([P, 2 * T], U8, "xs")
-        nc.gpsimd.memset(xs[:].bitcast(I32), 0)
-        xw = sb([P, 2 * T], I32, "xw")
-        nc.vector.memset(xw[:, T:], 0)
-        ident = keep.tile([P, P], F32, name="ident")
+        x_scales = sb([P, 2 * T], U8, "x_scales")
+        nc.gpsimd.memset(x_scales[:].bitcast(I32), 0)
+        x_words = sb([P, 2 * T], I32, "x_words")
+        nc.vector.memset(x_words[:, T:], 0)
+        ident = sb([P, P], F32, "ident")
         make_identity(nc, ident[:])
 
-        x_rows = xT.rearrange("(p j) t -> p j t", j=PACK)
-        x_raw = []
-        for half in range(2):
-            raw = keep.tile([P, PACK, T // 2], F32, name=f"x_raw{half}", align_bytes=256)
-            nc.sync.dma_start(out=raw[:], in_=x_rows[:, :, half * T // 2 : (half + 1) * T // 2])
-            x_raw.append(raw)
-        offs_t = keep.tile([P, E * C // 16], U16, name="offs_t")
-        nc.sync.dma_start(offs_t[:], offs)
-        w2_raw = {}
+        def load(name, rows, at=None):
+            raw = sb(rows.shape, F32, name, at, 256)
+            nc.sync.dma_start(out=raw[:], in_=rows)
+            return raw
 
-        def load_whole(e0, e1, at=None):
-            raw = sb([P, e1 - e0, PACK, N], F32, f"w2_whole{e0}", at)
-            nc.sync.dma_start(out=raw[:], in_=w2[e0:e1].rearrange("i (p j) n -> p i j n", j=PACK))
-            for e in range(e0, e1):
+        def load_list(name, lst):
+            t = keep.tile(lst.shape, U16, name=name)
+            nc.sync.dma_start(t[:], lst)
+            return t
+
+        def by_word(matrix):
+            return matrix.rearrange("(p j) c -> p j c", j=PACK)
+
+        x_raw = [load(f"x_raw{a}", by_word(xT)[:, :, a * T // 2 : (a + 1) * T // 2]) for a in range(2)]
+        offs_t = load_list("offs_t", offs)
+        w1_raw = []
+        for e in range(E):
+            parts = 2 if e < 2 else 1
+            width = H // parts
+            w1_raw.append(
+                [load(f"w1_raw{e}_{i}", by_word(w1[e])[:, :, i * width : (i + 1) * width], e * RAW + i * RAW // parts) for i in range(parts)]
+            )
+        w2_raw = {}
+        for e0 in (0, 2):
+            raw = load(f"w2_whole{e0}", w2[e0 : e0 + 2].rearrange("e (p j) n -> p e j n", j=PACK))
+            for e in (e0, e0 + 1):
                 for h in range(2):
                     w2_raw[h, e] = raw[:, e - e0, :, h * P : (h + 1) * P]
 
-        def load_half(h, q):
-            raw = sb([P, 2, PACK, P], F32, f"w2_raw{h}_{q}", LATE_AT + (q - 1) * 4 * KB if h else None)
-            for e in (2 * q, 2 * q + 1):
-                rows = w2[e].rearrange("(p j) n -> p j n", j=PACK)
-                nc.sync.dma_start(out=raw[:, e % 2], in_=rows[:, :, h * P : (h + 1) * P])
-                w2_raw[h, e] = raw[:, e % 2]
+        def load_halves(h):
+            for e0 in (4, 6):
+                raw = sb([P, 2, PACK, P], F32, f"w2_raw{h}_{e0}", LATE_AT + (e0 - 4) * 2 * KB if h else None, 256)
+                for e in (e0, e0 + 1):
+                    nc.sync.dma_start(out=raw[:, e - e0], in_=by_word(w2[e])[:, :, h * P : (h + 1) * P])
+                    w2_raw[h, e] = raw[:, e - e0]
 
-        w1_raw = []
-        for e in range(E):
-            rows = w1[e].rearrange("(p j) c -> p j c", j=PACK)
-            parts = 2 if e < 2 else 1
-            raw = []
-            for i in range(parts):
-                at = e * RAW + i * RAW // parts
-                raw.append(placed.tile([P, PACK, H // parts], F32, name=f"w1_raw{e}_{i}", align_bytes=256, offset=at))
-                nc.sync.dma_start(out=raw[i][:], in_=rows[:, :, i * H // parts : (i + 1) * H // parts])
-            w1_raw.append(raw)
-            if e == 6:
-                load_whole(0, 1, EARLY_AT)
-                load_whole(1, 2)
-        load_whole(2, 4)
-        for q in (2, 3):
-            load_half(0, q)
+        load_halves(0)
         pos_t, gates = [], []
         for r in range(TOP):
-            lst = keep.tile([P, T // 16], U16, name=f"pos_t{r}")
-            nc.sync.dma_start(lst[:], pos[r])
-            pos_t.append(lst)
-            rows = keep.tile([P, T], F32, name=f"gate{r}", align_bytes=256)
-            nc.sync.dma_start(out=rows[:], in_=gate[r, :P, :])
-            gates.append(rows)
+            pos_t.append(load_list(f"pos_t{r}", pos[r]))
+            gates.append(load(f"gate{r}", gate[r, :P, :]))
             if r == 1:
-                for q in (2, 3):
-                    load_half(1, q)
+                load_halves(1)
 
         def interleave(copy, dst, src):
             copy(out=dst.rearrange("p (c i) j -> p c j i", i=2), in_=src.rearrange("p j (c i) -> p c j i", i=2))
 
-        xg = [sb([P, T // 2, PACK], BF16, f"xg{half}") for half in range(2)]
-        cut = T // 2 - X_SCALAR
-        interleave(nc.scalar.copy, xg[1][:, cut:], x_raw[1][:, :, cut:])
-        for half in range(2):
-            upto = cut if half else T // 2
-            interleave(nc.vector.tensor_copy, xg[half][:, :upto], x_raw[half][:, :, :upto])
-            cols = slice(half * T // 2, (half + 1) * T // 2)
-            nc.vector.quantize_mx(out=xw[:, cols].bitcast(FP8X4), scales=xs[:, cols], in_=xg[half][:].rearrange("p c j -> p (c j)"))
+        def quantise(codes, scales, values):
+            nc.vector.quantize_mx(out=codes.bitcast(FP8X4), scales=scales, in_=values)
 
-        laid, slot_words, slot_scales, banks, y_banks = {}, {}, {}, {}, {}
-        w2_laid, h_codes, h_scales, w2_codes, w2_scales = {}, {}, {}, {}, {}
-        h_bf = [sb([P, 2 * C * PACK], BF16, f"h_bf{q}", H_LAST_AT if q == 3 else None) for q in range(E // 2)]
-        y = [sb([P, E * C], F32, "y0", RAW), sb([P, E * C], F32, "y1", Y1_AT)]
+        x_laid = [sb([P, T // 2, PACK], BF16, f"x_laid{a}") for a in range(2)]
+        cut = T // 2 - X_SCALAR
+        interleave(nc.scalar.copy, x_laid[1][:, cut:], x_raw[1][:, :, cut:])
+        for a in range(2):
+            upto = cut if a else T // 2
+            interleave(nc.vector.tensor_copy, x_laid[a][:, :upto], x_raw[a][:, :, :upto])
+            cols = slice(a * T // 2, (a + 1) * T // 2)
+            quantise(x_words[:, cols], x_scales[:, cols], x_laid[a][:].rearrange("p c j -> p (c j)"))
+
+        slot_words, slot_scales = {}, {}
+
+        def gather_tokens(e0, at=None):
+            columns = offs_t[:, e0 * C // 16 : (e0 + 2) * C // 16]
+            words = sb([P, 2, C], U32, f"slot_words{e0}", at)
+            nc.vector.tensor_copy(words[:].rearrange("p e c -> p (e c)"), x_words[:].bitcast(U32).indirect(columns))
+            scales = sb([P, 2, C], U8, f"slot_scales{e0}", at and at + 2 * KB)
+            nc.vector.tensor_copy(scales[:].rearrange("p e c -> p (e c)"), x_scales[:].indirect(columns))
+            for e in (e0, e0 + 1):
+                slot_words[e], slot_scales[e] = words[:, e - e0], scales[:, e - e0]
+
+        def on_vector(dst, src):
+            nc.vector.tensor_copy(out=dst, in_=src)
+
+        def on_scalar(dst, src):
+            nc.scalar.copy(out=dst, in_=src)
 
         def on_gpsimd(dst, src):
             nc.gpsimd.tensor_scalar(dst.rearrange("p m j v -> p m v j"), src.rearrange("p m j v -> p m v j"), 1.0, 0.0, MULT, ADD)
 
-        def w1_layout(e):
-            if e < 2:
-                tiles = [sb([P, 2 * H], BF16, f"w1_laid{e}_{u}", FIRST_AT + (2 * e + u) * 2 * KB) for u in range(2)]
-                laid[e] = list(enumerate(tiles))
-                for i in range(2):
-                    src = w1_raw[e][i][:].rearrange("p j (m u v) -> p u m j v", u=2, v=2)
-                    for u in range(2):
-                        dst = tiles[u][:].rearrange("p (v m j) -> p m j v", v=2, j=PACK)[:, i * P // 2 : (i + 1) * P // 2]
-                        if u and (e, i) != (1, 0):
-                            on_gpsimd(dst, src[:, u])
-                        else:
-                            nc.scalar.copy(out=dst, in_=src[:, u])
-                return
-            src = w1_raw[e][0][:].rearrange("p j (m u v) -> p u m j v", u=2, v=2)
-            at = {2: (RAW + 4 * KB + SHIFT, LAY_C), 3: (LAY_A, LAY_B), 4: (LAY_C, LAY_A), 5: (LAY_A, LAY_D), 6: (LAY_C, LAY_A), 7: (LAY_A, LAY_D)}[e]
+        w1_laid, a_banks = {}, {}
+
+        def lay_w1(e, at, copies, shared=0):
             tiles = [sb([P, 2 * H], BF16, f"w1_laid{e}_{u}", at[u]) for u in range(2)]
-            dst = [g[:].rearrange("p (v m j) -> p m j v", v=2, j=PACK) for g in tiles]
-            laid[e] = list(enumerate(tiles))
-            if e in (4, 6):
-                on_gpsimd(dst[1], src[:, 1])
-                on_gpsimd(dst[0][:, M_VECTOR:], src[:, 0, M_VECTOR:])
-                nc.vector.tensor_copy(out=dst[0][:, :M_VECTOR], in_=src[:, 0, :M_VECTOR])
-                laid[e].reverse()
-            else:
+            parts = len(w1_raw[e])
+            for i, raw in enumerate(w1_raw[e]):
+                src = raw[:].rearrange("p j (m u v) -> p u m j v", u=2, v=2)
                 for u in range(2):
-                    nc.vector.tensor_copy(out=dst[u], in_=src[:, u])
-
-        def gather(window, dtype, into, e0, e1, name, at=None):
-            g = sb([P, (e1 - e0) * C], dtype, f"{name}{e0}", at)
-            nc.vector.tensor_copy(g[:], window.indirect(offs_t[:, e0 * C // 16 : e1 * C // 16]))
-            for e in range(e0, e1):
-                into[e] = g[:, (e - e0) * C : (e - e0 + 1) * C]
-
-        def gather_words(e0, e1, at=None):
-            gather(xw[:].bitcast(U32), U32, slot_words, e0, e1, "slot_words", at)
-
-        def gather_scales(e0, e1, at=None):
-            gather(xs[:], U8, slot_scales, e0, e1, "slot_scales", at)
+                    dst = tiles[u][:].rearrange("p (v m j) -> p m j v", v=2, j=PACK)
+                    dst = dst[:, i * P // parts : (i + 1) * P // parts]
+                    if u and shared:
+                        on_gpsimd(dst[:, :shared], src[:, u, :shared])
+                    copies[2 * i + u](dst[:, shared * u :], src[:, u, shared * u :])
+            w1_laid[e] = tiles
 
         def first_product(e):
-            wc = stage.tile([P, H], U32, name="w1_codes", align_bytes=64)
-            ws = stage.tile([P, H], U8, name="w1_scales", align_bytes=64)
-            width = H // len(laid[e])
-            for u, g in laid[e]:
-                cols = slice(u * width, (u + 1) * width)
-                nc.vector.quantize_mx(out=wc[:, cols].bitcast(FP8X4), scales=ws[:, cols], in_=g[:])
-            banks[e] = []
+            codes = stage.tile([P, H], U32, name="w1_codes", align_bytes=64)
+            scales = stage.tile([P, H], U8, name="w1_scales", align_bytes=64)
+            for u in range(2):
+                cols = slice(u * 2 * P, (u + 1) * 2 * P)
+                quantise(codes[:, cols], scales[:, cols], w1_laid[e][u][:])
+            a_banks[e] = [bank([P, PACK, P], f"a{e}_{s}", (2 * e + s) % 8) for s in range(2)]
             for s in range(2):
-                ps = bank([P, PACK, P], f"a{e}_{s}", (2 * e + s) % 8)
                 slots = slice(s * P, (s + 1) * P)
-                for t in [u * width // P + v for u, g in laid[e] for v in range(width // P)]:
+                for t in range(PACK):
                     cols = slice(t * P, (t + 1) * P)
                     nc.tensor.matmul_mx(
-                        out=ps[:, t, :], lhsT=wc[:, cols].bitcast(FP8X4), lhsT_scale=ws[:, cols],
+                        out=a_banks[e][s][:, t, :], lhsT=codes[:, cols].bitcast(FP8X4), lhsT_scale=scales[:, cols],
                         rhs=slot_words[e][:, slots].bitcast(FP8X4), rhs_scale=slot_scales[e][:, slots],
                         start=True, stop=True,
                     )
-                banks[e].append(ps)
 
-        def squared_relu(e):
-            relu = sb([P, C, PACK], F32, f"relu{e}", {0: RAW + SHIFT, 6: EARLY_AT}.get(e, RELU_AT + (e % 2) * 4 * KB))
+        h_laid = [sb([P, 2, C * PACK], BF16, f"h_laid{q}") for q in range(E // 2)]
+
+        def squared_relu(e, at=None):
+            relu = sb([P, 2, P, PACK], F32, f"relu{e}", at or RELU_AT + (e % 2) * 4 * KB)
             for s in range(2):
-                nc.scalar.activation(relu[:, s * P : (s + 1) * P, :], banks[e][s][:].rearrange("p t n -> p n t"), RELU)
+                nc.scalar.activation(relu[:, s], a_banks[e][s][:].rearrange("p t n -> p n t"), RELU)
             for s in range(2):
-                first = ((e % 2) * C + s * P) * PACK
                 nc.scalar.activation(
-                    h_bf[e // 2][:, first : first + P * PACK], relu[:, s * P : (s + 1) * P, :].rearrange("p n t -> p (n t)"), SQUARE
+                    h_laid[e // 2][:, e % 2, s * P * PACK : (s + 1) * P * PACK], relu[:, s].rearrange("p n t -> p (n t)"), SQUARE
                 )
+
+        gather_tokens(0)
+        lay_w1(0, (FIRST_AT, FIRST_AT + 2 * KB), (on_scalar, on_gpsimd, on_scalar, on_gpsimd))
+        first_product(0)
+        gather_tokens(2, RAW // 2)
+        lay_w1(1, (FIRST_AT + 4 * KB, FIRST_AT + 6 * KB), (on_scalar, on_scalar, on_scalar, on_gpsimd))
+        squared_relu(0, RAW + EDGE)
+        first_product(1)
+        lay_w1(2, (RAW + 4 * KB + EDGE, LAID[2]), (on_vector, on_vector))
+        squared_relu(1)
+        first_product(2)
+        lay_w1(3, LAID[:2], (on_vector, on_vector))
+        squared_relu(2)
+        first_product(3)
+        gather_tokens(4, 3 * RAW)
+        gather_tokens(6, 3 * RAW + 3 * KB)
+        lay_w1(4, LAID[:2], (on_gpsimd, on_gpsimd))
+        squared_relu(3)
+        lay_w1(5, (LAID[2], 3 * RAW + 6 * KB), (on_scalar, on_scalar), M_GPSIMD)
+        first_product(4)
+        first_product(5)
+        squared_relu(4, 5 * RAW)
+        for e in (6, 7):
+            lay_w1(e, LAID[2 * (e % 2) :], (on_vector, on_vector))
+            first_product(e)
+            squared_relu(e - 1)
+        squared_relu(7)
+
+        w2_laid, w2_codes, w2_scales, h_codes, h_scales, y_banks = {}, {}, {}, {}, {}, {}
+        y = [sb([P, E * C], F32, "y0", RAW), sb([P, E * C], F32, "y1", Y1_AT)]
 
         def quantise_h(e0, e1, at):
-            hc = sb([P, (e1 - e0) * C], U32, f"h_codes{e0}", at)
-            hs = sb([P, (e1 - e0) * C], U8, f"h_scales{e0}")
-            first = (e0 % 2) * C * PACK
-            nc.vector.quantize_mx(
-                out=hc[:].bitcast(FP8X4), scales=hs[:], in_=h_bf[e0 // 2][:, first : first + (e1 - e0) * C * PACK]
-            )
+            codes = sb([P, e1 - e0, C], U32, f"h_codes{e0}", at)
+            scales = sb([P, e1 - e0, C], U8, f"h_scales{e0}")
+            values = h_laid[e0 // 2][:, e0 % 2 : e0 % 2 + e1 - e0].rearrange("p e c -> p (e c)")
+            quantise(codes[:].rearrange("p e c -> p (e c)"), scales[:].rearrange("p e c -> p (e c)"), values)
             for e in range(e0, e1):
-                h_codes[e], h_scales[e] = hc[:, (e - e0) * C : (e - e0 + 1) * C], hs[:, (e - e0) * C : (e - e0 + 1) * C]
+                h_codes[e], h_scales[e] = codes[:, e - e0], scales[:, e - e0]
 
-        def w2_layout(copy, h, e0, e1, at=None):
-            g = sb([P, e1 - e0, P, PACK], BF16, f"w2_laid{h}_{e0}", at)
-            w2_laid[h, e0] = g
+        def lay_w2(copy, h, e0, e1, at=None, shared=0):
+            w2_laid[h, e0] = sb([P, e1 - e0, P, PACK], BF16, f"w2_laid{h}_{e0}", at)
+            if shared:
+                interleave(nc.scalar.copy, w2_laid[h, e0][:, 0, :shared], w2_raw[h, e0][:, :, :shared])
             for e in range(e0, e1):
-                interleave(copy, g[:, e - e0], w2_raw[h, e])
+                first = shared if e == e0 else 0
+                interleave(copy, w2_laid[h, e0][:, e - e0, first:], w2_raw[h, e][:, :, first:])
 
-        def quantise_w2(h, e0, e1, at=None):
-            wc = sb([P, (e1 - e0) * P], U32, f"w2_codes{h}_{e0}", at)
-            ws = sb([P, (e1 - e0) * P], U8, f"w2_scales{h}_{e0}")
-            nc.vector.quantize_mx(
-                out=wc[:].bitcast(FP8X4), scales=ws[:], in_=w2_laid[h, e0][:].rearrange("p i c j -> p (i c j)")
-            )
+        def quantise_w2(h, e0, e1, at=None, scales_at=None):
+            codes = sb([P, e1 - e0, P], U32, f"w2_codes{h}_{e0}", at)
+            scales = sb([P, e1 - e0, P], U8, f"w2_scales{h}_{e0}", scales_at)
+            values = w2_laid[h, e0][:].rearrange("p e c j -> p (e c j)")
+            quantise(codes[:].rearrange("p e c -> p (e c)"), scales[:].rearrange("p e c -> p (e c)"), values)
             for e in range(e0, e1):
-                w2_codes[h, e], w2_scales[h, e] = wc[:, (e - e0) * P : (e - e0 + 1) * P], ws[:, (e - e0) * P : (e - e0 + 1) * P]
+                w2_codes[h, e], w2_scales[h, e] = codes[:, e - e0], scales[:, e - e0]
 
         def second_product(h, e0, e1, b):
-            ps = bank([P, e1 - e0, C], f"y{h}_{e0}", b)
+            y_banks[h, e0] = bank([P, e1 - e0, C], f"y{h}_{e0}", b)
             for e in range(e0, e1):
                 nc.tensor.matmul_mx(
-                    out=ps[:, e - e0, :], lhsT=w2_codes[h, e].bitcast(FP8X4), lhsT_scale=w2_scales[h, e],
+                    out=y_banks[h, e0][:, e - e0], lhsT=w2_codes[h, e].bitcast(FP8X4), lhsT_scale=w2_scales[h, e],
                     rhs=h_codes[e].bitcast(FP8X4), rhs_scale=h_scales[e], start=True, stop=True,
                 )
-            y_banks[h, e0] = ps
 
-        def y_copy(h, e0, e1):
-            nc.scalar.copy(out=y[h][:, e0 * C : e1 * C], in_=y_banks[h, e0][:].rearrange("p i c -> p (i c)"))
+        def copy_y(h, e0, e1):
+            nc.scalar.copy(out=y[h][:, e0 * C : e1 * C], in_=y_banks[h, e0][:].rearrange("p e c -> p (e c)"))
 
-        def fetch(h, r, t0, t1, at=None):
-            prod = sb([P, t1 - t0], F32, f"prod{h}_{r}_{t0}", at)
-            nc.vector.tensor_tensor(prod[:], y[h][:].indirect(pos_t[r][:, t0 // 16 : t1 // 16]), gates[r][:, t0:t1], MULT)
-            return prod
-
-        def turn(dst, src, first, last):
-            nc.tensor.matmul(dst, lhsT=src, rhs=ident[:], is_transpose=True, start=first, stop=last)
-
-        def turn_back(acc, name, b, at=None):
-            turned = sb([P, len(acc), P], F32, name, at)
-            back = bank([P, len(acc), P], f"back_{name}", b)
-            for c in range(len(acc)):
-                nc.scalar.copy(out=turned[:, c, :], in_=acc[c][:])
-                turn(back[:, c, :], turned[:, c, :], True, True)
-            return back[:].rearrange("p c t -> p (c t)")
-
-        def add_turned(acc, prod, first, last):
-            for c in range(len(acc)):
-                turn(acc[c][:], prod[:, c * P : (c + 1) * P], first, last)
-
-        gather_words(0, 2)
-        gather_scales(0, 2)
-        w1_layout(0)
-        first_product(0)
-        gather_words(2, 4, 4 * KB)
-        gather_scales(2, 4, 6 * KB)
-        w1_layout(1)
-        for e in range(E):
-            squared_relu(e)
-            if e + 1 < E:
-                first_product(e + 1)
-            if e in (2, 4):
-                gather_words(e + 2, e + 4, (e + 1) * RAW)
-                gather_scales(e + 2, e + 4, (e + 1) * RAW + 2 * KB)
-            if e == 5:
-                w2_layout(nc.scalar.copy, 1, 0, 1)
-                w2_layout(nc.scalar.copy, 0, 0, 2)
-            if e + 2 < E:
-                w1_layout(e + 2)
-
-        at7 = 7 * RAW
-        w2_last_at = PICKED_AT
-        quantise_h(0, 2, at7 - 2 * KB + SHIFT)
-        quantise_h(2, 4, at7 + SHIFT)
-        w2_layout(nc.vector.tensor_copy, 0, 2, 4)
-        w2_layout(nc.vector.tensor_copy, 1, 1, 2, at7 + 6 * KB)
-        quantise_w2(0, 0, 2, at7 + 3 * KB)
+        raw7 = 7 * RAW
+        quantise_h(0, 2, raw7 - 2 * KB + EDGE)
+        quantise_h(2, 4, raw7 + EDGE)
+        lay_w2(nc.vector.tensor_copy, 0, 0, 2)
+        lay_w2(nc.vector.tensor_copy, 0, 2, 4)
+        lay_w2(nc.vector.tensor_copy, 1, 0, 2, None, N_SCALAR)
+        quantise_w2(0, 0, 2)
         quantise_w2(0, 2, 4)
-        quantise_h(4, 6, at7 + 4 * KB)
-        for q in (2, 3):
-            for e in (2 * q, 2 * q + 1):
-                w2_layout(nc.vector.tensor_copy, 0, e, e + 1, {5: LAY5_AT, 7: LAY7_AT}.get(e))
-            for e in (2 * q, 2 * q + 1):
-                quantise_w2(0, e, e + 1, CODES7_AT if e == 7 else None)
-            quantise_h(q + 4, q + 5, LAY5_AT if q == 2 else LAY7_AT + KB - SHIFT)
+        quantise_h(4, 6, raw7 + 4 * KB)
+        for e0, at in ((4, LAID5_AT), (6, LAID7_AT)):
+            lay_w2(nc.vector.tensor_copy, 0, e0, e0 + 1)
+            lay_w2(nc.vector.tensor_copy, 0, e0 + 1, e0 + 2, at)
+            quantise_w2(0, e0, e0 + 1)
+            quantise_w2(0, e0 + 1, e0 + 2, CODES7_AT if e0 == 6 else None)
+            quantise_h(e0 // 2 + 4, e0 // 2 + 5, at if e0 == 4 else at + KB - EDGE)
         groups = ((0, 2, 6), (2, 4, 7), (4, 6, 4), (6, 7, 5), (7, 8, 0))
         for e0, e1, b in groups:
             second_product(0, e0, e1, b)
         for e0, e1, b in groups:
-            y_copy(0, e0, e1)
+            copy_y(0, e0, e1)
 
-        w2_layout(nc.vector.tensor_copy, 1, 2, 4, LAY7_AT - 2 * KB + SHIFT)
-        quantise_w2(1, 0, 1, LAY7_AT + SHIFT)
-        quantise_w2(1, 1, 2)
+        lay_w2(nc.vector.tensor_copy, 1, 2, 4, LAID7_AT - 2 * KB + EDGE)
+        quantise_w2(1, 0, 2, None, LAID7_AT + EDGE)
         quantise_w2(1, 2, 4)
-        for e0, e1, at in ((4, 6, CODES7_AT - 2 * KB + SHIFT), (6, 8, CODES7_AT + SHIFT)):
-            w2_layout(nc.scalar.copy, 1, e0, e1, at)
-            quantise_w2(1, e0, e1, w2_last_at if e0 == 6 else None)
+        for e0, at in ((4, CODES7_AT - 2 * KB + EDGE), (6, CODES7_AT + EDGE)):
+            lay_w2(nc.scalar.copy, 1, e0, e0 + 2, at)
+            quantise_w2(1, e0, e0 + 2, CODES_LAST_AT if e0 == 6 else None)
         for q, b in enumerate((2, 3, 0, 1)):
             second_product(1, 2 * q, 2 * q + 2, b)
         for q in range(E // 2):
-            y_copy(1, 2 * q, 2 * q + 2)
+            copy_y(1, 2 * q, 2 * q + 2)
 
-        acc = [bank([P, P], f"acc{c}", 4 + c) for c in range(T // P)]
-        for r in range(TOP):
-            prod = fetch(0, r, 0, T, (None, LATE_AT + 4 * KB, LATE_AT + 7 * KB, LATE_AT + 9 * KB)[r])
-            add_turned(acc, prod, r == 0, r == TOP - 1)
+        def picked(h, r, t0, t1):
+            return y[h][:].indirect(pos_t[r][:, t0 // 16 : t1 // 16])
 
-        def fetch_plain(r, t0, t1):
-            values = sb([P, t1 - t0], F32, f"fetched{r}_{t0}")
-            nc.scalar.activation(values[:], y[1][:].indirect(pos_t[r][:, t0 // 16 : t1 // 16]), COPY)
+        def combine(name, in0, in1, op, at=None):
+            res = sb(in1.shape, F32, name, at)
+            nc.vector.tensor_tensor(res[:], in0, in1, op)
+            return res
+
+        def fetch_gated(h, r, t0, t1, at=None):
+            return combine(f"product{h}_{r}_{t0}", picked(h, r, t0, t1), gates[r][:, t0:t1], MULT, at)
+
+        def fetch_plain(r, t0, t1, at=None):
+            values = sb([P, t1 - t0], F32, f"fetched{r}_{t0}", at)
+            nc.scalar.activation(values[:], picked(1, r, t0, t1), COPY)
             return values
 
-        halves = (slice(0, T // 2), slice(T // 2, T))
-        fetched0 = fetch_plain(0, 0, T)
-        back0 = turn_back(acc, "turned0", 4, w2_last_at)
-        fetched1 = [fetch_plain(1, half.start, half.stop) for half in halves]
-        res0 = sb([P, T], F32, "res0")
-        nc.scalar.copy(out=res0[:], in_=back0)
-        nc.sync.dma_start(out[:P, :], res0[:])
+        def add_turned(acc, term, first, last, c0=0):
+            blocks = term.shape[1] // P
+            for c in range(blocks):
+                nc.tensor.matmul(
+                    acc[:, c0 + c], lhsT=term[:, c * P : (c + 1) * P], rhs=ident[:], is_transpose=True,
+                    start=first and c == 0, stop=last and c == blocks - 1,
+                )
 
-        third, fourth = fetch(1, 2, 0, T), fetch(1, 3, 0, T)
-        first, second, two, three = (sb([P, T], F32, name) for name in ("first", "second", "two", "three"))
-        nc.vector.tensor_tensor(first[:], fetched0[:], gates[0][:], MULT)
-        nc.vector.tensor_tensor(two[:], third[:], fourth[:], ADD)
-        nc.vector.tensor_tensor(second[:, halves[0]], fetched1[0][:], gates[1][:, halves[0]], MULT)
-        nc.vector.tensor_tensor(three[:], two[:], first[:], ADD)
-        nc.vector.tensor_tensor(second[:, halves[1]], fetched1[1][:], gates[1][:, halves[1]], MULT)
-        for a, half in enumerate(halves):
-            res1 = sb([P, T // 2], F32, f"res1_{a}")
-            nc.vector.tensor_tensor(res1[:], three[:, half], second[:, half], ADD)
-            nc.sync.dma_start(out[P:, half], res1[:])
+        def copy_out(name, acc, at=None):
+            res = sb([P, acc.shape[1] * P], F32, name, at)
+            nc.scalar.copy(out=res[:], in_=acc[:].rearrange("p c n -> p (c n)"))
+            return res
+
+        def turn_back(name, turned, b):
+            back = bank([P, turned.shape[1] // P, P], name, b)
+            add_turned(back, turned, True, True)
+            return back[:].rearrange("p c t -> p (c t)")
+
+        half = T // 2
+        sum0 = bank([P, T // P, P], "sum0", 5)
+        add_turned(sum0, fetch_gated(0, 0, 0, T), True, False)
+        add_turned(sum0, fetch_gated(0, 1, 0, half), False, False)
+        add_turned(sum0, fetch_gated(0, 1, half, T, LATE_AT), False, False, 2)
+        add_turned(sum0, fetch_gated(0, 2, 0, T, LATE_AT + 3 * KB), False, False)
+        add_turned(sum0, fetch_gated(0, 3, 0, T, LATE_AT + 5 * KB), False, True)
+
+        early, late = slice(0, half), slice(half, T)
+        first = [fetch_plain(0, 0, half), fetch_plain(0, half, T)]
+        turned0 = copy_out("turned0", sum0, CODES_LAST_AT)
+        second_late = fetch_plain(1, half, T)
+        sum1 = bank([P, 2, P], "sum1", 2)
+        add_turned(sum1, fetch_gated(1, 2, 0, half), True, False)
+        add_turned(sum1, fetch_gated(1, 3, 0, half), False, False)
+        add_turned(sum1, combine("first_early", first[0][:], gates[0][:, early], MULT, GATED_AT), False, True)
+        back0 = turn_back("back0", turned0, 4)
+        back1 = turn_back("back1", copy_out("turned1", sum1), 0)
+        second_early = fetch_plain(1, 0, half, GATED_AT - KB + EDGE)
+        out0 = sb([P, T], F32, "out0", GATED_AT + KB // 2)
+        for cols in (early, late):
+            nc.scalar.copy(out=out0[:, cols], in_=back0[:, cols])
+            nc.sync.dma_start(out[:P, cols], out0[:, cols])
+
+        third, fourth = fetch_gated(1, 2, half, T), fetch_gated(1, 3, half, T)
+        first_late = combine("first_late", first[1][:], gates[0][:, late], MULT)
+        two = combine("two", third[:], fourth[:], ADD)
+        second_late = combine("second_late", second_late[:], gates[1][:, late], MULT)
+        three = combine("three", two[:], first_late[:], ADD)
+        second_early = combine("second_early", second_early[:], gates[1][:, early], MULT)
+        nc.sync.dma_start(out[P:, late], combine("out_late", three[:], second_late[:], ADD)[:])
+        for c in range(2):
+            cols = slice(c * P, (c + 1) * P)
+            nc.sync.dma_start(out[P:, cols], combine(f"out_early{c}", back1[:, cols], second_early[:, cols], ADD)[:])

@@ -23,23 +23,22 @@ SQUARE = mybir.ActivationFunctionType.Square
 COPY = mybir.ActivationFunctionType.Copy
 
 X_SCALAR = 80
-M_GPSIMD = 32
-N_SCALAR = 80
 
 KB = 1024
 BANK = 2 * KB
 EDGE = 64
 RAW = PACK * H * 4
-LAID = [64 * KB + 2 * KB * i for i in range(4)]
-FIRST_AT = 72 * KB
-RELU_AT = 80 * KB
-LATE_AT = 88 * KB
+ODD_AT = (64 * KB, 66 * KB)
+FIRST_AT = 68 * KB
+EVEN_AT = (FIRST_AT + 2 * KB + EDGE, FIRST_AT + 6 * KB + EDGE)
+RELU_AT = 77 * KB
+LATE_AT = 85 * KB
 Y1_AT = LATE_AT + 8 * KB - EDGE
-LAID5_AT = 104 * KB
-LAID7_AT = 108 * KB
-CODES7_AT = 112 * KB
-CODES_LAST_AT = 115 * KB
-GATED_AT = 118 * KB
+LAID5_AT = 101 * KB
+LAID7_AT = 105 * KB
+CODES7_AT = 109 * KB
+CODES_LAST_AT = 112 * KB
+GATED_AT = 115 * KB
 
 
 def tile_moe_tk_mlp_relu2_kernel(tc, xT, w1, w2, gate, offs, pos1, pos2, pos3, pos4, out):
@@ -91,16 +90,15 @@ def tile_moe_tk_mlp_relu2_kernel(tc, xT, w1, w2, gate, offs, pos1, pos2, pos3, p
         w2_raw = {}
         for e0 in (0, 2):
             raw = load(f"w2_whole{e0}", w2[e0 : e0 + 2].rearrange("e (p j) n -> p e j n", j=PACK))
-            for e in (e0, e0 + 1):
-                for h in range(2):
-                    w2_raw[h, e] = raw[:, e - e0, :, h * P : (h + 1) * P]
+            for h in range(2):
+                w2_raw[h, e0] = raw[:, :, :, h * P : (h + 1) * P]
 
         def load_halves(h):
             for e0 in (4, 6):
                 raw = sb([P, 2, PACK, P], F32, f"w2_raw{h}_{e0}", LATE_AT + (e0 - 4) * 2 * KB if h else None, 256)
                 for e in (e0, e0 + 1):
                     nc.sync.dma_start(out=raw[:, e - e0], in_=by_word(w2[e])[:, :, h * P : (h + 1) * P])
-                    w2_raw[h, e] = raw[:, e - e0]
+                w2_raw[h, e0] = raw[:]
 
         load_halves(0)
         pos_t, gates = [], []
@@ -118,23 +116,33 @@ def tile_moe_tk_mlp_relu2_kernel(tc, xT, w1, w2, gate, offs, pos1, pos2, pos3, p
 
         x_laid = [sb([P, T // 2, PACK], BF16, f"x_laid{a}") for a in range(2)]
         cut = T // 2 - X_SCALAR
-        interleave(nc.scalar.copy, x_laid[1][:, cut:], x_raw[1][:, :, cut:])
+
+        def quantise_x(a, t0, t1):
+            cols = slice(a * T // 2 + t0, a * T // 2 + t1)
+            quantise(x_words[:, cols], x_scales[:, cols], x_laid[a][:, t0:t1].rearrange("p c j -> p (c j)"))
+
         for a in range(2):
-            upto = cut if a else T // 2
-            interleave(nc.vector.tensor_copy, x_laid[a][:, :upto], x_raw[a][:, :, :upto])
-            cols = slice(a * T // 2, (a + 1) * T // 2)
-            quantise(x_words[:, cols], x_scales[:, cols], x_laid[a][:].rearrange("p c j -> p (c j)"))
+            interleave(nc.scalar.copy, x_laid[a][:, cut:], x_raw[a][:, :, cut:])
+        interleave(nc.vector.tensor_copy, x_laid[0][:, :cut], x_raw[0][:, :, :cut])
+        quantise_x(0, 0, T // 2)
+        interleave(nc.vector.tensor_copy, x_laid[1][:, :P], x_raw[1][:, :, :P])
+        interleave(nc.vector.tensor_copy, x_laid[1][:, P:cut], x_raw[1][:, :, P:cut])
+        quantise_x(1, 0, P)
+        quantise_x(1, P, T // 2)
 
         slot_words, slot_scales = {}, {}
 
-        def gather_tokens(e0, at=None):
-            columns = offs_t[:, e0 * C // 16 : (e0 + 2) * C // 16]
-            words = sb([P, 2, C], U32, f"slot_words{e0}", at)
-            nc.vector.tensor_copy(words[:].rearrange("p e c -> p (e c)"), x_words[:].bitcast(U32).indirect(columns))
-            scales = sb([P, 2, C], U8, f"slot_scales{e0}", at and at + 2 * KB)
-            nc.vector.tensor_copy(scales[:].rearrange("p e c -> p (e c)"), x_scales[:].indirect(columns))
-            for e in (e0, e0 + 1):
-                slot_words[e], slot_scales[e] = words[:, e - e0], scales[:, e - e0]
+        def gather(name, window, dtype, into, e0, e1, at=None):
+            picked = sb([P, e1 - e0, C], dtype, f"{name}{e0}", at)
+            nc.vector.tensor_copy(picked[:].rearrange("p e c -> p (e c)"), window.indirect(offs_t[:, e0 * C // 16 : e1 * C // 16]))
+            for e in range(e0, e1):
+                into[e] = picked[:, e - e0]
+
+        def gather_words(e0, e1, at=None):
+            gather("slot_words", x_words[:].bitcast(U32), U32, slot_words, e0, e1, at)
+
+        def gather_scales(e0, e1, at=None):
+            gather("slot_scales", x_scales[:], U8, slot_scales, e0, e1, at)
 
         def on_vector(dst, src):
             nc.vector.tensor_copy(out=dst, in_=src)
@@ -147,17 +155,14 @@ def tile_moe_tk_mlp_relu2_kernel(tc, xT, w1, w2, gate, offs, pos1, pos2, pos3, p
 
         w1_laid, a_banks = {}, {}
 
-        def lay_w1(e, at, copies, shared=0):
+        def lay_w1(e, at, copies):
             tiles = [sb([P, 2 * H], BF16, f"w1_laid{e}_{u}", at[u]) for u in range(2)]
             parts = len(w1_raw[e])
             for i, raw in enumerate(w1_raw[e]):
                 src = raw[:].rearrange("p j (m u v) -> p u m j v", u=2, v=2)
                 for u in range(2):
                     dst = tiles[u][:].rearrange("p (v m j) -> p m j v", v=2, j=PACK)
-                    dst = dst[:, i * P // parts : (i + 1) * P // parts]
-                    if u and shared:
-                        on_gpsimd(dst[:, :shared], src[:, u, :shared])
-                    copies[2 * i + u](dst[:, shared * u :], src[:, u, shared * u :])
+                    copies[2 * i + u](dst[:, i * P // parts : (i + 1) * P // parts], src[:, u])
             w1_laid[e] = tiles
 
         def first_product(e):
@@ -183,37 +188,36 @@ def tile_moe_tk_mlp_relu2_kernel(tc, xT, w1, w2, gate, offs, pos1, pos2, pos3, p
             relu = sb([P, 2, P, PACK], F32, f"relu{e}", at or RELU_AT + (e % 2) * 4 * KB)
             for s in range(2):
                 nc.scalar.activation(relu[:, s], a_banks[e][s][:].rearrange("p t n -> p n t"), RELU)
-            for s in range(2):
-                nc.scalar.activation(
-                    h_laid[e // 2][:, e % 2, s * P * PACK : (s + 1) * P * PACK], relu[:, s].rearrange("p n t -> p (n t)"), SQUARE
-                )
+            pieces = 2
+            values = relu[:].rearrange("p s n t -> p (s n t)")
+            for i in range(pieces):
+                cols = slice(i * C * PACK // pieces, (i + 1) * C * PACK // pieces)
+                nc.scalar.activation(h_laid[e // 2][:, e % 2, cols], values[:, cols], SQUARE)
 
-        gather_tokens(0)
+        gather_words(0, 2)
+        gather_scales(0, 2)
         lay_w1(0, (FIRST_AT, FIRST_AT + 2 * KB), (on_scalar, on_gpsimd, on_scalar, on_gpsimd))
         first_product(0)
-        gather_tokens(2, RAW // 2)
+        gather_words(2, 4, RAW // 2)
+        gather_scales(2, 4, RAW // 2 + 2 * KB)
         lay_w1(1, (FIRST_AT + 4 * KB, FIRST_AT + 6 * KB), (on_scalar, on_scalar, on_scalar, on_gpsimd))
-        squared_relu(0, RAW + EDGE)
+        squared_relu(0, RAW)
         first_product(1)
-        lay_w1(2, (RAW + 4 * KB + EDGE, LAID[2]), (on_vector, on_vector))
+        gather_words(4, 6, RAW + 4 * KB + EDGE)
+        gather_scales(4, 7, RAW + 6 * KB + EDGE)
+        gather_words(6, 8, FIRST_AT + 4 * KB + EDGE)
+        lay_w1(2, EVEN_AT, (on_gpsimd, on_gpsimd))
         squared_relu(1)
+        lay_w1(3, ODD_AT, (on_scalar, on_scalar))
         first_product(2)
-        lay_w1(3, LAID[:2], (on_vector, on_vector))
-        squared_relu(2)
+        gather_scales(7, 8, 2 * RAW)
         first_product(3)
-        gather_tokens(4, 3 * RAW)
-        gather_tokens(6, 3 * RAW + 3 * KB)
-        lay_w1(4, LAID[:2], (on_gpsimd, on_gpsimd))
-        squared_relu(3)
-        lay_w1(5, (LAID[2], 3 * RAW + 6 * KB), (on_scalar, on_scalar), M_GPSIMD)
-        first_product(4)
-        first_product(5)
-        squared_relu(4, 5 * RAW)
-        for e in (6, 7):
-            lay_w1(e, LAID[2 * (e % 2) :], (on_vector, on_vector))
+        squared_relu(2, 3 * RAW)
+        for e in range(4, E):
+            lay_w1(e, ODD_AT if e % 2 else EVEN_AT, (on_vector, on_vector))
             first_product(e)
             squared_relu(e - 1)
-        squared_relu(7)
+        squared_relu(E - 1)
 
         w2_laid, w2_codes, w2_scales, h_codes, h_scales, y_banks = {}, {}, {}, {}, {}, {}
         y = [sb([P, E * C], F32, "y0", RAW), sb([P, E * C], F32, "y1", Y1_AT)]
@@ -226,13 +230,11 @@ def tile_moe_tk_mlp_relu2_kernel(tc, xT, w1, w2, gate, offs, pos1, pos2, pos3, p
             for e in range(e0, e1):
                 h_codes[e], h_scales[e] = codes[:, e - e0], scales[:, e - e0]
 
-        def lay_w2(copy, h, e0, e1, at=None, shared=0):
+        def lay_w2(copy, h, e0, e1, at=None):
             w2_laid[h, e0] = sb([P, e1 - e0, P, PACK], BF16, f"w2_laid{h}_{e0}", at)
-            if shared:
-                interleave(nc.scalar.copy, w2_laid[h, e0][:, 0, :shared], w2_raw[h, e0][:, :, :shared])
-            for e in range(e0, e1):
-                first = shared if e == e0 else 0
-                interleave(copy, w2_laid[h, e0][:, e - e0, first:], w2_raw[h, e][:, :, first:])
+            dst = w2_laid[h, e0][:].rearrange("p e (c i) j -> p e c j i", i=2)
+            pair = w2_raw[h, e0 - e0 % 2][:, e0 % 2 : e0 % 2 + e1 - e0]
+            copy(out=dst, in_=pair.rearrange("p e j (c i) -> p e c j i", i=2))
 
         def quantise_w2(h, e0, e1, at=None, scales_at=None):
             codes = sb([P, e1 - e0, P], U32, f"w2_codes{h}_{e0}", at)
@@ -258,7 +260,7 @@ def tile_moe_tk_mlp_relu2_kernel(tc, xT, w1, w2, gate, offs, pos1, pos2, pos3, p
         quantise_h(2, 4, raw7 + EDGE)
         lay_w2(nc.vector.tensor_copy, 0, 0, 2)
         lay_w2(nc.vector.tensor_copy, 0, 2, 4)
-        lay_w2(nc.vector.tensor_copy, 1, 0, 2, None, N_SCALAR)
+        lay_w2(nc.vector.tensor_copy, 1, 0, 2)
         quantise_w2(0, 0, 2)
         quantise_w2(0, 2, 4)
         quantise_h(4, 6, raw7 + 4 * KB)

@@ -39,6 +39,7 @@ LAID7_AT = 105 * KB
 CODES7_AT = 109 * KB
 CODES_LAST_AT = 112 * KB
 GATED_AT = 115 * KB
+WHOLE_AT = 118 * KB
 
 
 def tile_moe_tk_mlp_relu2_kernel(tc, xT, w1, w2, gate, offs, pos1, pos2, pos3, pos4, out):
@@ -89,7 +90,7 @@ def tile_moe_tk_mlp_relu2_kernel(tc, xT, w1, w2, gate, offs, pos1, pos2, pos3, p
             )
         w2_raw = {}
         for e0 in (0, 2):
-            raw = load(f"w2_whole{e0}", w2[e0 : e0 + 2].rearrange("e (p j) n -> p e j n", j=PACK))
+            raw = load(f"w2_whole{e0}", w2[e0 : e0 + 2].rearrange("e (p j) n -> p e j n", j=PACK), None if e0 else WHOLE_AT)
             for h in range(2):
                 w2_raw[h, e0] = raw[:, :, :, h * P : (h + 1) * P]
 
@@ -194,6 +195,16 @@ def tile_moe_tk_mlp_relu2_kernel(tc, xT, w1, w2, gate, offs, pos1, pos2, pos3, p
                 cols = slice(i * C * PACK // pieces, (i + 1) * C * PACK // pieces)
                 nc.scalar.activation(h_laid[e // 2][:, e % 2, cols], values[:, cols], SQUARE)
 
+        h_codes, h_scales = {}, {}
+
+        def quantise_h(e0, e1, at):
+            codes = sb([P, e1 - e0, C], U32, f"h_codes{e0}", at)
+            scales = sb([P, e1 - e0, C], U8, f"h_scales{e0}")
+            values = h_laid[e0 // 2][:, e0 % 2 : e0 % 2 + e1 - e0].rearrange("p e c -> p (e c)")
+            quantise(codes[:].rearrange("p e c -> p (e c)"), scales[:].rearrange("p e c -> p (e c)"), values)
+            for e in range(e0, e1):
+                h_codes[e], h_scales[e] = codes[:, e - e0], scales[:, e - e0]
+
         gather_words(0, 2)
         gather_scales(0, 2)
         lay_w1(0, (FIRST_AT, FIRST_AT + 2 * KB), (on_scalar, on_gpsimd, on_scalar, on_gpsimd))
@@ -217,18 +228,12 @@ def tile_moe_tk_mlp_relu2_kernel(tc, xT, w1, w2, gate, offs, pos1, pos2, pos3, p
             lay_w1(e, ODD_AT if e % 2 else EVEN_AT, (on_vector, on_vector))
             first_product(e)
             squared_relu(e - 1)
+            if e == 5:
+                quantise_h(0, 2, e * RAW)
         squared_relu(E - 1)
 
-        w2_laid, w2_codes, w2_scales, h_codes, h_scales, y_banks = {}, {}, {}, {}, {}, {}
+        w2_laid, w2_codes, w2_scales, y_banks = {}, {}, {}, {}
         y = [sb([P, E * C], F32, "y0", RAW), sb([P, E * C], F32, "y1", Y1_AT)]
-
-        def quantise_h(e0, e1, at):
-            codes = sb([P, e1 - e0, C], U32, f"h_codes{e0}", at)
-            scales = sb([P, e1 - e0, C], U8, f"h_scales{e0}")
-            values = h_laid[e0 // 2][:, e0 % 2 : e0 % 2 + e1 - e0].rearrange("p e c -> p (e c)")
-            quantise(codes[:].rearrange("p e c -> p (e c)"), scales[:].rearrange("p e c -> p (e c)"), values)
-            for e in range(e0, e1):
-                h_codes[e], h_scales[e] = codes[:, e - e0], scales[:, e - e0]
 
         def lay_w2(copy, h, e0, e1, at=None):
             w2_laid[h, e0] = sb([P, e1 - e0, P, PACK], BF16, f"w2_laid{h}_{e0}", at)
@@ -256,14 +261,13 @@ def tile_moe_tk_mlp_relu2_kernel(tc, xT, w1, w2, gate, offs, pos1, pos2, pos3, p
             nc.scalar.copy(out=y[h][:, e0 * C : e1 * C], in_=y_banks[h, e0][:].rearrange("p e c -> p (e c)"))
 
         raw7 = 7 * RAW
-        quantise_h(0, 2, raw7 - 2 * KB + EDGE)
         quantise_h(2, 4, raw7 + EDGE)
         lay_w2(nc.vector.tensor_copy, 0, 0, 2)
         lay_w2(nc.vector.tensor_copy, 0, 2, 4)
         lay_w2(nc.vector.tensor_copy, 1, 0, 2)
         quantise_w2(0, 0, 2)
         quantise_w2(0, 2, 4)
-        quantise_h(4, 6, raw7 + 4 * KB)
+        quantise_h(4, 6, WHOLE_AT)
         for e0, at in ((4, LAID5_AT), (6, LAID7_AT)):
             lay_w2(nc.vector.tensor_copy, 0, e0, e0 + 1)
             lay_w2(nc.vector.tensor_copy, 0, e0 + 1, e0 + 2, at)

@@ -22,7 +22,8 @@ RELU = mybir.ActivationFunctionType.Relu
 SQUARE = mybir.ActivationFunctionType.Square
 COPY = mybir.ActivationFunctionType.Copy
 
-X_SCALAR = 80
+X_PIECES = ((0, 256), (256, 384), (384, 512))
+X_VECTOR = 11
 
 KB = 1024
 BANK = 2 * KB
@@ -30,7 +31,7 @@ EDGE = 64
 RAW = PACK * H * 4
 ODD_AT = (64 * KB, 66 * KB)
 FIRST_AT = 68 * KB
-EVEN_AT = (FIRST_AT + 2 * KB + EDGE, FIRST_AT + 6 * KB + EDGE)
+EVEN_AT = (FIRST_AT + EDGE, FIRST_AT + 2 * KB + EDGE)
 RELU_AT = 77 * KB
 LATE_AT = 85 * KB
 Y1_AT = LATE_AT + 8 * KB - EDGE
@@ -79,11 +80,11 @@ def tile_moe_tk_mlp_relu2_kernel(tc, xT, w1, w2, gate, offs, pos1, pos2, pos3, p
         def by_word(matrix):
             return matrix.rearrange("(p j) c -> p j c", j=PACK)
 
-        x_raw = [load(f"x_raw{a}", by_word(xT)[:, :, a * T // 2 : (a + 1) * T // 2]) for a in range(2)]
+        x_raw = [load(f"x_raw{t0}", by_word(xT)[:, :, t0:t1]) for t0, t1 in X_PIECES]
         offs_t = load_list("offs_t", offs)
         w1_raw = []
         for e in range(E):
-            parts = 2 if e < 2 else 1
+            parts = 2 if e in (0, 1, 3) else 1
             width = H // parts
             w1_raw.append(
                 [load(f"w1_raw{e}_{i}", by_word(w1[e])[:, :, i * width : (i + 1) * width], e * RAW + i * RAW // parts) for i in range(parts)]
@@ -115,21 +116,12 @@ def tile_moe_tk_mlp_relu2_kernel(tc, xT, w1, w2, gate, offs, pos1, pos2, pos3, p
         def quantise(codes, scales, values):
             nc.vector.quantize_mx(out=codes.bitcast(FP8X4), scales=scales, in_=values)
 
-        x_laid = [sb([P, T // 2, PACK], BF16, f"x_laid{a}") for a in range(2)]
-        cut = T // 2 - X_SCALAR
-
-        def quantise_x(a, t0, t1):
-            cols = slice(a * T // 2 + t0, a * T // 2 + t1)
-            quantise(x_words[:, cols], x_scales[:, cols], x_laid[a][:, t0:t1].rearrange("p c j -> p (c j)"))
-
-        for a in range(2):
-            interleave(nc.scalar.copy, x_laid[a][:, cut:], x_raw[a][:, :, cut:])
-        interleave(nc.vector.tensor_copy, x_laid[0][:, :cut], x_raw[0][:, :, :cut])
-        quantise_x(0, 0, T // 2)
-        interleave(nc.vector.tensor_copy, x_laid[1][:, :P], x_raw[1][:, :, :P])
-        interleave(nc.vector.tensor_copy, x_laid[1][:, P:cut], x_raw[1][:, :, P:cut])
-        quantise_x(1, 0, P)
-        quantise_x(1, P, T // 2)
+        x_laid = [sb([P, t1 - t0, PACK], BF16, f"x_laid{t0}") for t0, t1 in X_PIECES]
+        for raw, laid, (t0, t1) in zip(x_raw, x_laid, X_PIECES):
+            cut = (t1 - t0) * X_VECTOR // 16
+            interleave(nc.scalar.copy, laid[:, cut:], raw[:, :, cut:])
+            interleave(nc.vector.tensor_copy, laid[:, :cut], raw[:, :, :cut])
+            quantise(x_words[:, t0:t1], x_scales[:, t0:t1], laid[:].rearrange("p c j -> p (c j)"))
 
         slot_words, slot_scales = {}, {}
 
@@ -164,14 +156,14 @@ def tile_moe_tk_mlp_relu2_kernel(tc, xT, w1, w2, gate, offs, pos1, pos2, pos3, p
                 for u in range(2):
                     dst = tiles[u][:].rearrange("p (v m j) -> p m j v", v=2, j=PACK)
                     copies[2 * i + u](dst[:, i * P // parts : (i + 1) * P // parts], src[:, u])
-            w1_laid[e] = tiles
+            w1_laid[e] = [tile[:] for tile in tiles]
 
         def first_product(e):
             codes = stage.tile([P, H], U32, name="w1_codes", align_bytes=64)
             scales = stage.tile([P, H], U8, name="w1_scales", align_bytes=64)
             for u in range(2):
                 cols = slice(u * 2 * P, (u + 1) * 2 * P)
-                quantise(codes[:, cols], scales[:, cols], w1_laid[e][u][:])
+                quantise(codes[:, cols], scales[:, cols], w1_laid[e][u])
             a_banks[e] = [bank([P, PACK, P], f"a{e}_{s}", (2 * e + s) % 8) for s in range(2)]
             for s in range(2):
                 slots = slice(s * P, (s + 1) * P)
@@ -217,9 +209,14 @@ def tile_moe_tk_mlp_relu2_kernel(tc, xT, w1, w2, gate, offs, pos1, pos2, pos3, p
         gather_words(4, 6, RAW + 4 * KB + EDGE)
         gather_scales(4, 7, RAW + 6 * KB + EDGE)
         gather_words(6, 8, FIRST_AT + 4 * KB + EDGE)
-        lay_w1(2, EVEN_AT, (on_gpsimd, on_gpsimd))
+        whole = sb([P, 2, 2 * H], BF16, "w1_laid2", EVEN_AT[0])
+        nc.gpsimd.tensor_scalar(
+            whole[:].rearrange("p u (v m j) -> p m (u v) j", v=2, j=PACK),
+            w1_raw[2][0][:].rearrange("p j (m t) -> p m t j", t=PACK), 1.0, 0.0, MULT, ADD,
+        )
+        w1_laid[2] = [whole[:, u] for u in range(2)]
         squared_relu(1)
-        lay_w1(3, ODD_AT, (on_scalar, on_scalar))
+        lay_w1(3, ODD_AT, (on_scalar,) * 4)
         first_product(2)
         gather_scales(7, 8, 2 * RAW)
         first_product(3)

@@ -219,14 +219,13 @@ def tile_moe_tk_mlp_relu2_kernel(tc, xT, w1, w2, gate, offs, pos1, pos2, pos3, p
         lay_w1(3, ODD_AT, (on_scalar,) * 4)
         first_product(2)
         gather_scales(7, 8, 2 * RAW)
+        quantise_h(0, 2, 2 * RAW + KB)
         first_product(3)
         squared_relu(2, 3 * RAW)
         for e in range(4, E):
             lay_w1(e, ODD_AT if e % 2 else EVEN_AT, (on_vector, on_vector))
             first_product(e)
             squared_relu(e - 1)
-            if e == 5:
-                quantise_h(0, 2, e * RAW)
         squared_relu(E - 1)
 
         w2_laid, w2_codes, w2_scales, y_banks = {}, {}, {}, {}

from contextlib import ExitStack

import concourse.mybir as mybir
from concourse.masks import make_identity

K, T, E, C, H, N = 512, 512, 8, 256, 512, 256
TOP = 4
P = 128
PACK = 4
FLOPS = 2 * E * C * (K * H + H * N)

F32 = mybir.dt.float32
BF16 = mybir.dt.bfloat16
I32 = mybir.dt.int32
U32 = mybir.dt.uint32
U16 = mybir.dt.uint16
U8 = mybir.dt.uint8
FP8X4 = mybir.dt.float8_e4m3fn_x4
MULT = mybir.AluOpType.mult
ADD = mybir.AluOpType.add
RELU = mybir.ActivationFunctionType.Relu
SQUARE = mybir.ActivationFunctionType.Square
COPY = mybir.ActivationFunctionType.Copy

X_PIECES = ((0, 256), (256, 384), (384, 512))
X_VECTOR = 11

KB = 1024
BANK = 2 * KB
EDGE = 64
RAW = PACK * H * 4
ODD_AT = (64 * KB, 66 * KB)
FIRST_AT = 68 * KB
EVEN_AT = (FIRST_AT + EDGE, FIRST_AT + 2 * KB + EDGE)
RELU_AT = 77 * KB
LATE_AT = 85 * KB
Y1_AT = LATE_AT + 8 * KB - EDGE
LAID5_AT = 101 * KB
LAID7_AT = 105 * KB
CODES7_AT = 109 * KB
CODES_LAST_AT = 112 * KB
GATED_AT = 115 * KB
WHOLE_AT = 118 * KB


def tile_moe_tk_mlp_relu2_kernel(tc, xT, w1, w2, gate, offs, pos1, pos2, pos3, pos4, out):
    nc = tc.nc
    pos = (pos1, pos2, pos3, pos4)
    with ExitStack() as ctx:
        keep = ctx.enter_context(tc.tile_pool(name="keep", bufs=1))
        stage = ctx.enter_context(tc.tile_pool(name="stage", bufs=2))
        placed = ctx.enter_context(tc.tile_pool(name="placed", bufs=1))
        psum = ctx.enter_context(tc.psum_pool(name="psum", bufs=1))

        def sb(shape, dtype, name, at=None, align=64):
            if at is None:
                return keep.tile(shape, dtype, name=name, align_bytes=align)
            return placed.tile(shape, dtype, name=name, align_bytes=align, offset=at)

        def bank(shape, name, b):
            return psum.tile(shape, F32, name=name, offset=b * BANK)

        x_scales = sb([P, 2 * T], U8, "x_scales")
        nc.gpsimd.memset(x_scales[:].bitcast(I32), 0)
        x_words = sb([P, 2 * T], I32, "x_words")
        nc.vector.memset(x_words[:, T:], 0)
        ident = sb([P, P], F32, "ident")
        make_identity(nc, ident[:])

        def load(name, rows, at=None):
            raw = sb(rows.shape, F32, name, at, 256)
            nc.sync.dma_start(out=raw[:], in_=rows)
            return raw

        def load_list(name, lst):
            t = keep.tile(lst.shape, U16, name=name)
            nc.sync.dma_start(t[:], lst)
            return t

        def by_word(matrix):
            return matrix.rearrange("(p j) c -> p j c", j=PACK)

        x_raw = [load(f"x_raw{t0}", by_word(xT)[:, :, t0:t1]) for t0, t1 in X_PIECES]
        offs_t = load_list("offs_t", offs)
        w1_raw = []
        for e in range(E):
            parts = 2 if e in (0, 1, 3) else 1
            width = H // parts
            w1_raw.append(
                [load(f"w1_raw{e}_{i}", by_word(w1[e])[:, :, i * width : (i + 1) * width], e * RAW + i * RAW // parts) for i in range(parts)]
            )
        w2_raw = {}
        for e0 in (0, 2):
            raw = load(f"w2_whole{e0}", w2[e0 : e0 + 2].rearrange("e (p j) n -> p e j n", j=PACK), None if e0 else WHOLE_AT)
            for h in range(2):
                w2_raw[h, e0] = raw[:, :, :, h * P : (h + 1) * P]

        def load_halves(h):
            for e0 in (4, 6):
                raw = sb([P, 2, PACK, P], F32, f"w2_raw{h}_{e0}", LATE_AT + (e0 - 4) * 2 * KB if h else None, 256)
                for e in (e0, e0 + 1):
                    nc.sync.dma_start(out=raw[:, e - e0], in_=by_word(w2[e])[:, :, h * P : (h + 1) * P])
                w2_raw[h, e0] = raw[:]

        load_halves(0)
        pos_t, gates = [], []
        for r in range(TOP):
            pos_t.append(load_list(f"pos_t{r}", pos[r]))
            gates.append(load(f"gate{r}", gate[r, :P, :]))
            if r == 1:
                load_halves(1)

        def interleave(copy, dst, src):
            copy(out=dst.rearrange("p (c i) j -> p c j i", i=2), in_=src.rearrange("p j (c i) -> p c j i", i=2))

        def quantise(codes, scales, values):
            nc.vector.quantize_mx(out=codes.bitcast(FP8X4), scales=scales, in_=values)

        x_laid = [sb([P, t1 - t0, PACK], BF16, f"x_laid{t0}") for t0, t1 in X_PIECES]
        for raw, laid, (t0, t1) in zip(x_raw, x_laid, X_PIECES):
            cut = (t1 - t0) * X_VECTOR // 16
            interleave(nc.scalar.copy, laid[:, cut:], raw[:, :, cut:])
            interleave(nc.vector.tensor_copy, laid[:, :cut], raw[:, :, :cut])
            quantise(x_words[:, t0:t1], x_scales[:, t0:t1], laid[:].rearrange("p c j -> p (c j)"))

        slot_words, slot_scales = {}, {}

        def gather(name, window, dtype, into, e0, e1, at=None):
            picked = sb([P, e1 - e0, C], dtype, f"{name}{e0}", at)
            nc.vector.tensor_copy(picked[:].rearrange("p e c -> p (e c)"), window.indirect(offs_t[:, e0 * C // 16 : e1 * C // 16]))
            for e in range(e0, e1):
                into[e] = picked[:, e - e0]

        def gather_words(e0, e1, at=None):
            gather("slot_words", x_words[:].bitcast(U32), U32, slot_words, e0, e1, at)

        def gather_scales(e0, e1, at=None):
            gather("slot_scales", x_scales[:], U8, slot_scales, e0, e1, at)

        def on_vector(dst, src):
            nc.vector.tensor_copy(out=dst, in_=src)

        def on_scalar(dst, src):
            nc.scalar.copy(out=dst, in_=src)

        def on_gpsimd(dst, src):
            nc.gpsimd.tensor_scalar(dst.rearrange("p m j v -> p m v j"), src.rearrange("p m j v -> p m v j"), 1.0, 0.0, MULT, ADD)

        w1_laid, a_banks = {}, {}

        def lay_w1(e, at, copies):
            tiles = [sb([P, 2 * H], BF16, f"w1_laid{e}_{u}", at[u]) for u in range(2)]
            parts = len(w1_raw[e])
            for i, raw in enumerate(w1_raw[e]):
                src = raw[:].rearrange("p j (m u v) -> p u m j v", u=2, v=2)
                for u in range(2):
                    dst = tiles[u][:].rearrange("p (v m j) -> p m j v", v=2, j=PACK)
                    copies[2 * i + u](dst[:, i * P // parts : (i + 1) * P // parts], src[:, u])
            w1_laid[e] = [tile[:] for tile in tiles]

        def first_product(e):
            codes = stage.tile([P, H], U32, name="w1_codes", align_bytes=64)
            scales = stage.tile([P, H], U8, name="w1_scales", align_bytes=64)
            for u in range(2):
                cols = slice(u * 2 * P, (u + 1) * 2 * P)
                quantise(codes[:, cols], scales[:, cols], w1_laid[e][u])
            a_banks[e] = [bank([P, PACK, P], f"a{e}_{s}", (2 * e + s) % 8) for s in range(2)]
            for s in range(2):
                slots = slice(s * P, (s + 1) * P)
                for t in range(PACK):
                    cols = slice(t * P, (t + 1) * P)
                    nc.tensor.matmul_mx(
                        out=a_banks[e][s][:, t, :], lhsT=codes[:, cols].bitcast(FP8X4), lhsT_scale=scales[:, cols],
                        rhs=slot_words[e][:, slots].bitcast(FP8X4), rhs_scale=slot_scales[e][:, slots],
                        start=True, stop=True,
                    )

        h_laid = [sb([P, 2, C * PACK], BF16, f"h_laid{q}") for q in range(E // 2)]

        def squared_relu(e, at=None):
            relu = sb([P, 2, P, PACK], F32, f"relu{e}", at or RELU_AT + (e % 2) * 4 * KB)
            for s in range(2):
                nc.scalar.activation(relu[:, s], a_banks[e][s][:].rearrange("p t n -> p n t"), RELU)
            pieces = 2
            values = relu[:].rearrange("p s n t -> p (s n t)")
            for i in range(pieces):
                cols = slice(i * C * PACK // pieces, (i + 1) * C * PACK // pieces)
                nc.scalar.activation(h_laid[e // 2][:, e % 2, cols], values[:, cols], SQUARE)

        h_codes, h_scales = {}, {}

        def quantise_h(e0, e1, at):
            codes = sb([P, e1 - e0, C], U32, f"h_codes{e0}", at)
            scales = sb([P, e1 - e0, C], U8, f"h_scales{e0}")
            values = h_laid[e0 // 2][:, e0 % 2 : e0 % 2 + e1 - e0].rearrange("p e c -> p (e c)")
            quantise(codes[:].rearrange("p e c -> p (e c)"), scales[:].rearrange("p e c -> p (e c)"), values)
            for e in range(e0, e1):
                h_codes[e], h_scales[e] = codes[:, e - e0], scales[:, e - e0]

        gather_words(0, 2)
        gather_scales(0, 2)
        lay_w1(0, (FIRST_AT, FIRST_AT + 2 * KB), (on_scalar, on_gpsimd, on_scalar, on_gpsimd))
        first_product(0)
        gather_words(2, 4, RAW // 2)
        gather_scales(2, 4, RAW // 2 + 2 * KB)
        lay_w1(1, (FIRST_AT + 4 * KB, FIRST_AT + 6 * KB), (on_scalar, on_scalar, on_scalar, on_gpsimd))
        squared_relu(0, RAW)
        first_product(1)
        gather_words(4, 6, RAW + 4 * KB + EDGE)
        gather_scales(4, 7, RAW + 6 * KB + EDGE)
        gather_words(6, 8, FIRST_AT + 4 * KB + EDGE)
        whole = sb([P, 2, 2 * H], BF16, "w1_laid2", EVEN_AT[0])
        nc.gpsimd.tensor_scalar(
            whole[:].rearrange("p u (v m j) -> p m (u v) j", v=2, j=PACK),
            w1_raw[2][0][:].rearrange("p j (m t) -> p m t j", t=PACK), 1.0, 0.0, MULT, ADD,
        )
        w1_laid[2] = [whole[:, u] for u in range(2)]
        squared_relu(1)
        lay_w1(3, ODD_AT, (on_scalar,) * 4)
        first_product(2)
        gather_scales(7, 8, 2 * RAW)
        quantise_h(0, 2, 2 * RAW + KB)
        first_product(3)
        squared_relu(2, 3 * RAW)
        for e in range(4, E):
            lay_w1(e, ODD_AT if e % 2 else EVEN_AT, (on_vector, on_vector))
            first_product(e)
            squared_relu(e - 1)
        squared_relu(E - 1)

        w2_laid, w2_codes, w2_scales, y_banks = {}, {}, {}, {}
        y = [sb([P, E * C], F32, "y0", RAW), sb([P, E * C], F32, "y1", Y1_AT)]

        def lay_w2(copy, h, e0, e1, at=None):
            w2_laid[h, e0] = sb([P, e1 - e0, P, PACK], BF16, f"w2_laid{h}_{e0}", at)
            dst = w2_laid[h, e0][:].rearrange("p e (c i) j -> p e c j i", i=2)
            pair = w2_raw[h, e0 - e0 % 2][:, e0 % 2 : e0 % 2 + e1 - e0]
            copy(out=dst, in_=pair.rearrange("p e j (c i) -> p e c j i", i=2))

        def quantise_w2(h, e0, e1, at=None, scales_at=None):
            codes = sb([P, e1 - e0, P], U32, f"w2_codes{h}_{e0}", at)
            scales = sb([P, e1 - e0, P], U8, f"w2_scales{h}_{e0}", scales_at)
            values = w2_laid[h, e0][:].rearrange("p e c j -> p (e c j)")
            quantise(codes[:].rearrange("p e c -> p (e c)"), scales[:].rearrange("p e c -> p (e c)"), values)
            for e in range(e0, e1):
                w2_codes[h, e], w2_scales[h, e] = codes[:, e - e0], scales[:, e - e0]

        def second_product(h, e0, e1, b):
            y_banks[h, e0] = bank([P, e1 - e0, C], f"y{h}_{e0}", b)
            for e in range(e0, e1):
                nc.tensor.matmul_mx(
                    out=y_banks[h, e0][:, e - e0], lhsT=w2_codes[h, e].bitcast(FP8X4), lhsT_scale=w2_scales[h, e],
                    rhs=h_codes[e].bitcast(FP8X4), rhs_scale=h_scales[e], start=True, stop=True,
                )

        def copy_y(h, e0, e1):
            nc.scalar.copy(out=y[h][:, e0 * C : e1 * C], in_=y_banks[h, e0][:].rearrange("p e c -> p (e c)"))

        raw7 = 7 * RAW
        quantise_h(2, 4, raw7 + EDGE)
        lay_w2(nc.vector.tensor_copy, 0, 0, 2)
        lay_w2(nc.vector.tensor_copy, 0, 2, 4)
        lay_w2(nc.vector.tensor_copy, 1, 0, 2)
        quantise_w2(0, 0, 2)
        quantise_w2(0, 2, 4)
        quantise_h(4, 6, WHOLE_AT)
        for e0, at in ((4, LAID5_AT), (6, LAID7_AT)):
            lay_w2(nc.vector.tensor_copy, 0, e0, e0 + 1)
            lay_w2(nc.vector.tensor_copy, 0, e0 + 1, e0 + 2, at)
            quantise_w2(0, e0, e0 + 1)
            quantise_w2(0, e0 + 1, e0 + 2, CODES7_AT if e0 == 6 else None)
            quantise_h(e0 // 2 + 4, e0 // 2 + 5, at if e0 == 4 else at + KB - EDGE)
        groups = ((0, 2, 6), (2, 4, 7), (4, 6, 4), (6, 7, 5), (7, 8, 0))
        for e0, e1, b in groups:
            second_product(0, e0, e1, b)
        for e0, e1, b in groups:
            copy_y(0, e0, e1)

        lay_w2(nc.vector.tensor_copy, 1, 2, 4, LAID7_AT - 2 * KB + EDGE)
        quantise_w2(1, 0, 2, None, LAID7_AT + EDGE)
        quantise_w2(1, 2, 4)
        for e0, at in ((4, CODES7_AT - 2 * KB + EDGE), (6, CODES7_AT + EDGE)):
            lay_w2(nc.scalar.copy, 1, e0, e0 + 2, at)
            quantise_w2(1, e0, e0 + 2, CODES_LAST_AT if e0 == 6 else None)
        for q, b in enumerate((2, 3, 0, 1)):
            second_product(1, 2 * q, 2 * q + 2, b)
        for q in range(E // 2):
            copy_y(1, 2 * q, 2 * q + 2)

        def picked(h, r, t0, t1):
            return y[h][:].indirect(pos_t[r][:, t0 // 16 : t1 // 16])

        def combine(name, in0, in1, op, at=None):
            res = sb(in1.shape, F32, name, at)
            nc.vector.tensor_tensor(res[:], in0, in1, op)
            return res

        def fetch_gated(h, r, t0, t1, at=None):
            return combine(f"product{h}_{r}_{t0}", picked(h, r, t0, t1), gates[r][:, t0:t1], MULT, at)

        def fetch_plain(r, t0, t1, at=None):
            values = sb([P, t1 - t0], F32, f"fetched{r}_{t0}", at)
            nc.scalar.activation(values[:], picked(1, r, t0, t1), COPY)
            return values

        def add_turned(acc, term, first, last, c0=0):
            blocks = term.shape[1] // P
            for c in range(blocks):
                nc.tensor.matmul(
                    acc[:, c0 + c], lhsT=term[:, c * P : (c + 1) * P], rhs=ident[:], is_transpose=True,
                    start=first and c == 0, stop=last and c == blocks - 1,
                )

        def copy_out(name, acc, at=None):
            res = sb([P, acc.shape[1] * P], F32, name, at)
            nc.scalar.copy(out=res[:], in_=acc[:].rearrange("p c n -> p (c n)"))
            return res

        def turn_back(name, turned, b):
            back = bank([P, turned.shape[1] // P, P], name, b)
            add_turned(back, turned, True, True)
            return back[:].rearrange("p c t -> p (c t)")

        half = T // 2
        sum0 = bank([P, T // P, P], "sum0", 5)
        add_turned(sum0, fetch_gated(0, 0, 0, T), True, False)
        add_turned(sum0, fetch_gated(0, 1, 0, half), False, False)
        add_turned(sum0, fetch_gated(0, 1, half, T, LATE_AT), False, False, 2)
        add_turned(sum0, fetch_gated(0, 2, 0, T, LATE_AT + 3 * KB), False, False)
        add_turned(sum0, fetch_gated(0, 3, 0, T, LATE_AT + 5 * KB), False, True)

        early, late = slice(0, half), slice(half, T)
        first = [fetch_plain(0, 0, half), fetch_plain(0, half, T)]
        turned0 = copy_out("turned0", sum0, CODES_LAST_AT)
        second_late = fetch_plain(1, half, T)
        sum1 = bank([P, 2, P], "sum1", 2)
        add_turned(sum1, fetch_gated(1, 2, 0, half), True, False)
        add_turned(sum1, fetch_gated(1, 3, 0, half), False, False)
        add_turned(sum1, combine("first_early", first[0][:], gates[0][:, early], MULT, GATED_AT), False, True)
        back0 = turn_back("back0", turned0, 4)
        back1 = turn_back("back1", copy_out("turned1", sum1), 0)
        second_early = fetch_plain(1, 0, half, GATED_AT - KB + EDGE)
        out0 = sb([P, T], F32, "out0", GATED_AT + KB // 2)
        for cols in (early, late):
            nc.scalar.copy(out=out0[:, cols], in_=back0[:, cols])
            nc.sync.dma_start(out[:P, cols], out0[:, cols])

        third, fourth = fetch_gated(1, 2, half, T), fetch_gated(1, 3, half, T)
        first_late = combine("first_late", first[1][:], gates[0][:, late], MULT)
        two = combine("two", third[:], fourth[:], ADD)
        second_late = combine("second_late", second_late[:], gates[1][:, late], MULT)
        three = combine("three", two[:], first_late[:], ADD)
        second_early = combine("second_early", second_early[:], gates[1][:, early], MULT)
        nc.sync.dma_start(out[P:, late], combine("out_late", three[:], second_late[:], ADD)[:])
        for c in range(2):
            cols = slice(c * P, (c + 1) * P)
            nc.sync.dma_start(out[P:, cols], combine(f"out_early{c}", back1[:, cols], second_early[:, cols], ADD)[:])
